import numpy as np, ml_dtypes
CORES = [5,29,101,125,133,157,229,253]
N = 8
import mx_ref
BF = ml_dtypes.bfloat16
def entries(a):
    return np.ascontiguousarray(a.T).reshape(-1)
def table(e):
    return np.ascontiguousarray(np.reshape(e, (-1, 16)).T).astype(np.int32)
def cols(t, e):
    v = np.concatenate([t.reshape(128, -1, 4), np.zeros((128, 1, 4), BF)], axis=1)
    return np.ascontiguousarray(v[:, e]).reshape(128, -1)
def f(rng, *shape):
    return mx_ref.flush((rng.standard_normal(shape, dtype=np.float32) * np.exp2(rng.integers(-2, 3, shape[:-1] + (1,)))).astype(BF))
def wide(rng, *shape, cols=0):
    v = rng.standard_normal(shape, dtype=np.float32) * np.exp2(rng.integers(-12, 13, shape)).astype(np.float32)
    if cols: v *= np.repeat(np.exp2(rng.integers(-cols, cols + 1, shape[:-2] + (1, shape[-1] // 4))) * (rng.random(shape[:-2] + (1, shape[-1] // 4)) > 0.0625), 4, axis=-1).astype(np.float32)
    return mx_ref.flush(v.astype(BF))
T, O = 128, 4
CAP, ROOM = 144, 160
PAIR, MOVE, BOTH = 24, 8, 30
def turn(v, e):
    v = np.sort(v); return v[np.argsort((v // T - e) % N, kind="stable")]
def play(c1, c2):
    a, b = c1.reshape(-1), c2.reshape(-1)
    first = [turn(np.flatnonzero(a == e), e)[:CAP] for e in range(N)]
    refused = np.setdiff1d(np.arange(N * T), np.concatenate(first))
    second = [turn(refused[b[refused] == e], e)[:ROOM - len(first[e])] for e in range(N)]
    return first, second, refused
def broken(c1, c2):
    b = []
    if c1.min() < 0 or c1.max() >= N: return ["c1"]
    if c2.min() < 0 or c2.max() >= N: return ["c2"]
    if (c1 == c2).any(): b.append("a token with two equal choices")
    if max(np.bincount(v, minlength=N).max() for v in c1) > PAIR: b.append("first choices of a pair of ranks")
    first, second, refused = play(c1, c2)
    if np.bincount(c1.reshape(-1)[refused] * N + c2.reshape(-1)[refused], minlength=N * N).max() > MOVE: b.append("refused tokens of a pair of ranks")
    for e in range(N):
        if np.bincount(np.concatenate([first[e], second[e]]) // T, minlength=N).max() > BOTH: b.append("admitted tokens of a pair of ranks")
    return b
def fill(rng, low, high, total):
    n, p = np.array(low), rng.dirichlet(np.full(len(low), 16.0))
    while n.sum() < total: n = np.minimum(n + rng.multinomial(total - n.sum(), p), high)
    return n
def deal(rng, tot):
    n = np.stack([np.bincount(v, minlength=N) for v in rng.permutation(np.repeat(np.arange(N), tot)).reshape(N, T)])
    while n.max() > PAIR:
        s, e = np.argwhere(n > PAIR)[0]
        q = rng.choice(np.flatnonzero(n[:, e] < PAIR))
        g = rng.choice(np.flatnonzero(n[q] > n[s]))
        n[s, e] -= 1; n[q, e] += 1; n[q, g] -= 1; n[s, g] += 1
    return n
def bounds():
    return np.full(N, T >> 3), np.full(N, N * PAIR), np.zeros((N, N), int), MOVE * (1 - np.eye(N, dtype=int))
def lists(rng, low, high, mlow, mhigh, pair=None, skew=False, force=None):
    for _ in range(50):
        n = deal(rng, fill(rng, low, high, N * T))
        if pair or force:
            s, g, e = pair or (*force, force[1])
            for to in (g, e):
                while n[s, to] < PAIR:
                    h, q = [(h, q) for h in range(N) for q in range(N) if h not in (g, e) and n[s, h] > 0 and q != s and n[q, to] > 0 and n[q, h] < PAIR][0]
                    n[s, to] += 1; n[s, h] -= 1; n[q, to] -= 1; n[q, h] += 1
        c1 = np.concatenate([rng.permutation(np.repeat(np.arange(N), v)) for v in n])
        c2 = (c1 + rng.integers(1, N, N * T)) % N
        for e in range(N):
            at = turn(np.flatnonzero(c1 == e), e)[CAP:]
            c2[at] = rng.permutation(np.repeat(np.arange(N), fill(rng, mlow[e], mhigh[e], len(at))))
            if pair and e == pair[1]:
                mine = at[at // T == pair[0]]; named = c2[at]
                named = np.concatenate([named[named == pair[2]], named[named != pair[2]]]); k = int((named == pair[2]).sum())
                to = rng.permutation(mine)[:k]; c2[np.setdiff1d(at, to)] = named[k:]; c2[to] = pair[2]
        if skew:
            out = np.zeros(N * T, bool)
            for e in range(N): out[turn(np.flatnonzero(c1 == e), e)[CAP:]] = True
            for s in range(N):
                e = (s + rng.integers(3, N)) % N; k = np.arange(s * T, s * T + T)
                k = k[~out[k] & ((c1[k] - s - 1) % N < 2)]; c2[k] = e
        c1, c2 = c1.reshape(N, T), c2.reshape(N, T)
        if not broken(c1, c2): return {"c1": np.stack([table(v) for v in c1]), "c2": np.stack([table(v) for v in c2])}
    raise RuntimeError("no lists found")
def tiles(rng):
    return {"x": f(rng, N, 128, 4 * T), "w": f(rng, N, 128, 512 * O)}
def setup_inputs(rng):
    return {**tiles(rng), **lists(rng, *bounds())}
def setup_inputs_pair(rng):
    low, high, mlow, mhigh = bounds()
    p = rng.permutation(N); g, e, z = p[0], p[1], p[2]; s = (g - 1) % N
    if s in (e, z): e, z = [k for k in p if k not in (g, s)][:2]
    few = N - 2 - (N > 4)
    high[:] = CAP + (few - 1 + (N == 4)) * MOVE
    low[g] = high[g] = CAP + min(PAIR, BOTH - PAIR + few * MOVE); low[e] = N * PAIR >> 2; high[e] = CAP
    mhigh[:, e] = 0; mlow[g, e] = mhigh[g, e] = BOTH - PAIR
    if N > 4: low[z] = high[z] = 0; mhigh[:, z] = 0
    return {**tiles(rng), **lists(rng, low, high, mlow, mhigh, (int(s), int(g), int(e)))}
def setup_inputs_exact(rng):
    low, high, mlow, mhigh = bounds()
    p = rng.permutation(N); src = p[2:2 + (ROOM - CAP) // MOVE]
    high[:] = CAP
    low[p[0]] = CAP
    low[p[1]] = high[p[1]] = CAP + 1
    low[p[-1]] = N * PAIR >> 2
    mhigh[:, p[-1]] = np.minimum(mhigh[:, p[-1]], MOVE >> 1)
    low[src] = high[src] = N * PAIR
    mhigh[:, p[0]] = 0
    mlow[src, p[0]] = mhigh[src, p[0]] = MOVE
    return {**tiles(rng), **lists(rng, low, high, mlow, mhigh, skew=True, force=(int(p[-1] - 1) % N, int(p[-1])))}
def setup_inputs_full(rng):
    low, high, mlow, mhigh = bounds()
    p = rng.permutation(N); src = p[1:1 + 2 * ((ROOM - CAP) // MOVE)]
    low[p[0]] = CAP + 3 * MOVE // 2
    low[src] = CAP + MOVE
    mlow[src, p[0]] = MOVE
    return {**tiles(rng), **lists(rng, low, high, mlow, mhigh)}
def setup_inputs_room(rng):
    low, high, mlow, mhigh = bounds()
    p = rng.permutation(N); src = p[1:2 + (ROOM - CAP) // MOVE]
    low[p[0]] = high[p[0]] = CAP - 1
    low[src] = CAP + MOVE
    mlow[src, p[0]] = MOVE
    return {**tiles(rng), **lists(rng, low, high, mlow, mhigh)}
def setup_inputs_spread(rng):
    d = setup_inputs(rng); d["x"] = wide(rng, N, 128, 4 * T, cols=6); return d
def check_inputs(d):
    return broken(np.stack([entries(v) for v in d["c1"]]), np.stack([entries(v) for v in d["c2"]]))
def reference(x, w, c1, c2):
    first, second, _ = play(np.stack([entries(v) for v in c1]), np.stack([entries(v) for v in c2]))
    tokens = np.concatenate([x[r] for r in range(N)], axis=1)
    y = np.zeros((N, 128, O * ROOM), np.float32)
    for e in range(N):
        held = np.concatenate([first[e], second[e]])
        t = mx_ref.quantize(cols(tokens, np.concatenate([held, np.full(ROOM - len(held), -1)])))
        for o in range(O): y[e][:, ROOM * o:ROOM * o + ROOM] = mx_ref.matmul(mx_ref.quantize(w[e][:, 512 * o:512 * o + 512]), t)
    return {"y": y}

@@ -1,0 +1,496 @@
+import numpy as np
+from concourse.bass import DstId, RemoteDMATransfer
+from concourse.mybir import dt, AluOpType, AxisListType, ActivationFunctionType
+
+N = 8
+CAP, ROOM, O = 144, 160, 4
+W = 32
+LAND = N * W
+
+F4, B2, I4, U2, MX, U1 = "float32", "bfloat16", "int32", "uint16", "float8_e4m3fn_x4", "uint8"
+SIZES = {
+    I4: dict(c1b=8, c2b=8, cm=8, cs=8, pi=1, kk=8, r1i=64, r2i=64, r1=64, r2=64),
+    U2: dict(cu=8, cu1=8, so=4, offp=16, offh=10),
+    F4: dict(kf=8, bo=32, bt=32, wr=32, wc=32, ic=32, jw0=10, jw=10, val0=64, val=64, sc0=16, sc1=16, scl=16, fc=48,
+             cum=128, mm=128, mt=128, ss=128, win=384, rr=384, vv=32, vt=32, v2=32, vb=32, sw=320, wl=10, ys=640),
+    B2: dict(cr=96, c2c=64, cda=32, cdb=32, ca=128, cb=128, ya1=128, yb1=128, e1=96, e1t=96, e2=64, e2t=64, e2s=8,
+             k32=320, x16=384, kr=384, kp=320, jd=320, st=320, stt=320,
+             tn=8, ta=64, tb=64, te=64, tia=64, tib=64, eq2=64, eqa=64, eqb=64, gn=128, ga=128, gb=128, ge=128, gia=128,
+             gib=128, ya=128, yb=128, xa=128, xb=128, xs=128,
+             info1=16, info2=16, hand1=2, hand2=4, land1=22, land2=22,
+             xt=512, wt=2048, zt=640),
+    MX: dict(xq=128, wq=512, oq=256, rq=64, lq=416, hq=160),
+    U1: dict(xz=128, wz=512, oz=256, rz=64, lz=416, hz=160),
+}
+SCRATCH = {"ps": ("psum", [128, 2048], F4)}
+for _d in SIZES:
+    for _n in SIZES[_d]:
+        SCRATCH[_n] = ("sbuf", [128, SIZES[_d][_n]], _d)
+SEMAPHORES = ["v", "a", "p", "ld", "le", "lx", "lw", "ly", "i1", "i2", "tc", "ts", "lo", "pc1", "pc2", "pa1", "pa2", "n2",
+              "t0", "t1", "t2", "t3", "y0", "y1", "y2", "y3"]
+
+
+def bits(es):
+    m = 0
+    for e in es:
+        m |= 1 << e
+    return m
+
+
+def at(T, topo, s, u):
+    return T.cores[(s + u) % N]
+
+
+def order(T, topo, s):
+    cross = [u for u in range(1, N) if not topo.may_write(T.cores[s], at(T, topo, s, u))]
+    direct = [u for u in range(1, N) if u not in cross]
+    return cross, direct
+
+
+def relays(T, topo, s):
+    me = T.cores[s]
+    cross, _ = order(T, topo, s)
+    r = [c for c in topo.cores_of(me) if c != me and T.rank_of(c) is None
+         and all(topo.may_write(c, at(T, topo, s, u)) for u in cross)]
+    near = [c for c in r if topo.die(c) == topo.die(me)]
+    far = [c for c in r if topo.die(c) != topo.die(me)]
+    return [near[0], far[0]], [far[1], near[1]]
+
+
+SPLIT_C = ((0, 2), (2, 4), (4, 8))
+SPLIT_S = ((4, 6), (6, 8), (0, 4))
+
+
+def xfer(core, d, topo, es, sem, src, dst):
+    rid, pid = topo.addr(d, core)
+    return RemoteDMATransfer(dst_ids=[DstId(rid=rid, pnc=pid)], dma_engine_mask=bits(es), remote_sem=sem, src=src, dst=dst)
+
+
+def slot_of(u):
+    return (N - u) % N
+
+
+def hand_on(g, core, T, topo):
+    for s in range(N):
+        cross, _ = order(T, topo, s)
+        rc, rs = relays(T, topo, s)
+        if core not in rc + rs:
+            continue
+        codes = core in rc
+        h = (rc if codes else rs).index(core)
+        us = cross[2 * h:2 * h + 2]
+        dst = [at(T, topo, s, u) for u in us]
+        es = [topo.engines(core, d) for d in dst]
+        col = [8 + 2 * (slot_of(u) - 1) for u in us]
+        j = 0 if codes else 1
+        g.wait_ge(T.sem.i1, 4)
+        g.remote_dma_fused([xfer(core, dst[j], topo, es[j], T.sem.i1, T.hand1[:, :], T.land1[:, col[j]:col[j] + 2])],
+                           local_sem=T.sem.lo)
+        es = [es[0][0:4], es[1][4:8]]
+        if codes:
+            g.wait_ge(T.sem.i2, 4)
+            g.remote_dma_fused([xfer(core, dst[i], topo, es[i], T.sem.i2, T.hand2[:, 2 * i:2 * i + 2],
+                                     T.land2[:, col[i]:col[i] + 2]) for i in range(2)], local_sem=T.sem.lo)
+        tr = []
+        for i, u in enumerate(us):
+            c = W * slot_of(u)
+            if codes:
+                a, b = T.rq[:, W * i:W * i + W].bitcast(dt.uint8), T.lq[:, c:c + W].bitcast(dt.uint8)
+            else:
+                a, b = T.rz[:, W * i:W * i + W], T.lz[:, c:c + W]
+            tr.append(xfer(core, dst[i], topo, es[i], T.sem.tc if codes else T.sem.ts, a, b))
+        g.wait_ge(T.sem.tc if codes else T.sem.ts, 8 if codes else 4)
+        g.remote_dma_fused(tr, local_sem=T.sem.lo)
+        g.wait_ge(T.sem.lo, 24 if codes else 16)
+        return
+
+
+def rank_program(g, core, T, topo):
+    s = T.rank_of(core)
+    if s is None:
+        hand_on(g, core, T, topo)
+        return
+    A, X = AluOpType, AxisListType.X
+    Copy, Ident = ActivationFunctionType.Copy, ActivationFunctionType.Identity
+    sem = T.sem
+    vec, act, ten = g.vector, g.scalar, g.tensor
+    cross, direct = order(T, topo, s)
+    ords = [0] + cross + direct
+    rc, rs = relays(T, topo, s)
+
+    vn, vw = [0], [0]
+
+    def V(ins):
+        ins.then_inc(sem.v, 1)
+        vn[0] += 1
+
+    def fence():
+        if vw[0] < vn[0]:
+            vec.wait_ge(sem.v, vn[0])
+            vw[0] = vn[0]
+        return vn[0]
+
+    def ts(out, in0, a, b, op0, op1=None):
+        if op1 is None:
+            V(vec.tensor_scalar(out, in0, a, None, op0))
+        else:
+            V(vec.tensor_scalar(out, in0, a, b, op0, op1))
+
+    def tt(out, a, b, op):
+        V(vec.tensor_tensor(out, a, b, op))
+
+    def cp(out, a):
+        V(vec.tensor_copy(out, a))
+
+    def fill(out, c):
+        V(vec.memset(out, c))
+
+    def scan(out, a, b, ini, op0):
+        V(vec.tensor_tensor_scan(out, a, b, ini, op0, A.add))
+
+    an = [0]
+
+    def S(ins):
+        ins.then_inc(sem.a, 1)
+        an[0] += 1
+
+    pn = [0]
+
+    def I(out, pattern, base, cm=0, f=True):
+        if f:
+            g.iota(out, pattern, base, cm, allow_small_or_imprecise_dtypes=True).then_inc(sem.p, 1)
+        else:
+            g.iota(out, pattern, base, cm).then_inc(sem.p, 1)
+        pn[0] += 1
+
+    for big, src, sm in ((T.c1b, T.c1, sem.ld), (T.c2b, T.c2, sem.le)):
+        for q in range(8):
+            dq = g.sync if q % 2 else act
+            dq.dma_start(big[16 * q:16 * q + 16, :], src[:, :]).then_inc(sm, 16)
+    g.sync.dma_start(T.xt[:, :], T.x[:, :]).then_inc(sem.lx, 16)
+
+    I(T.ic[:, :], [[1, 32]], 0)
+    I(T.pi[:, :], [[0, 1]], 0, 1, False)
+    k = 0
+    while k < N:
+        n = 1
+        step = ords[k + 1] - ords[k] if k + 1 < N else 0
+        while k + n < N and ords[k + n] - ords[k + n - 1] == step:
+            n += 1
+        I(T.bo[:, k:k + n], [[step, n]], ords[k])
+        k += n
+    I(T.r1i[:, :], [[1, 8], [0, 8]], 8 - s, 0, False)
+    I(T.r2i[:, :], [[0, 8], [1, 8]], 8 - s, 0, False)
+    p1 = pn[0]
+
+    fc = lambda i: T.fc[:, i:i + 1]
+    KAP8, TY, K32, R16, HALF = [T.kf[:, i:i + 1] for i in range(5)]
+    UO = T.bt[:, 0:1]
+    k1, k2 = ords.index(1), ords.index(2)
+
+    fill(T.wr[:, :], 0.0)
+    fill(T.cr[:, :], 0.0)
+    fence()
+    for i in range(N):
+        fill(T.wr[:, i:i + 1], (s + ords[i] + 1) % N)
+        fill(T.wr[:, 8 + i:9 + i], (s + ords[i] + 2) % N if ords[i] + 1 < N else N)
+    fence()
+    V(vec.transpose(T.wc[:, :], T.wr[:, :]))
+    fill(T.cr[:, k1:k1 + 1], 1.0)
+    fill(T.cr[:, 8:16], -1.0)
+    fill(T.cr[:, 32 + k2:33 + k2], 1.0)
+    fill(T.cr[:, 72:80], -1.0)
+    fence()
+    vec.wait_ge(sem.p, 1)
+    ts(T.tn[:, :], T.ic[:, 0:8], T.wc[:, 0:1], None, A.is_equal)
+
+    vec.wait_ge(sem.ld, 128)
+    cp(T.cu1[:, :], T.c1b[:, :])
+    fence()
+    cp(T.gn[:, :], T.tn[:, 0:8].indirect(T.cu1[:, 0:8]))
+    fence()
+    V(vec.tensor_reduce(fc(3), T.gn[:, :], X, A.add))
+    fence()
+    ts(T.e1[:, :], T.cr[:, :], fc(3), None, A.mult)
+    fence()
+    V(vec.transpose(T.e1t[:, :], T.e1[:, :]))
+    fence()
+    tt(T.info1[:, 0:16:2], T.e1t[:, 0:8], T.e1t[:, 40:48], A.add)
+    cp(T.info1[:, 1:16:2], T.e1t[:, 72:80])
+    m1 = fence()
+
+    off = topo.engines(core, at(T, topo, s, direct[0]))
+    on = [e for e in topo.engines(core, rc[0]) if e not in off]
+    half = [on[0:4], on[4:8]]
+    grp = [off[0:4], off[4:8]] + half
+    to = [rc[0], rs[0], rc[1], rs[1]]
+
+    def to_plane(info, land, isem):
+        tr = []
+        for i, u in enumerate(direct):
+            b, c = 2 * ords.index(u), 8 + 2 * (slot_of(u) - 1)
+            tr.append(xfer(core, at(T, topo, s, u), topo, off[2 * i:2 * i + 2], isem, info[:, b:b + 2], land[:, c:c + 2]))
+        g.remote_dma_fused(tr, local_sem=sem.lo)
+
+    g.wait_ge(sem.v, m1)
+    g.remote_dma_fused([xfer(core, to[j], topo, grp[j], sem.i1, T.info1[:, 2 + 2 * j:4 + 2 * j], T.hand1[:, :])
+                        for j in range(4)], local_sem=sem.lo)
+    to_plane(T.info1, T.land1, sem.i1)
+    I(T.x16[:, :], [[0, 24], [1, 16]], 0)
+    px = pn[0]
+    I(T.k32[:, :], [[0, 10], [1, 32]], 0)
+    I(T.val0[:, :], [[32, 4], [1, 16]], 0)
+    I(T.jw0[:, :], [[16, 10]], 0)
+    p2 = pn[0]
+    I(T.jd[:, :], [[16, 10], [0, 2], [1, 16]], 0)
+    p3 = pn[0]
+
+    ISS, ISF, ISN = fc(4), fc(5), fc(6)
+    vec.wait_ge(sem.p, p1)
+    cp(T.bo[:, 8:16], T.bo[:, 0:8])
+    ts(T.kk[:, 0:1], T.pi[:, :], 7, None, A.bitwise_and)
+    ts(T.kk[:, 1:2], T.pi[:, :], 3, 3, A.logical_shift_right, A.bitwise_and)
+    ts(T.kk[:, 2:3], T.pi[:, :], 31, None, A.bitwise_and)
+    ts(T.kk[:, 3:4], T.pi[:, :], 15, None, A.bitwise_and)
+    ts(T.kk[:, 4:5], T.pi[:, :], 4, 1, A.logical_shift_right, A.bitwise_and)
+    ts(T.r1[:, :], T.r1i[:, :], 7, None, A.bitwise_and)
+    ts(T.r2[:, :], T.r2i[:, :], 7, None, A.bitwise_and)
+    vec.wait_ge(sem.le, 128)
+    ts(T.cm[:, :], T.c1b[:, :], 8, None, A.mult)
+    fence()
+    cp(T.bo[:, 16:32], T.bo[:, 0:16])
+    cp(T.kf[:, 0:5], T.kk[:, 0:5])
+    tt(T.cs[:, :], T.cm[:, :], T.c2b[:, :], A.add)
+    fence()
+    V(vec.transpose(T.bt[:, :], T.bo[:, :]))
+    ts(ISS, TY, 1.0, None, A.is_equal)
+    ts(ISF, TY, 0.0, None, A.is_equal)
+    ts(ISN, TY, 2.0, None, A.is_equal)
+    ts(T.tb[:, :], T.r1[:, :], 2.0, None, A.is_equal)
+    fence()
+    ts(fc(7), UO, -1.0, 1.0, A.mult, A.add)
+    ts(T.te[:, :], T.r1[:, :], UO, None, A.is_equal)
+    ts(T.eq2[:, :], T.r2[:, :], UO, None, A.is_equal)
+    ts(fc(9), ISS, -1.0, 1.0, A.mult, A.add)
+    fence()
+    ts(fc(8), fc(7), ISS, UO, A.mult, A.add)
+    cp(T.cu[:, :], T.cs[:, :])
+    ts(T.eqb[:, :], T.eq2[:, :], ISS, None, A.mult)
+    ts(T.eqa[:, :], T.eq2[:, :], fc(9), None, A.max)
+    fence()
+    ts(T.ta[:, :], T.r1[:, :], fc(8), None, A.is_equal)
+    tt(T.tib[:, :], T.tb[:, :], T.eqb[:, :], A.mult)
+    fence()
+    tt(T.tia[:, :], T.ta[:, :], T.eqa[:, :], A.mult)
+    m2 = fence()
+
+    act.wait_ge(sem.p, px)
+    S(act.activation(T.win[:, :], T.x16[:, :], Copy, scale=0.0))
+    S(act.activation(T.vv[:, :], T.x16[:, 0:32], Copy, scale=0.0))
+    act.wait_ge(sem.v, m2)
+    for out, tab in ((T.ga, T.ta), (T.gb, T.tb), (T.gia, T.tia), (T.gib, T.tib), (T.ge, T.te)):
+        S(act.activation(out[:, :], tab[:, 0:64].indirect(T.cu[:, 0:8]), Copy))
+    a1 = an[0]
+    act.dma_start(T.wt[:, :], T.w[:, :]).then_inc(sem.lw, 16)
+
+    fill(T.zt[:, 0:128], 0.0)
+    fill(T.land1[:, 0:8], 0.0)
+    tt(fc(10), ISS, ISF, A.subtract)
+    ts(fc(11), TY, -64.0, 174.0, A.mult, A.add)
+    ts(fc(12), KAP8, 48.0, -1.0, A.mult, A.add)
+    ts(fc(13), UO, -1.0, 8.0, A.mult, A.add)
+    ts(fc(14), UO, 0.0, -8.0, A.is_equal, A.mult)
+    ts(fc(15), HALF, 16.0, None, A.mult)
+    fence()
+    ts(T.land1[:, 0:1], ISS, 225.0, 30.0, A.mult, A.add)
+    fill(T.land1[:, 1:2], 255.0)
+    tt(fc(16), fc(13), fc(14), A.add)
+    fence()
+    ts(fc(17), TY, 8.0, fc(16), A.mult, A.add)
+    ts(fc(18), fc(16), -8.0, ISN, A.add, A.mult)
+    ts(fc(19), ISN, -8.0, 1.0, A.mult, A.add)
+    fence()
+    ts(fc(20), fc(18), 16.0, None, A.add)
+    tt(fc(21), fc(17), fc(19), A.add)
+    vec.wait_ge(sem.a, a1)
+    scan(T.ca[:, :], T.ga[:, :], T.zt[:, 0:128], 0.0, A.add)
+    scan(T.cb[:, :], T.gb[:, :], T.zt[:, 0:128], 0.0, A.add)
+    V(vec.tensor_reduce(fc(22), T.ge[:, :], X, A.add))
+    fence()
+    ts(T.ya1[:, :], T.ca[:, :], fc(10), fc(11), A.mult, A.add)
+    ts(T.yb1[:, :], T.cb[:, :], 110.0, None, A.add)
+    ts(fc(23), fc(22), ISS, fc(12), A.mult, A.add)
+    fence()
+    tt(T.ya[:, :], T.ya1[:, :], T.gia[:, :], A.mult)
+    tt(T.yb[:, :], T.yb1[:, :], T.gib[:, :], A.mult)
+    BASE = fc(23)
+    ts(fc(33), BASE, -1.0, None, A.mult)
+    vec.wait_ge(sem.p, p2)
+    ts(T.c2c[:, 0:32], T.ic[:, :], fc(17), None, A.is_gt)
+    ts(T.cda[:, :], T.ic[:, :], fc(20), None, A.is_equal)
+    ts(T.cdb[:, :], T.ic[:, :], fc(21), None, A.is_equal)
+    ts(T.kp[:, 0:128], T.k32[:, 0:128], 1.0, None, A.min)
+    ts(T.kr[:, :], T.x16[:, :], R16, 256.0, A.is_gt, A.mult)
+    ts(T.sc0[:, :], T.x16[:, 0:16], R16, 1.0 / 256.0, A.is_gt, A.mult)
+    ts(T.sc1[:, :], T.x16[:, 0:16], R16, None, A.is_equal)
+    ts(T.val[:, :], T.val0[:, :], fc(15), None, A.add)
+    fence()
+    tt(T.c2c[:, 32:64], T.cda[:, :], T.cdb[:, :], A.subtract)
+    scan(T.scl[:, :], T.sc0[:, :], T.sc1[:, :], 0.0, A.mult)
+    vec.wait_ge(sem.lx, 16)
+    V(vec.quantize_mx(T.xq[:, 0:128], T.xz[:, 0:128], T.xt[:, :]))
+    fence()
+
+    n1 = n2 = 0
+    for u in range(1, N):
+        here = u in order(T, topo, (s - u) % N)[1]
+        n1 += 2 if here else 8
+        n2 += 2 if here else 4
+    vec.wait_ge(sem.i1, n1)
+    V(vec.tensor_reduce(fc(24), T.land1[:, 0:22:2], X, A.add))
+    V(vec.tensor_reduce(fc(25), T.land1[:, 1:22:2], X, A.add))
+    fence()
+    ts(T.xa[:, :], T.ya[:, :], fc(24), None, A.is_ge)
+    ts(T.xb[:, :], T.yb[:, :], fc(25), None, A.is_ge)
+    fence()
+    scan(T.cum[:, :], T.xa[:, :], T.xb[:, :], BASE, A.add)
+    tt(T.xs[:, :], T.xa[:, :], T.xb[:, :], A.add)
+    mc = fence()
+    act.wait_ge(sem.v, mc)
+    S(act.activation(fc(26), T.cum[:, 127:128], Ident, bias=fc(33)))
+    act.wait_ge(sem.a, an[0])
+    S(act.activation(T.e2[:, :], T.c2c[:, :], Copy, scale=fc(26)))
+    tt(T.mm[:, :], T.xs[:, :], T.cum[:, :], A.mult)
+    fence()
+    V(vec.transpose(T.mt[:, :], T.mm[:, :]))
+    fence()
+    scan(T.ss[:, :], T.kp[:, 0:128], T.mt[:, :], 0.0, A.mult)
+    vec.wait_ge(sem.a, an[0])
+    V(vec.transpose(T.e2t[:, :], T.e2[:, :]))
+    fence()
+    cp(T.so[:, :], T.ss[:, 15:128:32])
+    tt(T.info2[:, 0:16:2], T.e2t[:, 0:8], T.e2t[:, 8:16], A.add)
+    tt(T.e2s[:, :], T.e2t[:, 32:40], T.e2t[:, 40:48], A.add)
+    m3 = fence()
+    vec.tensor_tensor(T.info2[:, 1:16:2], T.e2s[:, :], T.e2t[:, 48:56], A.add).then_inc(sem.n2, 1)
+    cp(T.win[:, 0:384].indirect(T.so[:, 0:4]), T.val[:, :])
+    fence()
+    scan(T.rr[:, :], T.kr[:, :], T.win[:, :], 0.0, A.mult)
+    fence()
+    ts(T.vv[:, 0:16:2], T.rr[:, 15:384:48], T.scl[:, 15:16], None, A.mult)
+    ts(T.vv[:, 1:16:2], T.rr[:, 31:384:48], T.scl[:, 15:16], None, A.mult)
+    fence()
+    V(vec.transpose(T.vt[:, :], T.vv[:, :]))
+    fence()
+    tt(T.v2[:, 0:16], T.vt[:, 0:16], T.vt[:, 16:32], A.add)
+    tt(T.v2[:, 16:32], T.vt[:, 0:16], T.vt[:, 16:32], A.add)
+    fence()
+    V(vec.transpose(T.vb[:, :], T.v2[:, :]))
+    fence()
+    cp(T.offp[:, :], T.vb[:, 0:16])
+    m4 = fence()
+
+    xc = lambda a, b: T.xq[:, 0:128].bitcast(dt.uint32).indirect(T.offp[:, a:b])
+    xz = lambda a, b: T.xz[:, 0:128].indirect(T.offp[:, a:b])
+    vec.tensor_copy(T.oq[:, 32:160].bitcast(dt.uint32), xc(2, 10)).then_inc(sem.pc1, 1)
+    vec.tensor_copy(T.oq[:, 160:256].bitcast(dt.uint32), xc(10, 16)).then_inc(sem.pc2, 1)
+    cp(T.lq[:, 0:32].bitcast(dt.uint32), xc(0, 2))
+    act.wait_ge(sem.v, m4)
+    act.activation(T.oz[:, 32:160], xz(2, 10), Copy).then_inc(sem.pa1, 1)
+    act.activation(T.oz[:, 160:256], xz(10, 16), Copy).then_inc(sem.pa2, 1)
+    S(act.activation(T.lz[:, 0:32], xz(0, 2), Copy))
+
+    g.wait_ge(sem.v, m3)
+    g.wait_ge(sem.n2, 1)
+    g.remote_dma_fused([xfer(core, rc[h], topo, half[h], sem.i2, T.info2[:, 2 + 4 * h:6 + 4 * h], T.hand2[:, :])
+                        for h in range(2)], local_sem=sem.lo)
+    to_plane(T.info2, T.land2, sem.i2)
+    g.wait_ge(sem.pc1, 1)
+    g.remote_dma_fused([xfer(core, rc[h], topo, (off, on)[h], sem.tc, T.oq[:, 32 + 64 * h:96 + 64 * h].bitcast(dt.uint8),
+                             T.rq[:, :].bitcast(dt.uint8)) for h in range(2)], local_sem=sem.lo)
+    g.wait_ge(sem.pa1, 1)
+    g.remote_dma_fused([xfer(core, rs[h], topo, half[h], sem.ts, T.oz[:, 32 + 64 * h:96 + 64 * h],
+                             T.rz[:, :]) for h in range(2)], local_sem=sem.lo)
+    g.wait_ge(sem.pc2, 1)
+    tr = []
+    for i, u in enumerate(direct):
+        b, c = W * ords.index(u), W * slot_of(u)
+        x, y = SPLIT_C[i]
+        tr.append(xfer(core, at(T, topo, s, u), topo, off[x:y], sem.tc, T.oq[:, b:b + W].bitcast(dt.uint8),
+                       T.lq[:, c:c + W].bitcast(dt.uint8)))
+    g.remote_dma_fused(tr, local_sem=sem.lo)
+    g.wait_ge(sem.pa2, 1)
+    tr = []
+    for i, u in enumerate(direct):
+        b, c = W * ords.index(u), W * slot_of(u)
+        x, y = SPLIT_S[i]
+        tr.append(xfer(core, at(T, topo, s, u), topo, off[x:y], sem.ts, T.oz[:, b:b + W], T.lz[:, c:c + W]))
+    g.remote_dma_fused(tr, local_sem=sem.lo)
+    g.wait_ge(sem.lo, 22 + 14 + 16 + 3 * 8)
+
+    fill(T.zt[:, 128:640], 0.0)
+    fill(T.land2[:, 0:8], 0.0)
+    ts(T.kp[:, 128:320], T.k32[:, 128:320], 1.0, None, A.min)
+    fence()
+    V(vec.quantize_mx(T.lq[:, LAND:LAND + ROOM], T.lz[:, LAND:LAND + ROOM], T.zt[:, :]))
+    vec.wait_ge(sem.n2, 1)
+    cp(T.land2[:, 0:2], T.info2[:, 0:2])
+    ts(fc(27), K32, 1.0, 32.0, A.is_ge, A.mult)
+    ts(fc(28), K32, 17.0, -32.0, A.is_ge, A.mult)
+    ts(fc(29), K32, 8.0, -256.0, A.is_equal, A.mult)
+    ts(T.jw[:, :], T.jw0[:, :], R16, None, A.add)
+    fence()
+    tt(fc(30), fc(27), fc(28), A.add)
+    fence()
+    tt(T.land2[:, 3:4], fc(30), fc(29), A.add)
+    vec.wait_ge(sem.lw, 16)
+    for o in range(O):
+        V(vec.quantize_mx(T.wq[:, 128 * o:128 * o + 128], T.wz[:, 128 * o:128 * o + 128], T.wt[:, 512 * o:512 * o + 512]))
+    fence()
+
+    vec.wait_ge(sem.p, p3)
+    vec.wait_ge(sem.i2, n2)
+    V(vec.tensor_reduce(fc(31), T.land2[:, 0:22:2], X, A.add))
+    V(vec.tensor_reduce(fc(32), T.land2[:, 1:22:2], X, A.add))
+    fence()
+    ts(T.st[:, :], T.jd[:, :], fc(31), fc(32), A.is_ge, A.mult)
+    fence()
+    V(vec.transpose(T.stt[:, :], T.st[:, :]))
+    fence()
+    scan(T.sw[:, :], T.kp[:, :], T.stt[:, :], 0.0, A.mult)
+    fence()
+    tt(T.wl[:, :], T.sw[:, 31:320:32], T.jw[:, :], A.add)
+    fence()
+    cp(T.offh[:, :], T.wl[:, :])
+    m5 = fence()
+
+    nt = 0
+    for u in range(1, N):
+        d = order(T, topo, (s - u) % N)[1]
+        nt += SPLIT_C[d.index(u)][1] - SPLIT_C[d.index(u)][0] if u in d else 4
+    act.wait_ge(sem.v, m5)
+    act.wait_ge(sem.a, an[0])
+    act.wait_ge(sem.ts, nt)
+    S(act.activation(T.hz[:, 0:160], T.lz[:, 0:416].indirect(T.offh[:, 0:10]), Copy))
+    a2 = an[0]
+    vec.wait_ge(sem.tc, nt)
+    cp(T.hq[:, 0:160].bitcast(dt.uint32), T.lq[:, 0:416].bitcast(dt.uint32).indirect(T.offh[:, 0:10]))
+    m6 = vn[0]
+    ten.wait_ge(sem.v, m6)
+    ten.wait_ge(sem.a, a2)
+    for o in range(O):
+        ten.matmul_mx(T.ps[:, 512 * o:512 * o + ROOM], T.wq[:, 128 * o:128 * o + 128], T.wz[:, 128 * o:128 * o + 128],
+                      T.hq[:, 0:ROOM], T.hz[:, 0:ROOM], True, True).then_inc(sem["t%d" % o], 1)
+    for o in range(O):
+        y, p = T.ys[:, ROOM * o:ROOM * o + ROOM], T.ps[:, 512 * o:512 * o + ROOM]
+        if o % 2 == 0:
+            vec.wait_ge(sem["t%d" % o], 1)
+            vec.tensor_copy(y, p).then_inc(sem["y%d" % o], 1)
+        else:
+            act.wait_ge(sem["t%d" % o], 1)
+            act.activation(y, p, Copy).then_inc(sem["y%d" % o], 1)
+    for q, o, e in ((g.sync, 0, 1), (act, 1, 4)):
+        for k in range(o, e):
+            q.wait_ge(sem["y%d" % k], 1)
+        q.dma_start(T.y[:, ROOM * o:ROOM * e], T.ys[:, ROOM * o:ROOM * e]).then_inc(sem.ly, 16)
+    act.wait_ge(sem.ly, 32)

@@ -4,30 +4,31 @@ from concourse.mybir import dt, AluOpType, AxisListType, ActivationFunctionType
 
 N = 8
 CAP, ROOM, O = 144, 160, 4
-W = 32
-LAND = N * W
+PAIR, MOVE, BOTH = 24, 8, 30
+B = 48
+Z = B * (N + 1)
+NOKEY = 24.0
+SC = 1.0 / 1024
 
 F4, B2, I4, U2, MX, U1 = "float32", "bfloat16", "int32", "uint16", "float8_e4m3fn_x4", "uint8"
 SIZES = {
-    I4: dict(c1b=8, c2b=8, cm=8, cs=8, pi=1, kk=8, r1i=64, r2i=64, r1=64, r2=64),
-    U2: dict(cu=8, cu1=8, so=4, offp=16, offh=10),
-    F4: dict(kf=8, bo=32, bt=32, wr=32, wc=32, ic=32, jw0=10, jw=10, val0=64, val=64, sc0=16, sc1=16, scl=16, fc=48,
-             cum=128, mm=128, mt=128, ss=128, win=384, rr=384, vv=32, vt=32, v2=32, vb=32, sw=320, wl=10, ys=640),
-    B2: dict(cr=96, c2c=64, cda=32, cdb=32, ca=128, cb=128, ya1=128, yb1=128, e1=96, e1t=96, e2=64, e2t=64, e2s=8,
-             k32=320, x16=384, kr=384, kp=320, jd=320, st=320, stt=320,
-             tn=8, ta=64, tb=64, te=64, tia=64, tib=64, eq2=64, eqa=64, eqb=64, gn=128, ga=128, gb=128, ge=128, gia=128,
-             gib=128, ya=128, yb=128, xa=128, xb=128, xs=128,
-             info1=16, info2=16, hand1=2, hand2=4, land1=22, land2=22,
-             xt=512, wt=2048, zt=640),
-    MX: dict(xq=128, wq=512, oq=256, rq=64, lq=416, hq=160),
-    U1: dict(xz=128, wz=512, oz=256, rz=64, lz=416, hz=160),
+    I4: dict(c1b=8, c2b=8, cm=8, cs=10, yi=64, yr=64, si=16, sj=16, zi=4),
+    U2: dict(cu1=8, cu=16, sh=2, cl=8, so=16, offp=48, kq=16, kl=2, km=2, lk=8, hand2=4, sl=16, rl=6, offl=2, offh=10),
+    F4: dict(r0=32, k0=32, ra=192, ka=192, rb=128, kb=128, rc=96, kc=96, k16=16, yc=64, sg=160, tq=10, fc=32,
+             d0i=128, d0=130, dl=16, jw=10, jm=10, st=96, stt=96, sw=96, ga0=10, msk=10, mm4=80, ms=80, wv=390,
+             ys=640, xal=16, xbl=16, wl=32, rep=96, rpt=96),
+    B2: dict(one=256, ident=256, kp=96, tn=8, gn=160, cnt=160, own=32, ta=80, tb=80, ga=160, gb=160, ca=160, cb=160,
+             ua=160, ub=160, xa=160, xb=160, xs=160, cum=160, mm=160, mt=160, win=288, wt1=544, key=128, win2=288, wt2=544,
+             thr=96, hand1=2, land1=48, sc=40, tot=32, sa=112, sb=112, fa=146, fb=146, w1=390, vl=32, jd=96,
+             xt=512, wt=2048, zt=512),
+    MX: dict(xq=128, wq=512, oq=288, pq=64, o2q=32, rq=136, lq=560, hq=160),
+    U1: dict(xz=128, wz=512, oz=288, pz=64, o2z=32, rz=136, lz=560, hz=160),
 }
 SCRATCH = {"ps": ("psum", [128, 2048], F4)}
 for _d in SIZES:
     for _n in SIZES[_d]:
         SCRATCH[_n] = ("sbuf", [128, SIZES[_d][_n]], _d)
-SEMAPHORES = ["v", "a", "p", "ld", "le", "lx", "lw", "ly", "i1", "i2", "tc", "ts", "lo", "pc1", "pc2", "pa1", "pa2", "n2",
-              "t0", "t1", "t2", "t3", "y0", "y1", "y2", "y3"]
+SEMAPHORES = ["i1", "i2", "il", "tc", "ts", "lo"] + ["s%d" % _i for _i in range(144)]
 
 
 def bits(es):
@@ -37,28 +38,23 @@ def bits(es):
     return m
 
 
-def at(T, topo, s, u):
+def at(T, s, u):
     return T.cores[(s + u) % N]
 
 
-def order(T, topo, s):
-    cross = [u for u in range(1, N) if not topo.may_write(T.cores[s], at(T, topo, s, u))]
+def roads(T, topo, s):
+    cross = [u for u in range(1, N) if not topo.may_write(T.cores[s], at(T, s, u))]
     direct = [u for u in range(1, N) if u not in cross]
-    return cross, direct
+    return cross, direct, [u for u in direct if u > 2][0]
 
 
 def relays(T, topo, s):
     me = T.cores[s]
-    cross, _ = order(T, topo, s)
     r = [c for c in topo.cores_of(me) if c != me and T.rank_of(c) is None
-         and all(topo.may_write(c, at(T, topo, s, u)) for u in cross)]
+         and all(topo.may_write(c, at(T, s, u)) for u in range(1, N))]
     near = [c for c in r if topo.die(c) == topo.die(me)]
     far = [c for c in r if topo.die(c) != topo.die(me)]
-    return [near[0], far[0]], [far[1], near[1]]
-
-
-SPLIT_C = ((0, 2), (2, 4), (4, 8))
-SPLIT_S = ((4, 6), (6, 8), (0, 4))
+    return [far[0], near[0], near[1], far[1]]
 
 
 def xfer(core, d, topo, es, sem, src, dst):
@@ -66,42 +62,44 @@ def xfer(core, d, topo, es, sem, src, dst):
     return RemoteDMATransfer(dst_ids=[DstId(rid=rid, pnc=pid)], dma_engine_mask=bits(es), remote_sem=sem, src=src, dst=dst)
 
 
-def slot_of(u):
-    return (N - u) % N
+def skip(u):
+    return MOVE if u <= 2 else 0
 
 
 def hand_on(g, core, T, topo):
     for s in range(N):
-        cross, _ = order(T, topo, s)
-        rc, rs = relays(T, topo, s)
-        if core not in rc + rs:
+        rel = relays(T, topo, s)
+        if core not in rel:
             continue
-        codes = core in rc
-        h = (rc if codes else rs).index(core)
-        us = cross[2 * h:2 * h + 2]
-        dst = [at(T, topo, s, u) for u in us]
-        es = [topo.engines(core, d) for d in dst]
-        col = [8 + 2 * (slot_of(u) - 1) for u in us]
-        j = 0 if codes else 1
+        cross, _, late = roads(T, topo, s)
+        j = rel.index(core)
+        codes, h = j < 2, j % 2
+        us = [u for u in range(1, N) if u != late][3 * h:3 * h + 3]
+        es = topo.engines(core, at(T, s, us[0]))
+        share = [es[0:4], es[4:8], es]
+
+        def two_calls(sem, piece):
+            tr = [xfer(core, at(T, s, u), topo, share[i], sem, *piece(i, u)) for i, u in enumerate(us)]
+            g.remote_dma_fused(tr[0:2], local_sem=T.sem.lo)
+            g.remote_dma_fused(tr[2:3], local_sem=T.sem.lo)
+
+        def block(a, b, i, u):
+            c, w = B * (N - u + 1) + skip(u), 16 + PAIR - skip(u)
+            return a[:, B * i + skip(u):B * i + skip(u) + w], b[:, c:c + w]
+
+        c = 8 + N - cross[j]
         g.wait_ge(T.sem.i1, 4)
-        g.remote_dma_fused([xfer(core, dst[j], topo, es[j], T.sem.i1, T.hand1[:, :], T.land1[:, col[j]:col[j] + 2])],
+        g.remote_dma_fused([xfer(core, at(T, s, cross[j]), topo, es, T.sem.i1, T.hand1[:, 0:1], T.land1[:, c:c + 1])],
                            local_sem=T.sem.lo)
-        es = [es[0][0:4], es[1][4:8]]
         if codes:
+            g.wait_ge(T.sem.tc, 16)
+            two_calls(T.sem.tc, lambda i, u: [v.bitcast(dt.uint8) for v in block(T.rq, T.lq, i, u)])
+        else:
             g.wait_ge(T.sem.i2, 4)
-            g.remote_dma_fused([xfer(core, dst[i], topo, es[i], T.sem.i2, T.hand2[:, 2 * i:2 * i + 2],
-                                     T.land2[:, col[i]:col[i] + 2]) for i in range(2)], local_sem=T.sem.lo)
-        tr = []
-        for i, u in enumerate(us):
-            c = W * slot_of(u)
-            if codes:
-                a, b = T.rq[:, W * i:W * i + W].bitcast(dt.uint8), T.lq[:, c:c + W].bitcast(dt.uint8)
-            else:
-                a, b = T.rz[:, W * i:W * i + W], T.lz[:, c:c + W]
-            tr.append(xfer(core, dst[i], topo, es[i], T.sem.tc if codes else T.sem.ts, a, b))
-        g.wait_ge(T.sem.tc if codes else T.sem.ts, 8 if codes else 4)
-        g.remote_dma_fused(tr, local_sem=T.sem.lo)
-        g.wait_ge(T.sem.lo, 24 if codes else 16)
+            two_calls(T.sem.i2, lambda i, u: (T.hand2[:, i:i + 1], T.lk[:, N - u - 1:N - u]))
+            g.wait_ge(T.sem.ts, 8)
+            two_calls(T.sem.ts, lambda i, u: block(T.rz, T.lz, i, u))
+        g.wait_ge(T.sem.lo, 24 if codes else 40)
         return
 
 
@@ -110,387 +108,402 @@ def rank_program(g, core, T, topo):
     if s is None:
         hand_on(g, core, T, topo)
         return
-    A, X = AluOpType, AxisListType.X
+    A = AluOpType
     Copy, Ident = ActivationFunctionType.Copy, ActivationFunctionType.Identity
     sem = T.sem
-    vec, act, ten = g.vector, g.scalar, g.tensor
-    cross, direct = order(T, topo, s)
-    ords = [0] + cross + direct
-    rc, rs = relays(T, topo, s)
+    vec, act, ten, syn = g.vector, g.scalar, g.tensor, g.sync
+    cross, direct, late = roads(T, topo, s)
+    rel = relays(T, topo, s)
+    U32 = dt.uint32
 
-    vn, vw = [0], [0]
+    steps, seen = {}, set()
 
-    def V(ins):
-        ins.then_inc(sem.v, 1)
-        vn[0] += 1
+    def done(ins, step, n=1):
+        if step not in steps:
+            steps[step] = [sem["s%d" % len(steps)], 0]
+        steps[step][1] += n
+        ins.then_inc(steps[step][0], n)
 
-    def fence():
-        if vw[0] < vn[0]:
-            vec.wait_ge(sem.v, vn[0])
-            vw[0] = vn[0]
-        return vn[0]
+    def need(q, *names):
+        for nm in names:
+            if (q[0], nm) not in seen:
+                seen.add((q[0], nm))
+                q[1].wait_ge(steps[nm][0], steps[nm][1])
 
-    def ts(out, in0, a, b, op0, op1=None):
-        if op1 is None:
-            V(vec.tensor_scalar(out, in0, a, None, op0))
+    QV, QA, QG, QT, QS = ("v", vec), ("a", act), ("g", g), ("t", ten), ("s", syn)
+
+    def ts(step, out, in0, a, b, op0, op1=None):
+        done(vec.tensor_scalar(out, in0, a, None, op0) if op1 is None else vec.tensor_scalar(out, in0, a, b, op0, op1), step)
+
+    def tt(step, out, a, b, op):
+        done(vec.tensor_tensor(out, a, b, op), step)
+
+    def cp(step, out, a):
+        done(vec.tensor_copy(out, a), step)
+
+    def fill(step, out, c):
+        done(vec.memset(out, c), step)
+
+    def scan(step, out, a, b, ini, op0=A.add, op1=A.add):
+        done(vec.tensor_tensor_scan(out, a, b, ini, op0, op1), step)
+
+    def turn(step, out, a):
+        done(vec.transpose(out, a), step)
+
+    def lin(step, out, a, scale=1.0, bias=0.0):
+        done(act.activation(out, a, Copy, bias=float(bias), scale=float(scale)), step)
+
+    def shift(step, out, a, scale, bias):
+        done(act.activation(out, a, Ident, bias=bias, scale=float(scale)), step)
+
+    def take(step, out, a):
+        done(act.activation(out, a, Copy), step)
+
+    def iota(step, out, pattern, base, whole=False):
+        if whole:
+            done(g.iota(out, pattern, base, 0), step)
         else:
-            V(vec.tensor_scalar(out, in0, a, b, op0, op1))
+            done(g.iota(out, pattern, base, 0, allow_small_or_imprecise_dtypes=True), step)
 
-    def tt(out, a, b, op):
-        V(vec.tensor_tensor(out, a, b, op))
+    V = lambda *n: need(QV, *n)
+    S = lambda *n: need(QA, *n)
+    G = lambda *n: need(QG, *n)
+    col = lambda t, i: t[:, i:i + 1]
+    fc = lambda i: col(T.fc, i)
+    g1, g2, gl = (s + 1) % N, (s + 2) % N, (s + late) % N
 
-    def cp(out, a):
-        V(vec.tensor_copy(out, a))
-
-    def fill(out, c):
-        V(vec.memset(out, c))
-
-    def scan(out, a, b, ini, op0):
-        V(vec.tensor_tensor_scan(out, a, b, ini, op0, A.add))
-
-    an = [0]
-
-    def S(ins):
-        ins.then_inc(sem.a, 1)
-        an[0] += 1
-
-    pn = [0]
-
-    def I(out, pattern, base, cm=0, f=True):
-        if f:
-            g.iota(out, pattern, base, cm, allow_small_or_imprecise_dtypes=True).then_inc(sem.p, 1)
-        else:
-            g.iota(out, pattern, base, cm).then_inc(sem.p, 1)
-        pn[0] += 1
-
-    for big, src, sm in ((T.c1b, T.c1, sem.ld), (T.c2b, T.c2, sem.le)):
+    for big, src, nm in ((T.c1b, T.c1, "c1"), (T.c2b, T.c2, "c2")):
         for q in range(8):
-            dq = g.sync if q % 2 else act
-            dq.dma_start(big[16 * q:16 * q + 16, :], src[:, :]).then_inc(sm, 16)
-    g.sync.dma_start(T.xt[:, :], T.x[:, :]).then_inc(sem.lx, 16)
+            done((syn if q % 2 else act).dma_start(big[16 * q:16 * q + 16, :], src[:, :]), nm, 16)
+    done(syn.dma_start(T.xt[:, :], T.x[:, :]), "x", 16)
+    done(syn.dma_start(T.wt[:, :], T.w[:, :]), "w", 16)
 
-    I(T.ic[:, :], [[1, 32]], 0)
-    I(T.pi[:, :], [[0, 1]], 0, 1, False)
-    k = 0
-    while k < N:
-        n = 1
-        step = ords[k + 1] - ords[k] if k + 1 < N else 0
-        while k + n < N and ords[k + n] - ords[k + n - 1] == step:
-            n += 1
-        I(T.bo[:, k:k + n], [[step, n]], ords[k])
-        k += n
-    I(T.r1i[:, :], [[1, 8], [0, 8]], 8 - s, 0, False)
-    I(T.r2i[:, :], [[0, 8], [1, 8]], 8 - s, 0, False)
-    p1 = pn[0]
+    iota("r0", T.r0[:, :], [[1, 8], [0, 4]], 0)
+    iota("k16", T.k16[:, :], [[0, 2], [1, 8]], 0)
+    iota("yi", T.yi[:, :], [[32, 8], [1, 8]], 33 * (N - 1 - s), True)
+    iota("ra0", T.ra[:, 0:32], [[-1, 2], [1, 16]], 1)
+    iota("rb", T.rb[:, 0:16], [[0, 2], [16, 4], [24, 2]], 7)
+    iota("rb", T.rb[:, 16:32], [[-80, 2], [16, 4], [-8, 2]], 95)
+    iota("rb", T.rb[:, 32:48], [[0, 2], [32, 4], [-256, 2]], 432)
+    iota("rb", T.rb[:, 48:64], [[0, 2], [32, 4], [288, 2]], 144)
+    iota("rb", T.rb[:, 64:96], [[-288, 2], [0, 2], [32, 8]], 288)
+    iota("rb", T.rb[:, 96:128], [[256, 2], [0, 2], [32, 8]], 32)
 
-    fc = lambda i: T.fc[:, i:i + 1]
-    KAP8, TY, K32, R16, HALF = [T.kf[:, i:i + 1] for i in range(5)]
-    UO = T.bt[:, 0:1]
-    k1, k2 = ords.index(1), ords.index(2)
+    fill("one", T.one[:, :], 1.0)
+    fill("z0", T.gn[:, 128:160], 0.0)
+    fill("z0", T.cs[:, 0:10:9], 64)
+    fill("z0", T.ta[:, 64:80], 0.0)
+    fill("z0", T.tb[:, 64:80], 0.0)
+    V("one", "r0")
+    scan("ident", T.ident[:, :], T.one[:, :], T.one[:, :], -1.0, A.add, A.mult)
+    fill("r0x", T.r0[:, 4 * g1 + 1:4 * g1 + 3], 99.0)
+    fill("r0x", col(T.r0, 4 * g2 + 2), 99.0)
+    fill("z1", T.win[:, :], 0.0)
+    V("r0x")
+    turn("k0", T.k0[:, :], T.r0[:, :])
+    fill("z1", T.win2[:, :], NOKEY)
+    fill("kp1", T.kp[:, :], 1.0)
+    V("k0", "ident", "yi", "kp1")
+    ts("tn", T.tn[:, :], T.ident[:, 0:8], col(T.k0, 0), None, A.is_equal)
+    ts("yr", T.yr[:, :], T.yi[:, :], 0xE7, None, A.bitwise_and)
+    fill("kp", T.kp[:, 0:96:8], 0.0)
 
-    fill(T.wr[:, :], 0.0)
-    fill(T.cr[:, :], 0.0)
-    fence()
-    for i in range(N):
-        fill(T.wr[:, i:i + 1], (s + ords[i] + 1) % N)
-        fill(T.wr[:, 8 + i:9 + i], (s + ords[i] + 2) % N if ords[i] + 1 < N else N)
-    fence()
-    V(vec.transpose(T.wc[:, :], T.wr[:, :]))
-    fill(T.cr[:, k1:k1 + 1], 1.0)
-    fill(T.cr[:, 8:16], -1.0)
-    fill(T.cr[:, 32 + k2:33 + k2], 1.0)
-    fill(T.cr[:, 72:80], -1.0)
-    fence()
-    vec.wait_ge(sem.p, 1)
-    ts(T.tn[:, :], T.ic[:, 0:8], T.wc[:, 0:1], None, A.is_equal)
+    S("k16")
+    for b, (f, c) in enumerate((((32, 0), (1, 0)), ((32, 7), (1, 0)), ((0, 999), (1, 32)), ((32, -1), (16, 127)),
+                                ((0, -999), (0, -MOVE)))):
+        lin("ra", T.ra[:, 32 * b + 32:32 * b + 64:2], T.k16[:, :], *f)
+        lin("ra", T.ra[:, 32 * b + 33:32 * b + 64:2], T.k16[:, :], *c)
+    S("ra")
+    lin("rax", T.ra[:, 129:160:16], T.k16[:, 0:2], 0, 127 + MOVE)
+    lin("rax", T.ra[:, 131:160:16], T.k16[:, 0:2], 0, 143 + MOVE)
+    V("ra0", "rax")
+    turn("ka", T.ka[:, :], T.ra[:, :])
+    SH, LO, HI, TB, BASE = [col(T.ka, 32 * i) for i in range(5)]
+    LIM = col(T.fa, 145)
+    S("one", "ident")
+    lin("z4", T.wt2[:, 0:128], T.one[:, 0:128], 0.0)
+    lin("z4", T.wt2[:, 288:416], T.one[:, 0:128], 0.0)
+    lin("thr1", T.thr[:, :], T.one[:, 0:96], 255.0)
+    lin("z2", T.land1[:, 16:48], T.one[:, 0:32], 0.0)
+    lin("dl", T.dl[:, :], T.ident[:, 48:64], -1.0 / 64)
+    lin("z3", col(T.fa, 144), col(T.one, 0), 200.0)
+    lin("z3", col(T.fb, 144), col(T.one, 0), 0.0)
+    lin("z3", T.mm4[:, :], T.one[:, 0:80], 0.0)
+    lin("z3", col(T.d0, 128), col(T.one, 0), 0.0)
+    S("thr1", "ka")
+    lin("thr", T.thr[:, 32:32 + PAIR], T.ident[:, 0:PAIR], -1.0, CAP)
+    take("thr", LIM, col(T.ka, 160))
 
-    vec.wait_ge(sem.ld, 128)
-    cp(T.cu1[:, :], T.c1b[:, :])
-    fence()
-    cp(T.gn[:, :], T.tn[:, 0:8].indirect(T.cu1[:, 0:8]))
-    fence()
-    V(vec.tensor_reduce(fc(3), T.gn[:, :], X, A.add))
-    fence()
-    ts(T.e1[:, :], T.cr[:, :], fc(3), None, A.mult)
-    fence()
-    V(vec.transpose(T.e1t[:, :], T.e1[:, :]))
-    fence()
-    tt(T.info1[:, 0:16:2], T.e1t[:, 0:8], T.e1t[:, 40:48], A.add)
-    cp(T.info1[:, 1:16:2], T.e1t[:, 72:80])
-    m1 = fence()
+    V("c1")
+    cp("cu1", T.cu1[:, :], T.c1b[:, :])
+    ts("cm", T.cm[:, :], T.c1b[:, :], 8, None, A.mult)
+    V("cu1", "tn")
+    cp("gn", T.gn[:, 0:128], T.tn[:, 0:8].indirect(T.cu1[:, 0:8]))
+    V("ka", "yr")
+    ts("yc", T.yc[:, :], T.yr[:, :], LO, HI, A.max, A.min)
+    V("gn", "z0")
+    scan("cnt", T.cnt[:, :], T.gn[:, :], T.one[:, 0:160], 0.0, A.add, A.mult)
+    V("c2", "cm", "yc")
+    tt("cs", T.cs[:, 1:9], T.cm[:, :], T.c2b[:, :], A.add)
+    ts("sh", T.sh[:, 0:1], SH, 9.0, None, A.min)
+    tt("ta", T.ta[:, 0:64], T.yc[:, :], T.yr[:, :], A.is_equal)
+    V("cs", "sh")
+    cp("cu", T.cu[:, :], T.cs[:, 0:10].indirect(T.sh[:, 0:1]))
+    ts("tb", T.tb[:, 0:64], T.yr[:, :], TB, None, A.is_equal)
 
-    off = topo.engines(core, at(T, topo, s, direct[0]))
-    on = [e for e in topo.engines(core, rc[0]) if e not in off]
-    half = [on[0:4], on[4:8]]
-    grp = [off[0:4], off[4:8]] + half
-    to = [rc[0], rs[0], rc[1], rs[1]]
+    off = topo.engines(core, at(T, s, late))
+    on = [e for e in topo.engines(core, rel[0]) if e not in off]
+    CNT = col(T.cnt, 127)
+    G("cnt")
+    quarter = [off[0:4], off[4:8], on[0:4], on[4:8]]
+    g.remote_dma_fused([xfer(core, rel[j], topo, quarter[j], sem.i1, CNT, T.hand1[:, 0:1]) for j in range(4)], local_sem=sem.lo)
+    g.remote_dma_fused([xfer(core, at(T, s, u), topo, es, sem.i1, CNT, col(T.land1, 8 + N - u))
+                        for u, es in zip(direct, (off[0:2], off[2:4], off[4:8]))], local_sem=sem.lo)
+    iota("rc", T.rc[:, 0:32], [[0, 2], [1, 16]], 0)
+    iota("rc", T.rc[:, 32:64], [[0, 4], [B, 8]], B)
+    iota("rc", T.rc[:, 64:96], [[-16, 4], [0, 8]], 0)
+    iota("si", T.si[:, :], [[5, 2], [4, 8]], 4 * (s + 2) + 1, True)
+    iota("jd", T.jd[:, :], [[64, 3], [0, 2], [1, 16]], 0)
+    iota("d0i", T.d0i[:, :], [[B, 8], [1, 16]], B)
 
-    def to_plane(info, land, isem):
-        tr = []
-        for i, u in enumerate(direct):
-            b, c = 2 * ords.index(u), 8 + 2 * (slot_of(u) - 1)
-            tr.append(xfer(core, at(T, topo, s, u), topo, off[2 * i:2 * i + 2], isem, info[:, b:b + 2], land[:, c:c + 2]))
-        g.remote_dma_fused(tr, local_sem=sem.lo)
+    S("cu", "ta", "z0")
+    take("ga", T.ga[:, :], T.ta[:, 0:80].indirect(T.cu[:, 0:10]))
+    lin("zt", T.zt[:, 0:256], T.one[:, :], 0.0)
+    lin("zt", T.zt[:, 256:512], T.one[:, :], 0.0)
+    S("cnt")
+    take("z2", col(T.sc, 0), CNT)
+    V("cu", "tb")
+    cp("gb", T.gb[:, :], T.tb[:, 0:80].indirect(T.cu[:, 0:10]))
+    V("rb")
+    turn("kb", T.kb[:, :], T.rb[:, :])
+    V("ga")
+    scan("ca", T.ca[:, :], T.ga[:, :], T.one[:, 0:160], 0.0, A.add, A.mult)
+    V("gb")
+    scan("cb", T.cb[:, :], T.gb[:, :], T.one[:, 0:160], 0.0, A.add, A.mult)
+    V("ca", "thr")
+    ts("ua", T.ua[:, :], T.ca[:, :], col(T.ca, 159), LIM, A.subtract, A.is_gt)
+    V("cb")
+    ts("ub", T.ub[:, :], T.cb[:, :], col(T.cb, 159), float(-MOVE), A.subtract, A.is_gt)
+    V("ua")
+    tt("xa", T.xa[:, :], T.ua[:, :], T.ga[:, :], A.mult)
+    V("ub")
+    tt("xb", T.xb[:, :], T.ub[:, :], T.gb[:, :], A.mult)
+    ts("tq", T.tq[:, :], T.ident[:, 0:160:16], SH, None, A.add)
+    V("xa", "xb")
+    tt("cum", T.xs[:, :], T.xa[:, :], T.xb[:, :], A.add)
+    scan("cum", T.cum[:, :], T.xa[:, :], T.xb[:, :], BASE)
+    V("kb")
+    cp("cl", T.cl[:, 0:8:2], T.kb[:, 0:128:32])
+    V("cum")
+    tt("mm", T.mm[:, :], T.xs[:, :], T.cum[:, :], A.mult)
+    V("cnt")
+    turn("own", T.own[:, :], T.cnt[:, 128:160])
+    V("mm")
+    turn("mt", T.mt[:, :], T.mm[:, :])
+    fill("rl", T.rl[:, 2:4], N - late - 1)
+    V("mt", "kp")
+    scan("sgc", T.sg[:, 80:160], T.kp[:, 0:80], T.mt[:, 1:160:2], 0.0, A.mult, A.add)
+    scan("sgf", T.sg[:, 0:80], T.kp[:, 0:80], T.mt[:, 0:160:2], 0.0, A.mult, A.add)
+    V("sgc", "tq")
+    tt("sgx", T.sg[:, 87:160:8], T.sg[:, 87:160:8], T.tq[:, :], A.max)
+    fill("rl", T.rl[:, 4:6], N - late)
+    V("sgx", "sgf", "cl")
+    cp("so", T.so[:, :], T.sg[:, 0:160].indirect(T.cl[:, 0:1]))
+    V("rc")
+    turn("kc", T.kc[:, :], T.rc[:, :])
+    R16, BK, Q16 = [col(T.kc, 32 * i) for i in range(3)]
+    S("so")
+    take("key", T.key[:, :], T.ident[:, 0:256].indirect(T.so[:, 8:16]))
+    V("so", "z1")
+    cp("win", T.win[:, 16:272].indirect(T.so[:, 0:8]), T.ident[:, 0:128])
+    V("key")
+    cp("win2", T.win2[:, 16:272].indirect(T.so[:, 0:8]), T.key[:, :])
+    V("win")
+    turn("wt1", T.wt1[:, 0:288], T.win[:, 0:288])
+    turn("wt1", T.wt1[:, 288:544], T.win[:, 16:272])
+    V("win2", "z4")
+    turn("wt2", T.wt2[:, 128:288], T.win2[:, 128:288])
+    turn("wt2", T.wt2[:, 416:544], T.win2[:, 144:272])
+    V("wt1")
+    for t in range(3):
+        cp("offp", T.offp[:, t:48:3], T.wt1[:, 0:544].indirect(T.cl[:, 2 * t + 2:2 * t + 3]))
+    V("wt2")
+    cp("kq", T.kq[:, :], T.wt2[:, 0:544].indirect(T.cl[:, 2:3]))
+    V("x")
+    done(vec.quantize_mx(T.xq[:, :], T.xz[:, :], T.xt[:, :]), "xq")
 
-    g.wait_ge(sem.v, m1)
-    g.remote_dma_fused([xfer(core, to[j], topo, grp[j], sem.i1, T.info1[:, 2 + 2 * j:4 + 2 * j], T.hand1[:, :])
-                        for j in range(4)], local_sem=sem.lo)
-    to_plane(T.info1, T.land1, sem.i1)
-    I(T.x16[:, :], [[0, 24], [1, 16]], 0)
-    px = pn[0]
-    I(T.k32[:, :], [[0, 10], [1, 32]], 0)
-    I(T.val0[:, :], [[32, 4], [1, 16]], 0)
-    I(T.jw0[:, :], [[16, 10]], 0)
-    p2 = pn[0]
-    I(T.jd[:, :], [[16, 10], [0, 2], [1, 16]], 0)
-    p3 = pn[0]
+    S("kc", "own", "d0i")
+    shift("jm1", T.jm[:, :], T.ident[:, 0:160:16], 1.0, R16)
+    lin("r15", fc(8), R16, 1.0, -15.0)
+    S("jm1")
+    lin("p2", T.fc[:, 0:2], T.jm[:, 0:2], -1.0, -1.0)
+    lin("p2", T.fc[:, 2:4], T.jm[:, 0:2], -1.0 / 64)
+    lin("jw", T.jw[:, :], T.jm[:, :], -1.0, Z - B - 16)
+    lin("d0", T.d0[:, 0:128], T.d0i[:, :], -SC, Z * SC)
+    S("p2", "jw")
+    shift("in1", T.fc[:, 4:6], T.fc[:, 0:2], 1.0, col(T.own, 4 * gl))
+    lin("jm", col(T.jm, 9), col(T.one, 0), 999.0)
 
-    ISS, ISF, ISN = fc(4), fc(5), fc(6)
-    vec.wait_ge(sem.p, p1)
-    cp(T.bo[:, 8:16], T.bo[:, 0:8])
-    ts(T.kk[:, 0:1], T.pi[:, :], 7, None, A.bitwise_and)
-    ts(T.kk[:, 1:2], T.pi[:, :], 3, 3, A.logical_shift_right, A.bitwise_and)
-    ts(T.kk[:, 2:3], T.pi[:, :], 31, None, A.bitwise_and)
-    ts(T.kk[:, 3:4], T.pi[:, :], 15, None, A.bitwise_and)
-    ts(T.kk[:, 4:5], T.pi[:, :], 4, 1, A.logical_shift_right, A.bitwise_and)
-    ts(T.r1[:, :], T.r1i[:, :], 7, None, A.bitwise_and)
-    ts(T.r2[:, :], T.r2i[:, :], 7, None, A.bitwise_and)
-    vec.wait_ge(sem.le, 128)
-    ts(T.cm[:, :], T.c1b[:, :], 8, None, A.mult)
-    fence()
-    cp(T.bo[:, 16:32], T.bo[:, 0:16])
-    cp(T.kf[:, 0:5], T.kk[:, 0:5])
-    tt(T.cs[:, :], T.cm[:, :], T.c2b[:, :], A.add)
-    fence()
-    V(vec.transpose(T.bt[:, :], T.bo[:, :]))
-    ts(ISS, TY, 1.0, None, A.is_equal)
-    ts(ISF, TY, 0.0, None, A.is_equal)
-    ts(ISN, TY, 2.0, None, A.is_equal)
-    ts(T.tb[:, :], T.r1[:, :], 2.0, None, A.is_equal)
-    fence()
-    ts(fc(7), UO, -1.0, 1.0, A.mult, A.add)
-    ts(T.te[:, :], T.r1[:, :], UO, None, A.is_equal)
-    ts(T.eq2[:, :], T.r2[:, :], UO, None, A.is_equal)
-    ts(fc(9), ISS, -1.0, 1.0, A.mult, A.add)
-    fence()
-    ts(fc(8), fc(7), ISS, UO, A.mult, A.add)
-    cp(T.cu[:, :], T.cs[:, :])
-    ts(T.eqb[:, :], T.eq2[:, :], ISS, None, A.mult)
-    ts(T.eqa[:, :], T.eq2[:, :], fc(9), None, A.max)
-    fence()
-    ts(T.ta[:, :], T.r1[:, :], fc(8), None, A.is_equal)
-    tt(T.tib[:, :], T.tb[:, :], T.eqb[:, :], A.mult)
-    fence()
-    tt(T.tia[:, :], T.ta[:, :], T.eqa[:, :], A.mult)
-    m2 = fence()
-
-    act.wait_ge(sem.p, px)
-    S(act.activation(T.win[:, :], T.x16[:, :], Copy, scale=0.0))
-    S(act.activation(T.vv[:, :], T.x16[:, 0:32], Copy, scale=0.0))
-    act.wait_ge(sem.v, m2)
-    for out, tab in ((T.ga, T.ta), (T.gb, T.tb), (T.gia, T.tia), (T.gib, T.tib), (T.ge, T.te)):
-        S(act.activation(out[:, :], tab[:, 0:64].indirect(T.cu[:, 0:8]), Copy))
-    a1 = an[0]
-    act.dma_start(T.wt[:, :], T.w[:, :]).then_inc(sem.lw, 16)
-
-    fill(T.zt[:, 0:128], 0.0)
-    fill(T.land1[:, 0:8], 0.0)
-    tt(fc(10), ISS, ISF, A.subtract)
-    ts(fc(11), TY, -64.0, 174.0, A.mult, A.add)
-    ts(fc(12), KAP8, 48.0, -1.0, A.mult, A.add)
-    ts(fc(13), UO, -1.0, 8.0, A.mult, A.add)
-    ts(fc(14), UO, 0.0, -8.0, A.is_equal, A.mult)
-    ts(fc(15), HALF, 16.0, None, A.mult)
-    fence()
-    ts(T.land1[:, 0:1], ISS, 225.0, 30.0, A.mult, A.add)
-    fill(T.land1[:, 1:2], 255.0)
-    tt(fc(16), fc(13), fc(14), A.add)
-    fence()
-    ts(fc(17), TY, 8.0, fc(16), A.mult, A.add)
-    ts(fc(18), fc(16), -8.0, ISN, A.add, A.mult)
-    ts(fc(19), ISN, -8.0, 1.0, A.mult, A.add)
-    fence()
-    ts(fc(20), fc(18), 16.0, None, A.add)
-    tt(fc(21), fc(17), fc(19), A.add)
-    vec.wait_ge(sem.a, a1)
-    scan(T.ca[:, :], T.ga[:, :], T.zt[:, 0:128], 0.0, A.add)
-    scan(T.cb[:, :], T.gb[:, :], T.zt[:, 0:128], 0.0, A.add)
-    V(vec.tensor_reduce(fc(22), T.ge[:, :], X, A.add))
-    fence()
-    ts(T.ya1[:, :], T.ca[:, :], fc(10), fc(11), A.mult, A.add)
-    ts(T.yb1[:, :], T.cb[:, :], 110.0, None, A.add)
-    ts(fc(23), fc(22), ISS, fc(12), A.mult, A.add)
-    fence()
-    tt(T.ya[:, :], T.ya1[:, :], T.gia[:, :], A.mult)
-    tt(T.yb[:, :], T.yb1[:, :], T.gib[:, :], A.mult)
-    BASE = fc(23)
-    ts(fc(33), BASE, -1.0, None, A.mult)
-    vec.wait_ge(sem.p, p2)
-    ts(T.c2c[:, 0:32], T.ic[:, :], fc(17), None, A.is_gt)
-    ts(T.cda[:, :], T.ic[:, :], fc(20), None, A.is_equal)
-    ts(T.cdb[:, :], T.ic[:, :], fc(21), None, A.is_equal)
-    ts(T.kp[:, 0:128], T.k32[:, 0:128], 1.0, None, A.min)
-    ts(T.kr[:, :], T.x16[:, :], R16, 256.0, A.is_gt, A.mult)
-    ts(T.sc0[:, :], T.x16[:, 0:16], R16, 1.0 / 256.0, A.is_gt, A.mult)
-    ts(T.sc1[:, :], T.x16[:, 0:16], R16, None, A.is_equal)
-    ts(T.val[:, :], T.val0[:, :], fc(15), None, A.add)
-    fence()
-    tt(T.c2c[:, 32:64], T.cda[:, :], T.cdb[:, :], A.subtract)
-    scan(T.scl[:, :], T.sc0[:, :], T.sc1[:, :], 0.0, A.mult)
-    vec.wait_ge(sem.lx, 16)
-    V(vec.quantize_mx(T.xq[:, 0:128], T.xz[:, 0:128], T.xt[:, :]))
-    fence()
-
-    n1 = n2 = 0
-    for u in range(1, N):
-        here = u in order(T, topo, (s - u) % N)[1]
-        n1 += 2 if here else 8
-        n2 += 2 if here else 4
-    vec.wait_ge(sem.i1, n1)
-    V(vec.tensor_reduce(fc(24), T.land1[:, 0:22:2], X, A.add))
-    V(vec.tensor_reduce(fc(25), T.land1[:, 1:22:2], X, A.add))
-    fence()
-    ts(T.xa[:, :], T.ya[:, :], fc(24), None, A.is_ge)
-    ts(T.xb[:, :], T.yb[:, :], fc(25), None, A.is_ge)
-    fence()
-    scan(T.cum[:, :], T.xa[:, :], T.xb[:, :], BASE, A.add)
-    tt(T.xs[:, :], T.xa[:, :], T.xb[:, :], A.add)
-    mc = fence()
-    act.wait_ge(sem.v, mc)
-    S(act.activation(fc(26), T.cum[:, 127:128], Ident, bias=fc(33)))
-    act.wait_ge(sem.a, an[0])
-    S(act.activation(T.e2[:, :], T.c2c[:, :], Copy, scale=fc(26)))
-    tt(T.mm[:, :], T.xs[:, :], T.cum[:, :], A.mult)
-    fence()
-    V(vec.transpose(T.mt[:, :], T.mm[:, :]))
-    fence()
-    scan(T.ss[:, :], T.kp[:, 0:128], T.mt[:, :], 0.0, A.mult)
-    vec.wait_ge(sem.a, an[0])
-    V(vec.transpose(T.e2t[:, :], T.e2[:, :]))
-    fence()
-    cp(T.so[:, :], T.ss[:, 15:128:32])
-    tt(T.info2[:, 0:16:2], T.e2t[:, 0:8], T.e2t[:, 8:16], A.add)
-    tt(T.e2s[:, :], T.e2t[:, 32:40], T.e2t[:, 40:48], A.add)
-    m3 = fence()
-    vec.tensor_tensor(T.info2[:, 1:16:2], T.e2s[:, :], T.e2t[:, 48:56], A.add).then_inc(sem.n2, 1)
-    cp(T.win[:, 0:384].indirect(T.so[:, 0:4]), T.val[:, :])
-    fence()
-    scan(T.rr[:, :], T.kr[:, :], T.win[:, :], 0.0, A.mult)
-    fence()
-    ts(T.vv[:, 0:16:2], T.rr[:, 15:384:48], T.scl[:, 15:16], None, A.mult)
-    ts(T.vv[:, 1:16:2], T.rr[:, 31:384:48], T.scl[:, 15:16], None, A.mult)
-    fence()
-    V(vec.transpose(T.vt[:, :], T.vv[:, :]))
-    fence()
-    tt(T.v2[:, 0:16], T.vt[:, 0:16], T.vt[:, 16:32], A.add)
-    tt(T.v2[:, 16:32], T.vt[:, 0:16], T.vt[:, 16:32], A.add)
-    fence()
-    V(vec.transpose(T.vb[:, :], T.v2[:, :]))
-    fence()
-    cp(T.offp[:, :], T.vb[:, 0:16])
-    m4 = fence()
-
-    xc = lambda a, b: T.xq[:, 0:128].bitcast(dt.uint32).indirect(T.offp[:, a:b])
+    xc = lambda a, b: T.xq[:, 0:128].bitcast(U32).indirect(T.offp[:, a:b])
     xz = lambda a, b: T.xz[:, 0:128].indirect(T.offp[:, a:b])
-    vec.tensor_copy(T.oq[:, 32:160].bitcast(dt.uint32), xc(2, 10)).then_inc(sem.pc1, 1)
-    vec.tensor_copy(T.oq[:, 160:256].bitcast(dt.uint32), xc(10, 16)).then_inc(sem.pc2, 1)
-    cp(T.lq[:, 0:32].bitcast(dt.uint32), xc(0, 2))
-    act.wait_ge(sem.v, m4)
-    act.activation(T.oz[:, 32:160], xz(2, 10), Copy).then_inc(sem.pa1, 1)
-    act.activation(T.oz[:, 160:256], xz(10, 16), Copy).then_inc(sem.pa2, 1)
-    S(act.activation(T.lz[:, 0:32], xz(0, 2), Copy))
+    picks = (("o0", T.oq, T.oz, 0, 0, 9), ("o1", T.oq, T.oz, 144, 12, 21), ("p", T.pq, T.pz, 0, 10, 12),
+             ("p", T.pq, T.pz, 32, 8, 10), ("l", T.lq, T.lz, B - 16, 20, 24))
+    V("offp", "xq")
+    S("offp", "xq")
+    for nm, q, z, c, a, b in picks:
+        if nm != "l":
+            cp(nm + "q", q[:, c:c + 16 * (b - a)].bitcast(U32), xc(a, b))
+        take(nm + "z", z[:, c:c + 16 * (b - a)], xz(a, b))
 
-    g.wait_ge(sem.v, m3)
-    g.wait_ge(sem.n2, 1)
-    g.remote_dma_fused([xfer(core, rc[h], topo, half[h], sem.i2, T.info2[:, 2 + 4 * h:6 + 4 * h], T.hand2[:, :])
+    G("kq")
+    g.remote_dma_fused([xfer(core, rel[2 + h], topo, quarter[2 + h], sem.i2, T.kq[:, 4 * h:4 * h + 3], T.hand2[:, 0:3])
                         for h in range(2)], local_sem=sem.lo)
-    to_plane(T.info2, T.land2, sem.i2)
-    g.wait_ge(sem.pc1, 1)
-    g.remote_dma_fused([xfer(core, rc[h], topo, (off, on)[h], sem.tc, T.oq[:, 32 + 64 * h:96 + 64 * h].bitcast(dt.uint8),
-                             T.rq[:, :].bitcast(dt.uint8)) for h in range(2)], local_sem=sem.lo)
-    g.wait_ge(sem.pa1, 1)
-    g.remote_dma_fused([xfer(core, rs[h], topo, half[h], sem.ts, T.oz[:, 32 + 64 * h:96 + 64 * h],
-                             T.rz[:, :]) for h in range(2)], local_sem=sem.lo)
-    g.wait_ge(sem.pc2, 1)
-    tr = []
-    for i, u in enumerate(direct):
-        b, c = W * ords.index(u), W * slot_of(u)
-        x, y = SPLIT_C[i]
-        tr.append(xfer(core, at(T, topo, s, u), topo, off[x:y], sem.tc, T.oq[:, b:b + W].bitcast(dt.uint8),
-                       T.lq[:, c:c + W].bitcast(dt.uint8)))
-    g.remote_dma_fused(tr, local_sem=sem.lo)
-    g.wait_ge(sem.pa2, 1)
-    tr = []
-    for i, u in enumerate(direct):
-        b, c = W * ords.index(u), W * slot_of(u)
-        x, y = SPLIT_S[i]
-        tr.append(xfer(core, at(T, topo, s, u), topo, off[x:y], sem.ts, T.oz[:, b:b + W], T.lz[:, c:c + W]))
-    g.remote_dma_fused(tr, local_sem=sem.lo)
-    g.wait_ge(sem.lo, 22 + 14 + 16 + 3 * 8)
+    g.remote_dma_fused([xfer(core, at(T, s, late), topo, off, sem.il, col(T.kq, late - 1), col(T.lk, N - late - 1))],
+                       local_sem=sem.lo)
+    for h in range(2):
+        G("o%dq" % h)
+        g.remote_dma_fused([xfer(core, rel[h], topo, off + on, sem.tc, T.oq[:, 144 * h:144 * h + 136].bitcast(dt.uint8),
+                                 T.rq[:, :].bitcast(dt.uint8))], local_sem=sem.lo)
+    G("o0z", "o1z")
+    g.remote_dma_fused([xfer(core, rel[2 + h], topo, (off, on)[h], sem.ts, T.oz[:, 144 * h:144 * h + 136], T.rz[:, :])
+                        for h in range(2)], local_sem=sem.lo)
 
-    fill(T.zt[:, 128:640], 0.0)
-    fill(T.land2[:, 0:8], 0.0)
-    ts(T.kp[:, 128:320], T.k32[:, 128:320], 1.0, None, A.min)
-    fence()
-    V(vec.quantize_mx(T.lq[:, LAND:LAND + ROOM], T.lz[:, LAND:LAND + ROOM], T.zt[:, :]))
-    vec.wait_ge(sem.n2, 1)
-    cp(T.land2[:, 0:2], T.info2[:, 0:2])
-    ts(fc(27), K32, 1.0, 32.0, A.is_ge, A.mult)
-    ts(fc(28), K32, 17.0, -32.0, A.is_ge, A.mult)
-    ts(fc(29), K32, 8.0, -256.0, A.is_equal, A.mult)
-    ts(T.jw[:, :], T.jw0[:, :], R16, None, A.add)
-    fence()
-    tt(fc(30), fc(27), fc(28), A.add)
-    fence()
-    tt(T.land2[:, 3:4], fc(30), fc(29), A.add)
-    vec.wait_ge(sem.lw, 16)
+    V("kq", "si", "kc", "in1")
+    cp("kl", T.kl[:, :], T.kq[:, late - 1:N:N - late])
+    tt("in2", T.fc[:, 6:8], T.fc[:, 4:6], T.fc[:, 2:4], A.min)
+    ts("rl", T.rl[:, 0:2], T.kc[:, 32:34], 1.0 / B, -1.0, A.mult, A.add)
+    ts("sj", T.sj[:, :], T.si[:, :], 31, None, A.bitwise_and)
+    V("w")
     for o in range(O):
-        V(vec.quantize_mx(T.wq[:, 128 * o:128 * o + 128], T.wz[:, 128 * o:128 * o + 128], T.wt[:, 512 * o:512 * o + 512]))
-    fence()
+        done(vec.quantize_mx(T.wq[:, 128 * o:128 * o + 128], T.wz[:, 128 * o:128 * o + 128], T.wt[:, 512 * o:512 * o + 512]), "wq")
+        if o == 0:
+            V("sj")
+            cp("sl", T.sl[:, :], T.sj[:, :])
 
-    vec.wait_ge(sem.p, p3)
-    vec.wait_ge(sem.i2, n2)
-    V(vec.tensor_reduce(fc(31), T.land2[:, 0:22:2], X, A.add))
-    V(vec.tensor_reduce(fc(32), T.land2[:, 1:22:2], X, A.add))
-    fence()
-    ts(T.st[:, :], T.jd[:, :], fc(31), fc(32), A.is_ge, A.mult)
-    fence()
-    V(vec.transpose(T.stt[:, :], T.st[:, :]))
-    fence()
-    scan(T.sw[:, :], T.kp[:, :], T.stt[:, :], 0.0, A.mult)
-    fence()
-    tt(T.wl[:, :], T.sw[:, 31:320:32], T.jw[:, :], A.add)
-    fence()
-    cp(T.offh[:, :], T.wl[:, :])
-    m5 = fence()
-
-    nt = 0
+    n1 = 0
     for u in range(1, N):
-        d = order(T, topo, (s - u) % N)[1]
-        nt += SPLIT_C[d.index(u)][1] - SPLIT_C[d.index(u)][0] if u in d else 4
-    act.wait_ge(sem.v, m5)
-    act.wait_ge(sem.a, an[0])
-    act.wait_ge(sem.ts, nt)
-    S(act.activation(T.hz[:, 0:160], T.lz[:, 0:416].indirect(T.offh[:, 0:10]), Copy))
-    a2 = an[0]
-    vec.wait_ge(sem.tc, nt)
-    cp(T.hq[:, 0:160].bitcast(dt.uint32), T.lq[:, 0:416].bitcast(dt.uint32).indirect(T.offh[:, 0:10]))
-    m6 = vn[0]
-    ten.wait_ge(sem.v, m6)
-    ten.wait_ge(sem.a, a2)
+        d = roads(T, topo, (s - u) % N)[1]
+        n1 += (2, 2, 4)[d.index(u)] if u in d else 8
+    V("z2")
+    vec.wait_ge(sem.i1, n1)
+    scan("sc", T.sc[:, 1:40], T.land1[:, 9:48], T.one[:, 0:39], CNT, A.add, A.mult)
+    V("sc")
+    turn("tot", T.tot[:, :], T.sc[:, 8:40])
+    S("sc", "rl")
+    take("rep", T.rep[:, :], T.sc[:, 0:16].indirect(T.rl[:, 0:6]))
+    tA = lambda k, a, b: T.thr[:, 32:96].indirect(k[:, a:b])
+    tB = lambda k, a, b: T.thr[:, 0:64].indirect(k[:, a:b])
+    V("tot", "thr", "kl")
+    ts("f0", T.fa[:, 0:32], tA(T.kl, 0, 2), col(T.tot, 4 * g1 + 1), None, A.is_le)
+    ts("f0", T.fb[:, 0:32], tB(T.kl, 0, 2), col(T.tot, 4 * g2 + 2), None, A.is_le)
+    S("tot", "sl")
+    take("sa", T.sa[:, :], T.tot[:, 0:32].indirect(T.sl[:, 0:7]))
+    take("sb", T.sb[:, :], T.tot[:, 0:32].indirect(T.sl[:, 8:15]))
+    V("r15")
+    ts("z", T.zi[:, 0:1], col(T.tot, 4 * s), float(CAP), fc(8), A.min, A.subtract)
+    V("f0")
+    for c in range(2):
+        scan("vl", T.vl[:, 16 * c:16 * c + 16], T.fa[:, 0:16], T.fb[:, 0:16], fc(4 + c))
+    V("rep")
+    turn("rpt", T.rpt[:, :], T.rep[:, :])
+    V("vl", "in2", "dl")
+    for c in range(2):
+        scan("wl", T.wl[:, 16 * c:16 * c + 16], T.dl[:, :], T.vl[:, 16 * c:16 * c + 16], fc(6 + c), A.max, A.min)
+    V("z")
+    ts("zz", T.zi[:, 1:2], T.zi[:, 0:1], 15, None, A.bitwise_and)
+    V("wl")
+    ts("offl", T.offl[:, :], T.wl[:, 15:32:16], -64.0, 63.0, A.mult, A.min)
+    ts("zz", T.zi[:, 2:3], T.zi[:, 0:1], 4, None, A.logical_shift_right)
+    V("offl", "pq")
+    cp("o2q", T.o2q[:, :].bitcast(U32), T.pq[:, 0:64].bitcast(U32).indirect(T.offl[:, 0:2]))
+    c = B * (N - late + 1) + 16
+    S("rpt")
+    PK = col(T.rpt, 4 * s)
+    shift("pd", fc(9), PK, -1.0, BK)
+    shift("pd", fc(10), PK, 1.0, Q16)
+    S("offl", "pz")
+    take("o2z", T.o2z[:, :], T.pz[:, 0:64].indirect(T.offl[:, 0:2]))
+    lin("nl", fc(11), col(T.rpt, 32 + 4 * s), SC, (Z - c + 1) * SC)
+    G("o2q")
+    g.remote_dma_fused([xfer(core, at(T, s, late), topo, off, sem.tc, T.o2q[:, 0:BOTH].bitcast(dt.uint8),
+                             T.lq[:, c:c + BOTH].bitcast(dt.uint8))], local_sem=sem.lo)
+    G("o2z")
+    g.remote_dma_fused([xfer(core, at(T, s, late), topo, off, sem.ts, T.o2z[:, 0:BOTH], T.lz[:, c:c + BOTH])], local_sem=sem.lo)
+    g.wait_ge(sem.lo, 24 + 16 + 32 + 16 + 16)
+
+    V("zz")
+    ts("zf", T.fc[:, 12:14], T.zi[:, 1:3], 0.5, None, A.add)
+    V("pd", "jd")
+    ts("st", T.st[:, :], T.jd[:, :], fc(10), fc(9), A.is_ge, A.mult)
+    vec.wait_ge(sem.il, 8)
+    cp("km", col(T.km, 0), col(T.lk, N - late - 1))
+    S("nl", "zf")
+    shift("nl2", fc(14), col(T.rpt, 64 + 4 * s), -SC, fc(11))
+    shift("ini", T.fc[:, 15:18], T.ident[:, 16:49:16], -1.0, fc(12))
+    shift("zm1", T.fc[:, 21:24], T.ident[:, 0:3], 1.0, fc(13))
+    S("zm1")
+    lin("zm", T.fc[:, 18:21], T.fc[:, 21:24], 1.0, -0.5)
+    V("st", "jm")
+    turn("stt", T.stt[:, :], T.st[:, :])
+    ts("msk", T.msk[:, :], T.jm[:, :], col(T.tot, 4 * s), SC, A.is_lt, A.mult)
+    V("stt")
+    scan("sw", T.sw[:, :], T.kp[:, :], T.stt[:, :], 0.0, A.mult, A.max)
+    V("km")
+    sl = (s + N - late) % N
+    ts("xl", T.xal[:, :], tA(T.km, 0, 1), col(T.tot, 4 * ((sl + 1) % N) + 1), -SC, A.is_le, A.mult)
+    ts("xl", T.xbl[:, :], tB(T.km, 0, 1), col(T.tot, 4 * ((sl + 2) % N) + 2), -SC, A.is_le, A.mult)
+    V("sw", "jw")
+    tt("ga0", T.ga0[:, :], T.jw[:, :], T.sw[:, 7:80:8], A.subtract)
+    V("xl", "nl2", "d0")
+    k = 16 * (N - late)
+    scan("d0l", T.d0[:, k:k + 16], T.xal[:, :], T.xbl[:, :], fc(14))
+    V("ga0", "msk", "z3")
+    tt("mf", T.mm4[:, 3:80:8], T.ga0[:, :], T.msk[:, :], A.mult)
+
+    vec.wait_ge(sem.i2, 32)
+    V("sa")
+    tt("f1", T.fa[:, 32:144], tA(T.lk, 0, 7), T.sa[:, :], A.is_le)
+    V("sb")
+    tt("f1", T.fb[:, 32:144], tB(T.lk, 0, 7), T.sb[:, :], A.is_le)
+    nm, q, z, c, a, b = picks[4]
+    cp("lq", q[:, c:c + 16 * (b - a)].bitcast(U32), xc(a, b))
+    V("f1", "ini")
+    for m in range(3):
+        scan("w1%d" % m, T.w1[:, 130 * m:130 * m + 129], T.fa[:, 16:145], T.fb[:, 16:145], fc(15 + m))
+    V("d0l")
+    for m in range(3):
+        V("w1%d" % m)
+        scan("wv%d" % m, T.wv[:, 130 * m:130 * m + 129], T.d0[:, 0:129], T.w1[:, 130 * m:130 * m + 129], -1.0, A.max, A.min)
+    V("zm")
+    for m in range(3):
+        V("wv%d" % m)
+        ts("mf", T.mm4[:, m:80:8], T.ident[:, 0:10], fc(18 + m), col(T.wv, 130 * m + 128), A.is_equal, A.mult)
+    V("mf")
+    scan("ms", T.ms[:, :], T.kp[:, 0:80], T.mm4[:, :], 0.0, A.mult, A.add)
+    V("zt")
+    done(vec.quantize_mx(T.lq[:, Z:Z + 128], T.lz[:, Z:Z + 128], T.zt[:, :]), "zq")
+    V("ms")
+    ts("offh", T.offh[:, :], T.ms[:, 7:80:8], -1024.0, float(Z), A.mult, A.add)
+
+    S("offh", "lz", "zq")
+    act.wait_ge(sem.ts, 40)
+    take("hz", T.hz[:, :], T.lz[:, 0:Z + 32].indirect(T.offh[:, 0:10]))
+    V("offh", "lq", "zq")
+    vec.wait_ge(sem.tc, 40)
+    cp("hq", T.hq[:, :].bitcast(U32), T.lq[:, 0:Z + 32].bitcast(U32).indirect(T.offh[:, 0:10]))
+    need(QT, "wq", "hq", "hz")
     for o in range(O):
-        ten.matmul_mx(T.ps[:, 512 * o:512 * o + ROOM], T.wq[:, 128 * o:128 * o + 128], T.wz[:, 128 * o:128 * o + 128],
-                      T.hq[:, 0:ROOM], T.hz[:, 0:ROOM], True, True).then_inc(sem["t%d" % o], 1)
+        done(ten.matmul_mx(T.ps[:, 512 * o:512 * o + ROOM], T.wq[:, 128 * o:128 * o + 128], T.wz[:, 128 * o:128 * o + 128],
+                           T.hq[:, 0:ROOM], T.hz[:, 0:ROOM], True, True), "t%d" % o)
     for o in range(O):
         y, p = T.ys[:, ROOM * o:ROOM * o + ROOM], T.ps[:, 512 * o:512 * o + ROOM]
         if o % 2 == 0:
-            vec.wait_ge(sem["t%d" % o], 1)
-            vec.tensor_copy(y, p).then_inc(sem["y%d" % o], 1)
+            V("t%d" % o)
+            cp("y%d" % o, y, p)
         else:
-            act.wait_ge(sem["t%d" % o], 1)
-            act.activation(y, p, Copy).then_inc(sem["y%d" % o], 1)
-    for q, o, e in ((g.sync, 0, 1), (act, 1, 4)):
-        for k in range(o, e):
-            q.wait_ge(sem["y%d" % k], 1)
-        q.dma_start(T.y[:, ROOM * o:ROOM * e], T.ys[:, ROOM * o:ROOM * e]).then_inc(sem.ly, 16)
-    act.wait_ge(sem.ly, 32)
+            S("t%d" % o)
+            take("y%d" % o, y, p)
+    for q, o, e in ((QS, 0, 1), (QA, 1, 4)):
+        need(q, *["y%d" % i for i in range(o, e)])
+        done(q[1].dma_start(T.y[:, ROOM * o:ROOM * e], T.ys[:, ROOM * o:ROOM * e]), "out", 16)
+    S("out")

@@ -6,29 +6,29 @@ N = 8
 CAP, ROOM, O = 144, 160, 4
 PAIR, MOVE, BOTH = 24, 8, 30
 B = 48
-Z = B * (N + 1)
+Z = B * (N + 1) + 8
 NOKEY = 24.0
 SC = 1.0 / 1024
+WHOLE = 1.5 * 2 ** 23
 
 F4, B2, I4, U2, MX, U1 = "float32", "bfloat16", "int32", "uint16", "float8_e4m3fn_x4", "uint8"
 SIZES = {
-    I4: dict(c1b=8, c2b=8, cm=8, cs=10, yi=64, yr=64, si=16, sj=16, zi=4),
-    U2: dict(cu1=8, cu=16, sh=2, cl=8, so=16, offp=48, kq=16, kl=2, km=2, lk=8, hand2=4, sl=16, rl=6, offl=2, offh=10),
-    F4: dict(r0=32, k0=32, ra=192, ka=192, rb=128, kb=128, rc=96, kc=96, k16=16, yc=64, sg=160, tq=10, fc=32,
-             d0i=128, d0=130, dl=16, jw=10, jm=10, st=96, stt=96, sw=96, ga0=10, msk=10, mm4=80, ms=80, wv=390,
-             ys=640, xal=16, xbl=16, wl=32, rep=96, rpt=96),
-    B2: dict(one=256, ident=256, kp=96, tn=8, gn=160, cnt=160, own=32, ta=80, tb=80, ga=160, gb=160, ca=160, cb=160,
-             ua=160, ub=160, xa=160, xb=160, xs=160, cum=160, mm=160, mt=160, win=288, wt1=544, key=128, win2=288, wt2=544,
-             thr=96, hand1=2, land1=48, sc=40, tot=32, sa=112, sb=112, fa=146, fb=146, w1=390, vl=32, jd=96,
-             xt=512, wt=2048, zt=512),
-    MX: dict(xq=128, wq=512, oq=288, pq=64, o2q=32, rq=136, lq=560, hq=160),
-    U1: dict(xz=128, wz=512, oz=288, pz=64, o2z=32, rz=136, lz=560, hz=160),
+    I4: dict(c1b=8, c2b=8, cm=8, cs=10, yi=64, yr=80),
+    U2: dict(cu1=8, cu=16, sh=2, cl=8, so=16, offp=48, kq=16, kl=2, lk=8, hand2=4, sl=22, offl=2, offh=10),
+    F4: dict(r0=32, k0=32, yc=80, sg=160, fc=32, d0i=128, d0=130, dl=34, slf=22, jm=10, st=96, stt=96, sw=96, em=24,
+             mm4=80, ms=80, wv=390, ys=640, xal=32, xbl=32, wl=34, rep=96, rpt=96),
+    B2: dict(ra=160, ka=160, rb=224, kb=224, one=256, ident=256, kp=96, kr=96, tq=80, tn=8, gn=160, cnt=160, own=32,
+             ta=80, tb=80, ga=160, gb=160, ca=160, cb=160, ua=160, ub=160, xa=160, xb=160, xs=160, cum=160, mm=160, mt=160,
+             win=288, wt1=544, key=128, win2=288, wt2=544, thr=96, hand1=2, land1=48, sc=40, tot=32, sa=112, sb=112,
+             kb2=112, fa=146, fb=146, w1=390, vl=34, jd=96, xt=520, wt=2048),
+    MX: dict(xq=130, wq=512, oq=288, pq=64, o2q=32, rq=136, lq=448, hq=160),
+    U1: dict(xz=130, wz=512, oz=288, pz=64, o2z=32, rz=136, lz=448, hz=160),
 }
 SCRATCH = {"ps": ("psum", [128, 2048], F4)}
 for _d in SIZES:
     for _n in SIZES[_d]:
         SCRATCH[_n] = ("sbuf", [128, SIZES[_d][_n]], _d)
-SEMAPHORES = ["i1", "i2", "il", "tc", "ts", "lo"] + ["s%d" % _i for _i in range(144)]
+SEMAPHORES = ["i1", "i2", "tc", "ts", "lo"] + ["s%d" % _i for _i in range(140)]
 
 
 def bits(es):
@@ -95,7 +95,7 @@ def hand_on(g, core, T, topo):
             g.wait_ge(T.sem.tc, 16)
             two_calls(T.sem.tc, lambda i, u: [v.bitcast(dt.uint8) for v in block(T.rq, T.lq, i, u)])
         else:
-            g.wait_ge(T.sem.i2, 4)
+            g.wait_ge(T.sem.i2, 8)
             two_calls(T.sem.i2, lambda i, u: (T.hand2[:, i:i + 1], T.lk[:, N - u - 1:N - u]))
             g.wait_ge(T.sem.ts, 8)
             two_calls(T.sem.ts, lambda i, u: block(T.rz, T.lz, i, u))
@@ -108,8 +108,7 @@ def rank_program(g, core, T, topo):
     if s is None:
         hand_on(g, core, T, topo)
         return
-    A = AluOpType
-    Copy, Ident = ActivationFunctionType.Copy, ActivationFunctionType.Identity
+    A, F = AluOpType, ActivationFunctionType
     sem = T.sem
     vec, act, ten, syn = g.vector, g.scalar, g.tensor, g.sync
     cross, direct, late = roads(T, topo, s)
@@ -147,23 +146,29 @@ def rank_program(g, core, T, topo):
     def scan(step, out, a, b, ini, op0=A.add, op1=A.add):
         done(vec.tensor_tensor_scan(out, a, b, ini, op0, op1), step)
 
+    def mask(step, out, rising, flags):
+        scan(step, out, rising, flags, 0.0, A.max, A.mult)
+
     def turn(step, out, a):
         done(vec.transpose(out, a), step)
 
     def lin(step, out, a, scale=1.0, bias=0.0):
-        done(act.activation(out, a, Copy, bias=float(bias), scale=float(scale)), step)
+        done(act.activation(out, a, F.Copy, bias=float(bias), scale=float(scale)), step)
 
-    def shift(step, out, a, scale, bias):
-        done(act.activation(out, a, Ident, bias=bias, scale=float(scale)), step)
+    def shift(step, out, a, scale, bias, f=F.Identity):
+        done(act.activation(out, a, f, bias=bias, scale=float(scale)), step)
 
     def take(step, out, a):
-        done(act.activation(out, a, Copy), step)
+        done(act.activation(out, a, F.Copy), step)
 
     def iota(step, out, pattern, base, whole=False):
         if whole:
             done(g.iota(out, pattern, base, 0), step)
         else:
             done(g.iota(out, pattern, base, 0, allow_small_or_imprecise_dtypes=True), step)
+
+    def quant_w(o):
+        done(vec.quantize_mx(T.wq[:, 128 * o:128 * o + 128], T.wz[:, 128 * o:128 * o + 128], T.wt[:, 512 * o:512 * o + 512]), "wq")
 
     V = lambda *n: need(QV, *n)
     S = lambda *n: need(QA, *n)
@@ -175,13 +180,13 @@ def rank_program(g, core, T, topo):
     for big, src, nm in ((T.c1b, T.c1, "c1"), (T.c2b, T.c2, "c2")):
         for q in range(8):
             done((syn if q % 2 else act).dma_start(big[16 * q:16 * q + 16, :], src[:, :]), nm, 16)
-    done(syn.dma_start(T.xt[:, :], T.x[:, :]), "x", 16)
+    done(syn.dma_start(T.xt[:, 0:512], T.x[:, :]), "x", 16)
     done(syn.dma_start(T.wt[:, :], T.w[:, :]), "w", 16)
 
-    iota("r0", T.r0[:, :], [[1, 8], [0, 4]], 0)
-    iota("k16", T.k16[:, :], [[0, 2], [1, 8]], 0)
+    iota("k16", T.ra[:, 32:64], [[0, 2], [1, 8], [0, 2]], 0)
+    iota("ra", T.ra[:, 0:32], [[-1, 2], [1, 16]], 1)
     iota("yi", T.yi[:, :], [[32, 8], [1, 8]], 33 * (N - 1 - s), True)
-    iota("ra0", T.ra[:, 0:32], [[-1, 2], [1, 16]], 1)
+    iota("r0", T.r0[:, :], [[1, 8], [0, 4]], 0)
     iota("rb", T.rb[:, 0:16], [[0, 2], [16, 4], [24, 2]], 7)
     iota("rb", T.rb[:, 16:32], [[-80, 2], [16, 4], [-8, 2]], 95)
     iota("rb", T.rb[:, 32:48], [[0, 2], [32, 4], [-256, 2]], 432)
@@ -190,66 +195,52 @@ def rank_program(g, core, T, topo):
     iota("rb", T.rb[:, 96:128], [[256, 2], [0, 2], [32, 8]], 32)
 
     fill("one", T.one[:, :], 1.0)
-    fill("z0", T.gn[:, 128:160], 0.0)
-    fill("z0", T.cs[:, 0:10:9], 64)
-    fill("z0", T.ta[:, 64:80], 0.0)
-    fill("z0", T.tb[:, 64:80], 0.0)
-    V("one", "r0")
+    fill("ra", T.ra[:, 64:96:2], 1.0 / 32)
+    fill("ra", T.ra[:, 65:96:2], 1.0)
+    fill("ra", T.ra[:, 128:160:2], -999.0)
+    fill("ra", T.ra[:, 129:160:2], float(-MOVE))
+    fill("ra", T.ra[:, 97:128:16], float(127 + MOVE))
+    fill("ra", T.ra[:, 99:128:16], float(143 + MOVE))
+    V("k16", "one")
+    ts("ra", T.ra[:, 96:128:2], T.ra[:, 32:64:2], 32.0, -1.0, A.mult, A.add)
+    for h in range(2):
+        ts("ra", T.ra[:, 101 + 16 * h:112 + 16 * h:2], T.ra[:, 36:48:2], 16.0, 127.0, A.mult, A.add)
     scan("ident", T.ident[:, :], T.one[:, :], T.one[:, :], -1.0, A.add, A.mult)
+    fill("yr", T.yr[:, 64:80], 999)
+    V("ra")
+    turn("ka", T.ka[:, :], T.ra[:, :])
+    V("yi")
+    ts("yr", T.yr[:, 0:64], T.yi[:, :], 0xE7, None, A.bitwise_and)
+    SH, K, MUL, BASE, LIM = [col(T.ka, 32 * i) for i in range(5)]
+    V("r0")
     fill("r0x", T.r0[:, 4 * g1 + 1:4 * g1 + 3], 99.0)
     fill("r0x", col(T.r0, 4 * g2 + 2), 99.0)
-    fill("z1", T.win[:, :], 0.0)
+    V("ka", "yr")
+    ts("yc", T.yc[:, :], T.yr[:, :], MUL, WHOLE, A.mult, A.add)
     V("r0x")
     turn("k0", T.k0[:, :], T.r0[:, :])
-    fill("z1", T.win2[:, :], NOKEY)
-    fill("kp1", T.kp[:, :], 1.0)
-    V("k0", "ident", "yi", "kp1")
+    ts("sh", T.sh[:, 0:1], SH, 9.0, None, A.min)
+    fill("sh", T.cs[:, 0:10:9], 64)
+    V("yc")
+    ts("ta", T.ta[:, :], T.yc[:, :], -WHOLE, K, A.add, A.is_equal)
+    V("k0", "ident")
     ts("tn", T.tn[:, :], T.ident[:, 0:8], col(T.k0, 0), None, A.is_equal)
-    ts("yr", T.yr[:, :], T.yi[:, :], 0xE7, None, A.bitwise_and)
-    fill("kp", T.kp[:, 0:96:8], 0.0)
-
-    S("k16")
-    for b, (f, c) in enumerate((((32, 0), (1, 0)), ((32, 7), (1, 0)), ((0, 999), (1, 32)), ((32, -1), (16, 127)),
-                                ((0, -999), (0, -MOVE)))):
-        lin("ra", T.ra[:, 32 * b + 32:32 * b + 64:2], T.k16[:, :], *f)
-        lin("ra", T.ra[:, 32 * b + 33:32 * b + 64:2], T.k16[:, :], *c)
-    S("ra")
-    lin("rax", T.ra[:, 129:160:16], T.k16[:, 0:2], 0, 127 + MOVE)
-    lin("rax", T.ra[:, 131:160:16], T.k16[:, 0:2], 0, 143 + MOVE)
-    V("ra0", "rax")
-    turn("ka", T.ka[:, :], T.ra[:, :])
-    SH, LO, HI, TB, BASE = [col(T.ka, 32 * i) for i in range(5)]
-    LIM = col(T.fa, 145)
-    S("one", "ident")
-    lin("z4", T.wt2[:, 0:128], T.one[:, 0:128], 0.0)
-    lin("z4", T.wt2[:, 288:416], T.one[:, 0:128], 0.0)
-    lin("thr1", T.thr[:, :], T.one[:, 0:96], 255.0)
-    lin("z2", T.land1[:, 16:48], T.one[:, 0:32], 0.0)
-    lin("dl", T.dl[:, :], T.ident[:, 48:64], -1.0 / 64)
-    lin("z3", col(T.fa, 144), col(T.one, 0), 200.0)
-    lin("z3", col(T.fb, 144), col(T.one, 0), 0.0)
-    lin("z3", T.mm4[:, :], T.one[:, 0:80], 0.0)
-    lin("z3", col(T.d0, 128), col(T.one, 0), 0.0)
-    S("thr1", "ka")
-    lin("thr", T.thr[:, 32:32 + PAIR], T.ident[:, 0:PAIR], -1.0, CAP)
-    take("thr", LIM, col(T.ka, 160))
+    ts("tb", T.tb[:, :], T.yc[:, :], -WHOLE - 32, K, A.add, A.is_equal)
 
     V("c1")
     cp("cu1", T.cu1[:, :], T.c1b[:, :])
     ts("cm", T.cm[:, :], T.c1b[:, :], 8, None, A.mult)
-    V("cu1", "tn")
-    cp("gn", T.gn[:, 0:128], T.tn[:, 0:8].indirect(T.cu1[:, 0:8]))
-    V("ka", "yr")
-    ts("yc", T.yc[:, :], T.yr[:, :], LO, HI, A.max, A.min)
-    V("gn", "z0")
-    scan("cnt", T.cnt[:, :], T.gn[:, :], T.one[:, 0:160], 0.0, A.add, A.mult)
-    V("c2", "cm", "yc")
+    fill("gn", T.gn[:, 128:160], 0.0)
+    S("cu1", "tn")
+    take("gn", T.gn[:, 0:128], T.tn[:, 0:8].indirect(T.cu1[:, 0:8]))
+    V("c2", "cm")
     tt("cs", T.cs[:, 1:9], T.cm[:, :], T.c2b[:, :], A.add)
-    ts("sh", T.sh[:, 0:1], SH, 9.0, None, A.min)
-    tt("ta", T.ta[:, 0:64], T.yc[:, :], T.yr[:, :], A.is_equal)
+    fill("kp1", T.kp[:, :], 1.0)
+    fill("kp1", T.tq[:, :], 999.0)
     V("cs", "sh")
     cp("cu", T.cu[:, :], T.cs[:, 0:10].indirect(T.sh[:, 0:1]))
-    ts("tb", T.tb[:, 0:64], T.yr[:, :], TB, None, A.is_equal)
+    V("gn")
+    scan("cnt", T.cnt[:, :], T.gn[:, :], T.one[:, 0:160], 0.0, A.add, A.mult)
 
     off = topo.engines(core, at(T, s, late))
     on = [e for e in topo.engines(core, rel[0]) if e not in off]
@@ -259,214 +250,246 @@ def rank_program(g, core, T, topo):
     g.remote_dma_fused([xfer(core, rel[j], topo, quarter[j], sem.i1, CNT, T.hand1[:, 0:1]) for j in range(4)], local_sem=sem.lo)
     g.remote_dma_fused([xfer(core, at(T, s, u), topo, es, sem.i1, CNT, col(T.land1, 8 + N - u))
                         for u, es in zip(direct, (off[0:2], off[2:4], off[4:8]))], local_sem=sem.lo)
-    iota("rc", T.rc[:, 0:32], [[0, 2], [1, 16]], 0)
-    iota("rc", T.rc[:, 32:64], [[0, 4], [B, 8]], B)
-    iota("rc", T.rc[:, 64:96], [[-16, 4], [0, 8]], 0)
-    iota("si", T.si[:, :], [[5, 2], [4, 8]], 4 * (s + 2) + 1, True)
+    for v in (1, 2):
+        a = (s + 1 + v) % N
+        iota("slf", T.slf[:, 8 * v - 8:8 * v - a], [[4, N - a]], 4 * a + v)
+        if a:
+            iota("slf", T.slf[:, 8 * v - a:8 * v], [[4, a]], v)
     iota("jd", T.jd[:, :], [[64, 3], [0, 2], [1, 16]], 0)
     iota("d0i", T.d0i[:, :], [[B, 8], [1, 16]], B)
 
-    S("cu", "ta", "z0")
+    S("one", "ident", "ka")
+    lin("r15", fc(28), SH, -1.0, 127.0)
+    lin("z1", T.win[:, 0:256], T.one[:, :], 128.0)
+    S("cu", "ta")
     take("ga", T.ga[:, :], T.ta[:, 0:80].indirect(T.cu[:, 0:10]))
-    lin("zt", T.zt[:, 0:256], T.one[:, :], 0.0)
-    lin("zt", T.zt[:, 256:512], T.one[:, :], 0.0)
-    S("cnt")
-    take("z2", col(T.sc, 0), CNT)
+    S("kp1", "r15")
+    lin("kp", T.kp[:, 0:96:8], T.one[:, 0:12], 0.0)
+    shift("kp", T.tq[:, 0:80:8], T.ident[:, 0:160:16], -1.0, fc(28))
+    lin("z1", T.win[:, 256:288], T.one[:, 0:32], 128.0)
+    lin("z1", T.win2[:, 128:288], T.one[:, 0:160], NOKEY)
+    lin("z1", T.xt[:, 512:520], T.one[:, 0:8], 0.0)
+    lin("thr1", T.thr[:, :], T.one[:, 0:96], 255.0)
+    lin("thr1", T.kr[:, :], T.one[:, 0:96], 0.0)
+    for h in range(2):
+        lin("rc", T.rb[:, 128 + 16 * h:144 + 16 * h], T.ident[:, 0:16])
+        lin("thr1", T.rb[:, 160 + 16 * h:176 + 16 * h], T.ra[:, 32:64:2], B, B)
+    for q in range(4):
+        lin("rc", T.rb[:, 192 + 8 * q:200 + 8 * q], T.one[:, 0:8], -16 * q)
+    S("thr1")
+    lin("rc", T.rb[:, 167:192:8], T.one[:, 0:4], 2048.0)
+    lin("z4", T.wt2[:, 0:128], T.one[:, 0:128], 0.0)
+    lin("z4", T.wt2[:, 288:416], T.one[:, 0:128], 0.0)
     V("cu", "tb")
     cp("gb", T.gb[:, :], T.tb[:, 0:80].indirect(T.cu[:, 0:10]))
     V("rb")
-    turn("kb", T.kb[:, :], T.rb[:, :])
-    V("ga")
-    scan("ca", T.ca[:, :], T.ga[:, :], T.one[:, 0:160], 0.0, A.add, A.mult)
+    turn("kb", T.kb[:, 0:128], T.rb[:, 0:128])
+    V("cnt")
+    turn("own", T.own[:, :], T.cnt[:, 128:160])
     V("gb")
     scan("cb", T.cb[:, :], T.gb[:, :], T.one[:, 0:160], 0.0, A.add, A.mult)
-    V("ca", "thr")
-    ts("ua", T.ua[:, :], T.ca[:, :], col(T.ca, 159), LIM, A.subtract, A.is_gt)
+    V("ga")
+    scan("ca", T.ca[:, :], T.ga[:, :], T.one[:, 0:160], 0.0, A.add, A.mult)
+    V("kb")
+    cp("cl", T.cl[:, 0:8:2], T.kb[:, 0:97:32])
     V("cb")
     ts("ub", T.ub[:, :], T.cb[:, :], col(T.cb, 159), float(-MOVE), A.subtract, A.is_gt)
-    V("ua")
-    tt("xa", T.xa[:, :], T.ua[:, :], T.ga[:, :], A.mult)
+    V("ca")
+    ts("ua", T.ua[:, :], T.ca[:, :], col(T.ca, 159), LIM, A.subtract, A.is_gt)
     V("ub")
-    tt("xb", T.xb[:, :], T.ub[:, :], T.gb[:, :], A.mult)
-    ts("tq", T.tq[:, :], T.ident[:, 0:160:16], SH, None, A.add)
+    mask("xb", T.xb[:, :], T.ub[:, :], T.gb[:, :])
+    V("ua")
+    mask("xa", T.xa[:, :], T.ua[:, :], T.ga[:, :])
+    V("x", "z1")
+    done(vec.quantize_mx(T.xq[:, :], T.xz[:, :], T.xt[:, :]), "xq")
     V("xa", "xb")
     tt("cum", T.xs[:, :], T.xa[:, :], T.xb[:, :], A.add)
     scan("cum", T.cum[:, :], T.xa[:, :], T.xb[:, :], BASE)
-    V("kb")
-    cp("cl", T.cl[:, 0:8:2], T.kb[:, 0:128:32])
+    R16, BK, Q16 = [col(T.kb, 128 + 32 * i) for i in range(3)]
     V("cum")
-    tt("mm", T.mm[:, :], T.xs[:, :], T.cum[:, :], A.mult)
-    V("cnt")
-    turn("own", T.own[:, :], T.cnt[:, 128:160])
+    mask("mm", T.mm[:, :], T.cum[:, :], T.xs[:, :])
+    V("rc")
+    turn("own", T.kb[:, 128:224], T.rb[:, 128:224])
     V("mm")
     turn("mt", T.mt[:, :], T.mm[:, :])
-    fill("rl", T.rl[:, 2:4], N - late - 1)
+    V("w")
+    quant_w(0)
     V("mt", "kp")
-    scan("sgc", T.sg[:, 80:160], T.kp[:, 0:80], T.mt[:, 1:160:2], 0.0, A.mult, A.add)
-    scan("sgf", T.sg[:, 0:80], T.kp[:, 0:80], T.mt[:, 0:160:2], 0.0, A.mult, A.add)
-    V("sgc", "tq")
-    tt("sgx", T.sg[:, 87:160:8], T.sg[:, 87:160:8], T.tq[:, :], A.max)
-    fill("rl", T.rl[:, 4:6], N - late)
-    V("sgx", "sgf", "cl")
+    scan("sg", T.sg[:, 80:160], T.tq[:, :], T.mt[:, 1:160:2], 999.0, A.min, A.max)
+    scan("sg", T.sg[:, 0:80], T.kp[:, 0:80], T.mt[:, 0:160:2], 0.0, A.mult, A.add)
+    quant_w(1)
+    V("sg", "cl")
     cp("so", T.so[:, :], T.sg[:, 0:160].indirect(T.cl[:, 0:1]))
-    V("rc")
-    turn("kc", T.kc[:, :], T.rc[:, :])
-    R16, BK, Q16 = [col(T.kc, 32 * i) for i in range(3)]
+    quant_w(2)
     S("so")
     take("key", T.key[:, :], T.ident[:, 0:256].indirect(T.so[:, 8:16]))
-    V("so", "z1")
+    V("so")
     cp("win", T.win[:, 16:272].indirect(T.so[:, 0:8]), T.ident[:, 0:128])
     V("key")
     cp("win2", T.win2[:, 16:272].indirect(T.so[:, 0:8]), T.key[:, :])
     V("win")
     turn("wt1", T.wt1[:, 0:288], T.win[:, 0:288])
     turn("wt1", T.wt1[:, 288:544], T.win[:, 16:272])
-    V("win2", "z4")
+    V("win2")
     turn("wt2", T.wt2[:, 128:288], T.win2[:, 128:288])
     turn("wt2", T.wt2[:, 416:544], T.win2[:, 144:272])
     V("wt1")
     for t in range(3):
         cp("offp", T.offp[:, t:48:3], T.wt1[:, 0:544].indirect(T.cl[:, 2 * t + 2:2 * t + 3]))
-    V("wt2")
+    V("wt2", "z4")
     cp("kq", T.kq[:, :], T.wt2[:, 0:544].indirect(T.cl[:, 2:3]))
-    V("x")
-    done(vec.quantize_mx(T.xq[:, :], T.xz[:, :], T.xt[:, :]), "xq")
+    quant_w(3)
 
-    S("kc", "own", "d0i")
+    S("cnt", "own")
     shift("jm1", T.jm[:, :], T.ident[:, 0:160:16], 1.0, R16)
-    lin("r15", fc(8), R16, 1.0, -15.0)
+    lin("slf", T.slf[:, 16:18], T.kb[:, 160:162], 1.0 / B, -1.0)
+    lin("slf", T.slf[:, 18:20], T.one[:, 0:2], N - late - 1)
+    lin("slf", T.slf[:, 20:22], T.one[:, 0:2], N - late)
+    take("z2", col(T.sc, 0), CNT)
+    lin("z2", T.land1[:, 16:48], T.one[:, 0:32], 0.0)
+    lin("z2", T.thr[:, 32:32 + PAIR], T.ident[:, 0:PAIR], -1.0, CAP)
     S("jm1")
     lin("p2", T.fc[:, 0:2], T.jm[:, 0:2], -1.0, -1.0)
-    lin("p2", T.fc[:, 2:4], T.jm[:, 0:2], -1.0 / 64)
-    lin("jw", T.jw[:, :], T.jm[:, :], -1.0, Z - B - 16)
-    lin("d0", T.d0[:, 0:128], T.d0i[:, :], -SC, Z * SC)
-    S("p2", "jw")
-    shift("in1", T.fc[:, 4:6], T.fc[:, 0:2], 1.0, col(T.own, 4 * gl))
-    lin("jm", col(T.jm, 9), col(T.one, 0), 999.0)
+    lin("in1", fc(8), R16, -1.0 / 16, 7.5 / 16)
+    lin("in1", T.dl[:, 0:18:17], T.jm[:, 0:2], -1.0 / 64)
+    lin("in1", T.dl[:, 1:17], T.ident[:, 48:64], -1.0 / 64)
+    lin("in1", T.dl[:, 18:34], T.ident[:, 48:64], -1.0 / 64)
+    S("p2")
+    shift("in1", T.vl[:, 0:18:17], T.fc[:, 0:2], 1.0, col(T.own, 4 * gl))
+    lin("z3", T.fc[:, 24:27], T.jm[:, 0:3], -1.0, 31.5)
+    lin("z3", fc(27), R16, -SC, (Z - B - 16) * SC)
+    lin("z3", T.kr[:, 0:96:8], T.one[:, 0:12], -4096.0)
+    lin("z3", T.kr[:, 7:72:8], T.ident[:, 0:9], 16.0)
+    lin("z3", col(T.kr, 79), col(T.one, 0), 4096.0)
 
-    xc = lambda a, b: T.xq[:, 0:128].bitcast(U32).indirect(T.offp[:, a:b])
-    xz = lambda a, b: T.xz[:, 0:128].indirect(T.offp[:, a:b])
-    picks = (("o0", T.oq, T.oz, 0, 0, 9), ("o1", T.oq, T.oz, 144, 12, 21), ("p", T.pq, T.pz, 0, 10, 12),
-             ("p", T.pq, T.pz, 32, 8, 10), ("l", T.lq, T.lz, B - 16, 20, 24))
-    V("offp", "xq")
+    picks = dict(o0=(T.oq, T.oz, 0, 0, 9), o1=(T.oq, T.oz, 144, 12, 21), p0=(T.pq, T.pz, 0, 10, 12), p1=(T.pq, T.pz, 32, 8, 10),
+                 l0=(T.lq, T.lz, B - 16, 20, 24), l1=(T.lq, T.lz, Z - 8, 2, 3))
+
+    def codes(nm, step):
+        q, z, c, a, b = picks[nm]
+        cp(step, q[:, c:c + 16 * (b - a)].bitcast(U32), T.xq[:, 0:130].bitcast(U32).indirect(T.offp[:, a:b]))
+
+    def scales(nm, step):
+        q, z, c, a, b = picks[nm]
+        take(step, z[:, c:c + 16 * (b - a)], T.xz[:, 0:130].indirect(T.offp[:, a:b]))
+
     S("offp", "xq")
-    for nm, q, z, c, a, b in picks:
-        if nm != "l":
-            cp(nm + "q", q[:, c:c + 16 * (b - a)].bitcast(U32), xc(a, b))
-        take(nm + "z", z[:, c:c + 16 * (b - a)], xz(a, b))
+    for nm, step in (("o0", "oz"), ("o1", "oz"), ("p0", "pz"), ("p1", "pz")):
+        scales(nm, step)
+    V("offp", "xq")
+    codes("o0", "o0q")
+    codes("o1", "o1q")
 
     G("kq")
-    g.remote_dma_fused([xfer(core, rel[2 + h], topo, quarter[2 + h], sem.i2, T.kq[:, 4 * h:4 * h + 3], T.hand2[:, 0:3])
+    g.remote_dma_fused([xfer(core, rel[2 + h], topo, (off, on)[h], sem.i2, T.kq[:, 4 * h:4 * h + 3], T.hand2[:, 0:3])
                         for h in range(2)], local_sem=sem.lo)
-    g.remote_dma_fused([xfer(core, at(T, s, late), topo, off, sem.il, col(T.kq, late - 1), col(T.lk, N - late - 1))],
+    g.remote_dma_fused([xfer(core, at(T, s, late), topo, off, sem.i2, col(T.kq, late - 1), col(T.lk, N - late - 1))],
                        local_sem=sem.lo)
     for h in range(2):
         G("o%dq" % h)
         g.remote_dma_fused([xfer(core, rel[h], topo, off + on, sem.tc, T.oq[:, 144 * h:144 * h + 136].bitcast(dt.uint8),
                                  T.rq[:, :].bitcast(dt.uint8))], local_sem=sem.lo)
-    G("o0z", "o1z")
+    G("oz")
     g.remote_dma_fused([xfer(core, rel[2 + h], topo, (off, on)[h], sem.ts, T.oz[:, 144 * h:144 * h + 136], T.rz[:, :])
                         for h in range(2)], local_sem=sem.lo)
-
-    V("kq", "si", "kc", "in1")
-    cp("kl", T.kl[:, :], T.kq[:, late - 1:N:N - late])
-    tt("in2", T.fc[:, 6:8], T.fc[:, 4:6], T.fc[:, 2:4], A.min)
-    ts("rl", T.rl[:, 0:2], T.kc[:, 32:34], 1.0 / B, -1.0, A.mult, A.add)
-    ts("sj", T.sj[:, :], T.si[:, :], 31, None, A.bitwise_and)
-    V("w")
-    for o in range(O):
-        done(vec.quantize_mx(T.wq[:, 128 * o:128 * o + 128], T.wz[:, 128 * o:128 * o + 128], T.wt[:, 512 * o:512 * o + 512]), "wq")
-        if o == 0:
-            V("sj")
-            cp("sl", T.sl[:, :], T.sj[:, :])
 
     n1 = 0
     for u in range(1, N):
         d = roads(T, topo, (s - u) % N)[1]
         n1 += (2, 2, 4)[d.index(u)] if u in d else 8
-    V("z2")
-    vec.wait_ge(sem.i1, n1)
-    scan("sc", T.sc[:, 1:40], T.land1[:, 9:48], T.one[:, 0:39], CNT, A.add, A.mult)
-    V("sc")
-    turn("tot", T.tot[:, :], T.sc[:, 8:40])
-    S("sc", "rl")
-    take("rep", T.rep[:, :], T.sc[:, 0:16].indirect(T.rl[:, 0:6]))
     tA = lambda k, a, b: T.thr[:, 32:96].indirect(k[:, a:b])
     tB = lambda k, a, b: T.thr[:, 0:64].indirect(k[:, a:b])
-    V("tot", "thr", "kl")
+    c = B * (N - late + 1) + 16
+    PK = col(T.rpt, 4 * s)
+    V("z2", "slf", "kq")
+    ts("sl", T.sl[:, :], T.slf[:, :], 31.0, None, A.min)
+    vec.wait_ge(sem.i1, n1)
+    scan("sc", T.sc[:, 1:40], T.land1[:, 9:48], T.one[:, 0:39], CNT, A.add, A.mult)
+    cp("kl", T.kl[:, :], T.kq[:, late - 1:N:N - late])
+    codes("p0", "pq")
+    V("sc")
+    turn("tot", T.tot[:, :], T.sc[:, 8:40])
+    codes("p1", "pq")
+    codes("l1", "lq")
+    S("sc", "sl")
+    take("rep", T.rep[:, :], T.sc[:, 0:32].indirect(T.sl[:, 16:22]))
+    S("tot")
+    take("sa", T.sa[:, :], T.tot[:, 0:32].indirect(T.sl[:, 0:7]))
+    take("sa", T.sb[:, :], T.tot[:, 0:32].indirect(T.sl[:, 8:15]))
+    V("tot", "kl")
     ts("f0", T.fa[:, 0:32], tA(T.kl, 0, 2), col(T.tot, 4 * g1 + 1), None, A.is_le)
     ts("f0", T.fb[:, 0:32], tB(T.kl, 0, 2), col(T.tot, 4 * g2 + 2), None, A.is_le)
-    S("tot", "sl")
-    take("sa", T.sa[:, :], T.tot[:, 0:32].indirect(T.sl[:, 0:7]))
-    take("sb", T.sb[:, :], T.tot[:, 0:32].indirect(T.sl[:, 8:15]))
-    V("r15")
-    ts("z", T.zi[:, 0:1], col(T.tot, 4 * s), float(CAP), fc(8), A.min, A.subtract)
-    V("f0")
-    for c in range(2):
-        scan("vl", T.vl[:, 16 * c:16 * c + 16], T.fa[:, 0:16], T.fb[:, 0:16], fc(4 + c))
+    ts("za", fc(12), col(T.tot, 4 * s), float(CAP), 1.0 / 16, A.min, A.mult)
     V("rep")
     turn("rpt", T.rpt[:, :], T.rep[:, :])
-    V("vl", "in2", "dl")
-    for c in range(2):
-        scan("wl", T.wl[:, 16 * c:16 * c + 16], T.dl[:, :], T.vl[:, 16 * c:16 * c + 16], fc(6 + c), A.max, A.min)
-    V("z")
-    ts("zz", T.zi[:, 1:2], T.zi[:, 0:1], 15, None, A.bitwise_and)
+    V("f0", "in1")
+    for i in range(2):
+        scan("vl", T.vl[:, 17 * i + 1:17 * i + 17], T.fa[:, 0:16], T.fb[:, 0:16], col(T.vl, 17 * i))
+    V("za")
+    ts("zc", fc(21), fc(12), fc(8), WHOLE, A.add, A.add)
+    V("rpt")
+    ts("pd", fc(9), PK, -1.0, BK, A.mult, A.add)
+    V("vl")
+    for i in range(2):
+        scan("wl", T.wl[:, 17 * i:17 * i + 17], T.dl[:, 17 * i:17 * i + 17], T.vl[:, 17 * i:17 * i + 17], -1.0, A.max, A.min)
+    ts("pd", fc(10), PK, Q16, None, A.add)
+    V("zc")
+    ts("zf", fc(18), fc(21), 2.0 - WHOLE, None, A.add)
     V("wl")
-    ts("offl", T.offl[:, :], T.wl[:, 15:32:16], -64.0, 63.0, A.mult, A.min)
-    ts("zz", T.zi[:, 2:3], T.zi[:, 0:1], 4, None, A.logical_shift_right)
+    ts("offl", T.offl[:, :], T.wl[:, 16:34:17], -64.0, 63.0, A.mult, A.min)
+    V("pd", "jd")
+    ts("st", T.st[:, :], T.jd[:, :], fc(10), fc(9), A.is_ge, A.mult)
+    V("zf")
+    ts("ze", fc(23), fc(12), fc(18), 16.0, A.subtract, A.mult)
     V("offl", "pq")
     cp("o2q", T.o2q[:, :].bitcast(U32), T.pq[:, 0:64].bitcast(U32).indirect(T.offl[:, 0:2]))
-    c = B * (N - late + 1) + 16
-    S("rpt")
-    PK = col(T.rpt, 4 * s)
-    shift("pd", fc(9), PK, -1.0, BK)
-    shift("pd", fc(10), PK, 1.0, Q16)
+    V("st")
+    turn("stt", T.stt[:, :], T.st[:, :])
+    codes("l0", "lq")
+
+    S("rpt", "d0i")
+    lin("nl", fc(11), col(T.rpt, 32 + 4 * s), SC, (Z - c + 1) * SC)
+    lin("z3", T.d0[:, 0:128], T.d0i[:, :], -SC, Z * SC)
+    lin("z3", col(T.d0, 128), col(T.one, 0), 0.0)
+    lin("z3", col(T.fa, 144), col(T.one, 0), 200.0)
+    lin("z3", col(T.fb, 144), col(T.one, 0), 0.0)
+    lin("z3", T.mm4[:, :], T.one[:, 0:80], 0.0)
+    S("nl")
+    shift("nl2", fc(14), col(T.rpt, 64 + 4 * s), -SC, fc(11))
     S("offl", "pz")
     take("o2z", T.o2z[:, :], T.pz[:, 0:64].indirect(T.offl[:, 0:2]))
-    lin("nl", fc(11), col(T.rpt, 32 + 4 * s), SC, (Z - c + 1) * SC)
+    S("zf", "ze", "z3")
+    shift("ini", T.fc[:, 15:18], T.fc[:, 24:27], 1.0, fc(23))
+    shift("zg", T.em[:, 0:12], T.ident[:, 0:12], -1.0, fc(18), F.Abs)
+
     G("o2q")
     g.remote_dma_fused([xfer(core, at(T, s, late), topo, off, sem.tc, T.o2q[:, 0:BOTH].bitcast(dt.uint8),
                              T.lq[:, c:c + BOTH].bitcast(dt.uint8))], local_sem=sem.lo)
     G("o2z")
     g.remote_dma_fused([xfer(core, at(T, s, late), topo, off, sem.ts, T.o2z[:, 0:BOTH], T.lz[:, c:c + BOTH])], local_sem=sem.lo)
-    g.wait_ge(sem.lo, 24 + 16 + 32 + 16 + 16)
+    g.wait_ge(sem.lo, 24 + 24 + 32 + 16 + 16)
 
-    V("zz")
-    ts("zf", T.fc[:, 12:14], T.zi[:, 1:3], 0.5, None, A.add)
-    V("pd", "jd")
-    ts("st", T.st[:, :], T.jd[:, :], fc(10), fc(9), A.is_ge, A.mult)
-    vec.wait_ge(sem.il, 8)
-    cp("km", col(T.km, 0), col(T.lk, N - late - 1))
-    S("nl", "zf")
-    shift("nl2", fc(14), col(T.rpt, 64 + 4 * s), -SC, fc(11))
-    shift("ini", T.fc[:, 15:18], T.ident[:, 16:49:16], -1.0, fc(12))
-    shift("zm1", T.fc[:, 21:24], T.ident[:, 0:3], 1.0, fc(13))
-    S("zm1")
-    lin("zm", T.fc[:, 18:21], T.fc[:, 21:24], 1.0, -0.5)
-    V("st", "jm")
-    turn("stt", T.stt[:, :], T.st[:, :])
-    ts("msk", T.msk[:, :], T.jm[:, :], col(T.tot, 4 * s), SC, A.is_lt, A.mult)
-    V("stt")
-    scan("sw", T.sw[:, :], T.kp[:, :], T.stt[:, :], 0.0, A.mult, A.max)
-    V("km")
-    sl = (s + N - late) % N
-    ts("xl", T.xal[:, :], tA(T.km, 0, 1), col(T.tot, 4 * ((sl + 1) % N) + 1), -SC, A.is_le, A.mult)
-    ts("xl", T.xbl[:, :], tB(T.km, 0, 1), col(T.tot, 4 * ((sl + 2) % N) + 2), -SC, A.is_le, A.mult)
-    V("sw", "jw")
-    tt("ga0", T.ga0[:, :], T.jw[:, :], T.sw[:, 7:80:8], A.subtract)
-    V("xl", "nl2", "d0")
-    k = 16 * (N - late)
-    scan("d0l", T.d0[:, k:k + 16], T.xal[:, :], T.xbl[:, :], fc(14))
-    V("ga0", "msk", "z3")
-    tt("mf", T.mm4[:, 3:80:8], T.ga0[:, :], T.msk[:, :], A.mult)
-
-    vec.wait_ge(sem.i2, 32)
+    S("z2")
+    act.wait_ge(sem.i2, 40)
+    take("kb2", T.kb2[:, :], tB(T.lk, 0, 7))
+    S("zg")
+    shift("zm", T.em[:, 12:24], T.em[:, 0:12], -1.0, col(T.one, 0), F.Relu)
+    scales("l0", "lz")
+    scales("l1", "lz")
+    V("stt", "z3")
+    scan("sw", T.sw[:, :], T.kr[:, :], T.stt[:, :], 0.0, A.add, A.max)
+    vec.wait_ge(sem.i2, 40)
+    sl, k = (s + N - late) % N, N - late
+    ts("xl", T.xal[:, :], tA(T.lk, k - 2, k), col(T.tot, 4 * ((sl + 1) % N) + 1), -SC, A.is_le, A.mult)
+    ts("xl", T.xbl[:, :], tB(T.lk, k - 2, k), col(T.tot, 4 * ((sl + 2) % N) + 2), -SC, A.is_le, A.mult)
     V("sa")
     tt("f1", T.fa[:, 32:144], tA(T.lk, 0, 7), T.sa[:, :], A.is_le)
-    V("sb")
-    tt("f1", T.fb[:, 32:144], tB(T.lk, 0, 7), T.sb[:, :], A.is_le)
-    nm, q, z, c, a, b = picks[4]
-    cp("lq", q[:, c:c + 16 * (b - a)].bitcast(U32), xc(a, b))
+    V("kb2")
+    tt("f1", T.fb[:, 32:144], T.kb2[:, :], T.sb[:, :], A.is_le)
+    V("xl", "nl2")
+    scan("d0l", T.d0[:, 16 * k:16 * k + 16], T.xal[:, 16:32], T.xbl[:, 16:32], fc(14))
+    S("sw")
+    shift("mf", T.mm4[:, 3:80:8], T.sw[:, 7:80:8], -SC, fc(27), F.Relu)
     V("f1", "ini")
     for m in range(3):
         scan("w1%d" % m, T.w1[:, 130 * m:130 * m + 129], T.fa[:, 16:145], T.fb[:, 16:145], fc(15 + m))
@@ -477,20 +500,18 @@ def rank_program(g, core, T, topo):
     V("zm")
     for m in range(3):
         V("wv%d" % m)
-        ts("mf", T.mm4[:, m:80:8], T.ident[:, 0:10], fc(18 + m), col(T.wv, 130 * m + 128), A.is_equal, A.mult)
+        ts("mf", T.mm4[:, m:80:8], T.em[:, 14 - m:24 - m], col(T.wv, 130 * m + 128), None, A.mult)
     V("mf")
     scan("ms", T.ms[:, :], T.kp[:, 0:80], T.mm4[:, :], 0.0, A.mult, A.add)
-    V("zt")
-    done(vec.quantize_mx(T.lq[:, Z:Z + 128], T.lz[:, Z:Z + 128], T.zt[:, :]), "zq")
     V("ms")
     ts("offh", T.offh[:, :], T.ms[:, 7:80:8], -1024.0, float(Z), A.mult, A.add)
 
-    S("offh", "lz", "zq")
+    S("offh", "lz")
     act.wait_ge(sem.ts, 40)
-    take("hz", T.hz[:, :], T.lz[:, 0:Z + 32].indirect(T.offh[:, 0:10]))
-    V("offh", "lq", "zq")
+    take("hz", T.hz[:, :], T.lz[:, 0:Z + 8].indirect(T.offh[:, 0:10]))
+    V("offh", "lq")
     vec.wait_ge(sem.tc, 40)
-    cp("hq", T.hq[:, :].bitcast(U32), T.lq[:, 0:Z + 32].bitcast(U32).indirect(T.offh[:, 0:10]))
+    cp("hq", T.hq[:, :].bitcast(U32), T.lq[:, 0:Z + 8].bitcast(U32).indirect(T.offh[:, 0:10]))
     need(QT, "wq", "hq", "hz")
     for o in range(O):
         done(ten.matmul_mx(T.ps[:, 512 * o:512 * o + ROOM], T.wq[:, 128 * o:128 * o + 128], T.wz[:, 128 * o:128 * o + 128],

@@ -14,13 +14,14 @@ WHOLE = 1.5 * 2 ** 23
 F4, B2, I4, U2, MX, U1 = "float32", "bfloat16", "int32", "uint16", "float8_e4m3fn_x4", "uint8"
 SIZES = {
     I4: dict(c1b=8, c2b=8, cm=8, cs=10, yi=64, yr=80),
-    U2: dict(cu1=8, cu=16, sh=2, cl=8, so=16, offp=48, kq=16, kl=2, lk=8, hand2=4, sl=22, offl=2, offh=10),
-    F4: dict(r0=32, k0=32, yc=80, sg=160, fc=32, d0i=128, d0=130, dl=34, slf=22, jm=10, st=96, stt=96, sw=96, em=24,
-             mm4=80, ms=80, wv=390, ys=640, xal=32, xbl=32, wl=34, rep=96, rpt=96),
+    U2: dict(cu1=8, cu=16, sh=2, cl=8, so=16, offp=48, kq=16, kl=2, km=2, cf=4, lk=8, hand2=4, sl=22, offl=2, offh=16),
+    F4: dict(r0=32, k0=32, yc=80, fc=32, d0i=128, d0=146, dl=34, slf=22, jm=10, st=96, stt=96, sw=96,
+             wv=534, ys=640, xal=16, xbl=16, wl=34, rep=96, rpt=96),
     B2: dict(ra=160, ka=160, rb=224, kb=224, one=256, ident=256, kp=96, kr=96, tq=80, tn=8, gn=160, cnt=160, own=32,
-             ta=80, tb=80, ga=160, gb=160, ca=160, cb=160, ua=160, ub=160, xa=160, xb=160, xs=160, cum=160, mm=160, mt=160,
+             ta=80, tb=80, ga=144, gb=144, ca=144, cb=144, ua=144, ub=144, xa=144, xb=144, xs=144, cum=144, mm=160, mt=160,
+             sg=160, tk=32, ka1=128, kb1=128, ka2=128, kb2=128, ka3=128, kb3=128,
              win=288, wt1=544, key=128, win2=288, wt2=544, thr=96, hand1=2, land1=48, sc=40, tot=32, sa=112, sb=112,
-             kb2=112, fa=146, fb=146, w1=390, vl=34, jd=96, xt=520, wt=2048),
+             fa=146, fb=146, w1=520, vl=34, jd=96, xt=520, wt=2048),
     MX: dict(xq=130, wq=512, oq=288, pq=64, o2q=32, rq=136, lq=448, hq=160),
     U1: dict(xz=130, wz=512, oz=288, pz=64, o2z=32, rz=136, lz=448, hz=160),
 }
@@ -28,7 +29,7 @@ SCRATCH = {"ps": ("psum", [128, 2048], F4)}
 for _d in SIZES:
     for _n in SIZES[_d]:
         SCRATCH[_n] = ("sbuf", [128, SIZES[_d][_n]], _d)
-SEMAPHORES = ["i1", "i2", "tc", "ts", "lo"] + ["s%d" % _i for _i in range(140)]
+SEMAPHORES = ["i1", "i2", "il", "tc", "ts", "lo"] + ["s%d" % _i for _i in range(140)]
 
 
 def bits(es):
@@ -183,10 +184,10 @@ def rank_program(g, core, T, topo):
     done(syn.dma_start(T.xt[:, 0:512], T.x[:, :]), "x", 16)
     done(syn.dma_start(T.wt[:, :], T.w[:, :]), "w", 16)
 
+    iota("r0", T.r0[:, :], [[1, 8], [0, 4]], 0)
     iota("k16", T.ra[:, 32:64], [[0, 2], [1, 8], [0, 2]], 0)
     iota("ra", T.ra[:, 0:32], [[-1, 2], [1, 16]], 1)
     iota("yi", T.yi[:, :], [[32, 8], [1, 8]], 33 * (N - 1 - s), True)
-    iota("r0", T.r0[:, :], [[1, 8], [0, 4]], 0)
     iota("rb", T.rb[:, 0:16], [[0, 2], [16, 4], [24, 2]], 7)
     iota("rb", T.rb[:, 16:32], [[-80, 2], [16, 4], [-8, 2]], 95)
     iota("rb", T.rb[:, 32:48], [[0, 2], [32, 4], [-256, 2]], 432)
@@ -201,42 +202,46 @@ def rank_program(g, core, T, topo):
     fill("ra", T.ra[:, 129:160:2], float(-MOVE))
     fill("ra", T.ra[:, 97:128:16], float(127 + MOVE))
     fill("ra", T.ra[:, 99:128:16], float(143 + MOVE))
+    V("r0")
+    fill("r0x", T.r0[:, 4 * g1 + 1:4 * g1 + 3], 99.0)
+    fill("r0x", col(T.r0, 4 * g2 + 2), 99.0)
     V("k16", "one")
     ts("ra", T.ra[:, 96:128:2], T.ra[:, 32:64:2], 32.0, -1.0, A.mult, A.add)
     for h in range(2):
         ts("ra", T.ra[:, 101 + 16 * h:112 + 16 * h:2], T.ra[:, 36:48:2], 16.0, 127.0, A.mult, A.add)
-    scan("ident", T.ident[:, :], T.one[:, :], T.one[:, :], -1.0, A.add, A.mult)
-    fill("yr", T.yr[:, 64:80], 999)
-    V("ra")
-    turn("ka", T.ka[:, :], T.ra[:, :])
-    V("yi")
-    ts("yr", T.yr[:, 0:64], T.yi[:, :], 0xE7, None, A.bitwise_and)
-    SH, K, MUL, BASE, LIM = [col(T.ka, 32 * i) for i in range(5)]
-    V("r0")
-    fill("r0x", T.r0[:, 4 * g1 + 1:4 * g1 + 3], 99.0)
-    fill("r0x", col(T.r0, 4 * g2 + 2), 99.0)
-    V("ka", "yr")
-    ts("yc", T.yc[:, :], T.yr[:, :], MUL, WHOLE, A.mult, A.add)
     V("r0x")
     turn("k0", T.k0[:, :], T.r0[:, :])
-    ts("sh", T.sh[:, 0:1], SH, 9.0, None, A.min)
-    fill("sh", T.cs[:, 0:10:9], 64)
-    V("yc")
-    ts("ta", T.ta[:, :], T.yc[:, :], -WHOLE, K, A.add, A.is_equal)
+    scan("ident", T.ident[:, :], T.one[:, :], T.one[:, :], -1.0, A.add, A.mult)
+    V("ra")
+    turn("ka", T.ka[:, :], T.ra[:, :])
+    fill("yr", T.yr[:, 64:80], 999)
+    V("yi")
+    ts("yr", T.yr[:, 0:64], T.yi[:, :], 0xE7, None, A.bitwise_and)
     V("k0", "ident")
-    ts("tn", T.tn[:, :], T.ident[:, 0:8], col(T.k0, 0), None, A.is_equal)
-    ts("tb", T.tb[:, :], T.yc[:, :], -WHOLE - 32, K, A.add, A.is_equal)
+    ts("cu1", T.tn[:, :], T.ident[:, 0:8], col(T.k0, 0), None, A.is_equal)
+    SH, K, MUL, BASE, LIM = [col(T.ka, 32 * i) for i in range(5)]
+    fill("sh", T.cs[:, 0:10:9], 64)
+    V("ka", "yr")
+    ts("yc", T.yc[:, :], T.yr[:, :], MUL, WHOLE, A.mult, A.add)
+    ts("sh", T.sh[:, 0:1], SH, 9.0, None, A.min)
+    ts("cu1", T.tk[:, 0:16], T.ident[:, 0:16], float(g1), None, A.is_equal)
+    ts("cu1", T.tk[:, 16:32], T.ident[:, 0:16], float(g2), None, A.is_equal)
 
     V("c1")
     cp("cu1", T.cu1[:, :], T.c1b[:, :])
     ts("cm", T.cm[:, :], T.c1b[:, :], 8, None, A.mult)
-    fill("gn", T.gn[:, 128:160], 0.0)
-    S("cu1", "tn")
+    S("one")
+    lin("gn", T.gn[:, 128:160], T.one[:, 0:32], 0.0)
+    lin("kp1", T.kp[:, :], T.one[:, 0:96])
+    lin("kp1", T.tq[:, :], T.one[:, 0:80], 999.0)
+    lin("z1", T.win[:, 0:256], T.one[:, :], 128.0)
+    S("cu1")
     take("gn", T.gn[:, 0:128], T.tn[:, 0:8].indirect(T.cu1[:, 0:8]))
+    V("yc")
+    ts("ta", T.ta[:, :], T.yc[:, :], -WHOLE, K, A.add, A.is_equal)
     V("c2", "cm")
     tt("cs", T.cs[:, 1:9], T.cm[:, :], T.c2b[:, :], A.add)
-    fill("kp1", T.kp[:, :], 1.0)
-    fill("kp1", T.tq[:, :], 999.0)
+    ts("tb", T.tb[:, :], T.yc[:, :], -WHOLE - 32, K, A.add, A.is_equal)
     V("cs", "sh")
     cp("cu", T.cu[:, :], T.cs[:, 0:10].indirect(T.sh[:, 0:1]))
     V("gn")
@@ -258,86 +263,94 @@ def rank_program(g, core, T, topo):
     iota("jd", T.jd[:, :], [[64, 3], [0, 2], [1, 16]], 0)
     iota("d0i", T.d0i[:, :], [[B, 8], [1, 16]], B)
 
-    S("one", "ident", "ka")
-    lin("r15", fc(28), SH, -1.0, 127.0)
-    lin("z1", T.win[:, 0:256], T.one[:, :], 128.0)
+    take("g1", T.ka1[:, :], T.tk[:, 0:16].indirect(T.cu1[:, 0:8]))
     S("cu", "ta")
-    take("ga", T.ga[:, :], T.ta[:, 0:80].indirect(T.cu[:, 0:10]))
+    take("ga", T.ga[:, :], T.ta[:, 0:80].indirect(T.cu[:, 0:9]))
+    take("g2", T.kb1[:, :], T.tk[:, 16:32].indirect(T.cu1[:, 0:8]))
+    S("ident", "ka")
+    lin("xt0", T.xt[:, 512:520], T.one[:, 0:8], 0.0)
+    lin("r15", fc(28), SH, -1.0, 127.0)
+    lin("mm", T.mm[:, 144:160], T.one[:, 0:16], 0.0)
     S("kp1", "r15")
     lin("kp", T.kp[:, 0:96:8], T.one[:, 0:12], 0.0)
     shift("kp", T.tq[:, 0:80:8], T.ident[:, 0:160:16], -1.0, fc(28))
-    lin("z1", T.win[:, 256:288], T.one[:, 0:32], 128.0)
-    lin("z1", T.win2[:, 128:288], T.one[:, 0:160], NOKEY)
-    lin("z1", T.xt[:, 512:520], T.one[:, 0:8], 0.0)
+    for h in range(2):
+        lin("thr1", T.rb[:, 160 + 16 * h:176 + 16 * h], T.ra[:, 32:64:2], B, B)
+        lin("rc", T.rb[:, 128 + 16 * h:144 + 16 * h], T.ident[:, 0:16])
     lin("thr1", T.thr[:, :], T.one[:, 0:96], 255.0)
     lin("thr1", T.kr[:, :], T.one[:, 0:96], 0.0)
-    for h in range(2):
-        lin("rc", T.rb[:, 128 + 16 * h:144 + 16 * h], T.ident[:, 0:16])
-        lin("thr1", T.rb[:, 160 + 16 * h:176 + 16 * h], T.ra[:, 32:64:2], B, B)
     for q in range(4):
         lin("rc", T.rb[:, 192 + 8 * q:200 + 8 * q], T.one[:, 0:8], -16 * q)
     S("thr1")
     lin("rc", T.rb[:, 167:192:8], T.one[:, 0:4], 2048.0)
+    lin("z1", T.win[:, 256:288], T.one[:, 0:32], 128.0)
+    lin("z1", T.win2[:, 128:288], T.one[:, 0:160], NOKEY)
     lin("z4", T.wt2[:, 0:128], T.one[:, 0:128], 0.0)
     lin("z4", T.wt2[:, 288:416], T.one[:, 0:128], 0.0)
     V("cu", "tb")
-    cp("gb", T.gb[:, :], T.tb[:, 0:80].indirect(T.cu[:, 0:10]))
+    cp("gb", T.gb[:, :], T.tb[:, 0:80].indirect(T.cu[:, 0:9]))
     V("rb")
     turn("kb", T.kb[:, 0:128], T.rb[:, 0:128])
     V("cnt")
     turn("own", T.own[:, :], T.cnt[:, 128:160])
-    V("gb")
-    scan("cb", T.cb[:, :], T.gb[:, :], T.one[:, 0:160], 0.0, A.add, A.mult)
     V("ga")
-    scan("ca", T.ca[:, :], T.ga[:, :], T.one[:, 0:160], 0.0, A.add, A.mult)
-    V("kb")
-    cp("cl", T.cl[:, 0:8:2], T.kb[:, 0:97:32])
-    V("cb")
-    ts("ub", T.ub[:, :], T.cb[:, :], col(T.cb, 159), float(-MOVE), A.subtract, A.is_gt)
+    scan("ca", T.ca[:, :], T.ga[:, :], T.one[:, 0:144], 0.0, A.add, A.mult)
+    V("gb")
+    scan("cb", T.cb[:, :], T.gb[:, :], T.one[:, 0:144], 0.0, A.add, A.mult)
+    V("g1")
+    scan("k1", T.ka2[:, :], T.ka1[:, :], T.one[:, 0:128], -1.0, A.add, A.mult)
     V("ca")
-    ts("ua", T.ua[:, :], T.ca[:, :], col(T.ca, 159), LIM, A.subtract, A.is_gt)
-    V("ub")
-    mask("xb", T.xb[:, :], T.ub[:, :], T.gb[:, :])
+    ts("ua", T.ua[:, :], T.ca[:, :], col(T.ca, 143), LIM, A.subtract, A.is_gt)
+    V("cb")
+    ts("ub", T.ub[:, :], T.cb[:, :], col(T.cb, 143), float(-MOVE), A.subtract, A.is_gt)
+    V("g2")
+    scan("k1", T.kb2[:, :], T.kb1[:, :], T.one[:, 0:128], 31.0, A.add, A.mult)
     V("ua")
     mask("xa", T.xa[:, :], T.ua[:, :], T.ga[:, :])
-    V("x", "z1")
+    V("ub")
+    mask("xb", T.xb[:, :], T.ub[:, :], T.gb[:, :])
+    V("x", "xt0")
     done(vec.quantize_mx(T.xq[:, :], T.xz[:, :], T.xt[:, :]), "xq")
     V("xa", "xb")
     tt("cum", T.xs[:, :], T.xa[:, :], T.xb[:, :], A.add)
     scan("cum", T.cum[:, :], T.xa[:, :], T.xb[:, :], BASE)
+    V("k1")
+    mask("k2", T.ka3[:, :], T.ka2[:, :], T.ka1[:, :])
+    mask("k2", T.kb3[:, :], T.kb2[:, :], T.kb1[:, :])
     R16, BK, Q16 = [col(T.kb, 128 + 32 * i) for i in range(3)]
     V("cum")
-    mask("mm", T.mm[:, :], T.cum[:, :], T.xs[:, :])
-    V("rc")
-    turn("own", T.kb[:, 128:224], T.rb[:, 128:224])
+    mask("mm", T.mm[:, 0:144], T.cum[:, :], T.xs[:, :])
+    V("k2")
+    tt("key", T.key[:, :], T.ka3[:, :], T.kb3[:, :], A.add)
     V("mm")
     turn("mt", T.mt[:, :], T.mm[:, :])
-    V("w")
-    quant_w(0)
+    V("kb")
+    cp("cl", T.cl[:, 0:8:2], T.kb[:, 0:97:32])
+    V("rc")
+    turn("own", T.kb[:, 128:224], T.rb[:, 128:224])
     V("mt", "kp")
     scan("sg", T.sg[:, 80:160], T.tq[:, :], T.mt[:, 1:160:2], 999.0, A.min, A.max)
     scan("sg", T.sg[:, 0:80], T.kp[:, 0:80], T.mt[:, 0:160:2], 0.0, A.mult, A.add)
-    quant_w(1)
+    V("w")
+    quant_w(0)
     V("sg", "cl")
     cp("so", T.so[:, :], T.sg[:, 0:160].indirect(T.cl[:, 0:1]))
-    quant_w(2)
-    S("so")
-    take("key", T.key[:, :], T.ident[:, 0:256].indirect(T.so[:, 8:16]))
-    V("so")
-    cp("win", T.win[:, 16:272].indirect(T.so[:, 0:8]), T.ident[:, 0:128])
-    V("key")
+    quant_w(1)
+    V("so", "key", "z1")
     cp("win2", T.win2[:, 16:272].indirect(T.so[:, 0:8]), T.key[:, :])
-    V("win")
-    turn("wt1", T.wt1[:, 0:288], T.win[:, 0:288])
-    turn("wt1", T.wt1[:, 288:544], T.win[:, 16:272])
+    cp("win", T.win[:, 16:272].indirect(T.so[:, 0:8]), T.ident[:, 0:128])
     V("win2")
     turn("wt2", T.wt2[:, 128:288], T.win2[:, 128:288])
     turn("wt2", T.wt2[:, 416:544], T.win2[:, 144:272])
+    V("win")
+    turn("wt1", T.wt1[:, 0:288], T.win[:, 0:288])
+    V("wt2", "z4")
+    cp("kq", T.kq[:, :], T.wt2[:, 0:544].indirect(T.cl[:, 2:3]))
+    turn("wt1", T.wt1[:, 288:544], T.win[:, 16:272])
+    quant_w(2)
     V("wt1")
     for t in range(3):
         cp("offp", T.offp[:, t:48:3], T.wt1[:, 0:544].indirect(T.cl[:, 2 * t + 2:2 * t + 3]))
-    V("wt2", "z4")
-    cp("kq", T.kq[:, :], T.wt2[:, 0:544].indirect(T.cl[:, 2:3]))
     quant_w(3)
 
     S("cnt", "own")
@@ -350,17 +363,21 @@ def rank_program(g, core, T, topo):
     lin("z2", T.thr[:, 32:32 + PAIR], T.ident[:, 0:PAIR], -1.0, CAP)
     S("jm1")
     lin("p2", T.fc[:, 0:2], T.jm[:, 0:2], -1.0, -1.0)
-    lin("in1", fc(8), R16, -1.0 / 16, 7.5 / 16)
     lin("in1", T.dl[:, 0:18:17], T.jm[:, 0:2], -1.0 / 64)
     lin("in1", T.dl[:, 1:17], T.ident[:, 48:64], -1.0 / 64)
     lin("in1", T.dl[:, 18:34], T.ident[:, 48:64], -1.0 / 64)
     S("p2")
     shift("in1", T.vl[:, 0:18:17], T.fc[:, 0:2], 1.0, col(T.own, 4 * gl))
-    lin("z3", T.fc[:, 24:27], T.jm[:, 0:3], -1.0, 31.5)
+    lin("z3", T.fc[:, 23:27], T.jm[:, 0:4], -1.0, 7.0)
     lin("z3", fc(27), R16, -SC, (Z - B - 16) * SC)
+    lin("z3", fc(8), R16, 1.0, 12.0)
+    lin("z3", fc(4), R16, -1.0, 4.0)
+    lin("z3", fc(5), R16, -100.0)
     lin("z3", T.kr[:, 0:96:8], T.one[:, 0:12], -4096.0)
     lin("z3", T.kr[:, 7:72:8], T.ident[:, 0:9], 16.0)
     lin("z3", col(T.kr, 79), col(T.one, 0), 4096.0)
+    S("d0i")
+    lin("z3", T.d0[:, 0:128], T.d0i[:, :], -SC, Z * SC)
 
     picks = dict(o0=(T.oq, T.oz, 0, 0, 9), o1=(T.oq, T.oz, 144, 12, 21), p0=(T.pq, T.pz, 0, 10, 12), p1=(T.pq, T.pz, 32, 8, 10),
                  l0=(T.lq, T.lz, B - 16, 20, 24), l1=(T.lq, T.lz, Z - 8, 2, 3))
@@ -374,8 +391,13 @@ def rank_program(g, core, T, topo):
         take(step, z[:, c:c + 16 * (b - a)], T.xz[:, 0:130].indirect(T.offp[:, a:b]))
 
     S("offp", "xq")
-    for nm, step in (("o0", "oz"), ("o1", "oz"), ("p0", "pz"), ("p1", "pz")):
-        scales(nm, step)
+    scales("o0", "oz")
+    scales("o1", "oz")
+    lin("z3", col(T.d0, 128), col(T.one, 0), 0.0)
+    lin("z3", T.fa[:, 144:146], T.one[:, 0:2], 8192.0)
+    lin("z3", T.fa[:, 128:144], T.one[:, 0:16], 0.0)
+    lin("z3", T.fb[:, 144:146], T.one[:, 0:2], 0.0)
+    lin("z3", T.wv[:, 520:524], T.one[:, 0:4], 0.0)
     V("offp", "xq")
     codes("o0", "o0q")
     codes("o1", "o1q")
@@ -383,7 +405,7 @@ def rank_program(g, core, T, topo):
     G("kq")
     g.remote_dma_fused([xfer(core, rel[2 + h], topo, (off, on)[h], sem.i2, T.kq[:, 4 * h:4 * h + 3], T.hand2[:, 0:3])
                         for h in range(2)], local_sem=sem.lo)
-    g.remote_dma_fused([xfer(core, at(T, s, late), topo, off, sem.i2, col(T.kq, late - 1), col(T.lk, N - late - 1))],
+    g.remote_dma_fused([xfer(core, at(T, s, late), topo, off, sem.il, col(T.kq, late - 1), col(T.lk, N - late - 1))],
                        local_sem=sem.lo)
     for h in range(2):
         G("o%dq" % h)
@@ -410,57 +432,68 @@ def rank_program(g, core, T, topo):
     V("sc")
     turn("tot", T.tot[:, :], T.sc[:, 8:40])
     codes("p1", "pq")
-    codes("l1", "lq")
+    vec.wait_ge(sem.il, 8)
+    cp("km", T.km[:, 0:1], col(T.lk, N - late - 1))
     S("sc", "sl")
     take("rep", T.rep[:, :], T.sc[:, 0:32].indirect(T.sl[:, 16:22]))
-    S("tot")
-    take("sa", T.sa[:, :], T.tot[:, 0:32].indirect(T.sl[:, 0:7]))
-    take("sa", T.sb[:, :], T.tot[:, 0:32].indirect(T.sl[:, 8:15]))
     V("tot", "kl")
     ts("f0", T.fa[:, 0:32], tA(T.kl, 0, 2), col(T.tot, 4 * g1 + 1), None, A.is_le)
     ts("f0", T.fb[:, 0:32], tB(T.kl, 0, 2), col(T.tot, 4 * g2 + 2), None, A.is_le)
-    ts("za", fc(12), col(T.tot, 4 * s), float(CAP), 1.0 / 16, A.min, A.mult)
+    ts("za", fc(12), col(T.tot, 4 * s), float(CAP), -7.5, A.min, A.add)
     V("rep")
     turn("rpt", T.rpt[:, :], T.rep[:, :])
     V("f0", "in1")
     for i in range(2):
         scan("vl", T.vl[:, 17 * i + 1:17 * i + 17], T.fa[:, 0:16], T.fb[:, 0:16], col(T.vl, 17 * i))
-    V("za")
-    ts("zc", fc(21), fc(12), fc(8), WHOLE, A.add, A.add)
-    V("rpt")
-    ts("pd", fc(9), PK, -1.0, BK, A.mult, A.add)
+    V("km")
+    sl, k = (s + N - late) % N, N - late
+    ts("xl", T.xal[:, :], tA(T.km, 0, 1), col(T.tot, 4 * ((sl + 1) % N) + 1), -SC, A.is_le, A.mult)
+    ts("xl", T.xbl[:, :], tB(T.km, 0, 1), col(T.tot, 4 * ((sl + 2) % N) + 2), -SC, A.is_le, A.mult)
+    scales("p0", "pz")
+    scales("p1", "pz")
+    S("tot")
+    take("sa", T.sa[:, :], T.tot[:, 0:32].indirect(T.sl[:, 0:7]))
+    S("za")
+    lin("zc", fc(21), fc(12), 1.0 / 16, WHOLE)
+    S("rpt")
+    shift("pd", fc(9), PK, -1.0, BK)
+    shift("pd", fc(10), PK, 1.0, Q16)
+    lin("nl", fc(11), col(T.rpt, 32 + 4 * s), SC, (Z - c + 1) * SC)
+    S("zc")
+    lin("zf", fc(19), fc(21), 1.0, -WHOLE)
+    S("nl")
+    shift("nl2", fc(14), col(T.rpt, 64 + 4 * s), -SC, fc(11))
+    take("sa", T.sb[:, :], T.tot[:, 0:32].indirect(T.sl[:, 8:15]))
     V("vl")
     for i in range(2):
         scan("wl", T.wl[:, 17 * i:17 * i + 17], T.dl[:, 17 * i:17 * i + 17], T.vl[:, 17 * i:17 * i + 17], -1.0, A.max, A.min)
-    ts("pd", fc(10), PK, Q16, None, A.add)
-    V("zc")
-    ts("zf", fc(18), fc(21), 2.0 - WHOLE, None, A.add)
-    V("wl")
-    ts("offl", T.offl[:, :], T.wl[:, 16:34:17], -64.0, 63.0, A.mult, A.min)
+    codes("l1", "lq")
     V("pd", "jd")
     ts("st", T.st[:, :], T.jd[:, :], fc(10), fc(9), A.is_ge, A.mult)
+    V("wl")
+    ts("offl", T.offl[:, :], T.wl[:, 16:34:17], -64.0, 63.0, A.mult, A.min)
     V("zf")
-    ts("ze", fc(23), fc(12), fc(18), 16.0, A.subtract, A.mult)
-    V("offl", "pq")
-    cp("o2q", T.o2q[:, :].bitcast(U32), T.pq[:, 0:64].bitcast(U32).indirect(T.offl[:, 0:2]))
+    ts("c0", T.cf[:, 0:1], fc(19), 4.0, None, A.add)
     V("st")
     turn("stt", T.stt[:, :], T.st[:, :])
-    codes("l0", "lq")
+    V("offl", "pq")
+    cp("o2q", T.o2q[:, :].bitcast(U32), T.pq[:, 0:64].bitcast(U32).indirect(T.offl[:, 0:2]))
 
-    S("rpt", "d0i")
-    lin("nl", fc(11), col(T.rpt, 32 + 4 * s), SC, (Z - c + 1) * SC)
-    lin("z3", T.d0[:, 0:128], T.d0i[:, :], -SC, Z * SC)
-    lin("z3", col(T.d0, 128), col(T.one, 0), 0.0)
-    lin("z3", col(T.fa, 144), col(T.one, 0), 200.0)
-    lin("z3", col(T.fb, 144), col(T.one, 0), 0.0)
-    lin("z3", T.mm4[:, :], T.one[:, 0:80], 0.0)
-    S("nl")
-    shift("nl2", fc(14), col(T.rpt, 64 + 4 * s), -SC, fc(11))
+    S("zf", "z3")
+    shift("ze", fc(22), fc(19), -16.0, fc(12))
     S("offl", "pz")
     take("o2z", T.o2z[:, :], T.pz[:, 0:64].indirect(T.offl[:, 0:2]))
-    S("zf", "ze", "z3")
-    shift("ini", T.fc[:, 15:18], T.fc[:, 24:27], 1.0, fc(23))
-    shift("zg", T.em[:, 0:12], T.ident[:, 0:12], -1.0, fc(18), F.Abs)
+    S("ze")
+    shift("in2", fc(6), fc(23), 1.0, fc(22))
+    shift("ini", T.fc[:, 16:19], T.fc[:, 24:27], 1.0, fc(22))
+    shift("u1", fc(29), fc(19), 1.0, fc(4), F.Relu)
+    S("in2")
+    done(act.activation(fc(7), fc(6), F.Relu, scale=400.0), "in3")
+    shift("u1", fc(30), fc(19), 100.0, fc(5), F.Relu)
+    S("in3")
+    shift("in0", fc(15), fc(7), -1.0, fc(6))
+    S("u1")
+    shift("u2", fc(31), fc(29), -1.0, fc(30))
 
     G("o2q")
     g.remote_dma_fused([xfer(core, at(T, s, late), topo, off, sem.tc, T.o2q[:, 0:BOTH].bitcast(dt.uint8),
@@ -469,42 +502,35 @@ def rank_program(g, core, T, topo):
     g.remote_dma_fused([xfer(core, at(T, s, late), topo, off, sem.ts, T.o2z[:, 0:BOTH], T.lz[:, c:c + BOTH])], local_sem=sem.lo)
     g.wait_ge(sem.lo, 24 + 24 + 32 + 16 + 16)
 
-    S("z2")
-    act.wait_ge(sem.i2, 40)
-    take("kb2", T.kb2[:, :], tB(T.lk, 0, 7))
-    S("zg")
-    shift("zm", T.em[:, 12:24], T.em[:, 0:12], -1.0, col(T.one, 0), F.Relu)
-    scales("l0", "lz")
-    scales("l1", "lz")
-    V("stt", "z3")
-    scan("sw", T.sw[:, :], T.kr[:, :], T.stt[:, :], 0.0, A.add, A.max)
-    vec.wait_ge(sem.i2, 40)
-    sl, k = (s + N - late) % N, N - late
-    ts("xl", T.xal[:, :], tA(T.lk, k - 2, k), col(T.tot, 4 * ((sl + 1) % N) + 1), -SC, A.is_le, A.mult)
-    ts("xl", T.xbl[:, :], tB(T.lk, k - 2, k), col(T.tot, 4 * ((sl + 2) % N) + 2), -SC, A.is_le, A.mult)
+    vec.wait_ge(sem.i2, 32)
     V("sa")
-    tt("f1", T.fa[:, 32:144], tA(T.lk, 0, 7), T.sa[:, :], A.is_le)
-    V("kb2")
-    tt("f1", T.fb[:, 32:144], T.kb2[:, :], T.sb[:, :], A.is_le)
-    V("xl", "nl2")
-    scan("d0l", T.d0[:, 16 * k:16 * k + 16], T.xal[:, 16:32], T.xbl[:, 16:32], fc(14))
+    tt("f1", T.fa[:, 32:128], tA(T.lk, 0, 6), T.sa[:, 0:96], A.is_le)
+    tt("f1", T.fb[:, 32:144], tB(T.lk, 0, 7), T.sb[:, :], A.is_le)
+    V("stt", "xl", "nl2", "z3")
+    scan("sw", T.sw[:, :], T.kr[:, :], T.stt[:, :], 0.0, A.add, A.max)
+    scan("d0l", T.d0[:, 16 * k:16 * k + 16], T.xal[:, :], T.xbl[:, :], fc(14))
     S("sw")
-    shift("mf", T.mm4[:, 3:80:8], T.sw[:, 7:80:8], -SC, fc(27), F.Relu)
+    shift("mf", T.wv[:, 524:534], T.sw[:, 7:80:8], -SC, fc(27), F.Relu)
+    scales("l1", "lz")
+    S("mf", "c0")
+    take("fv", T.d0[:, 129:145], T.wv[:, 520:534].indirect(T.cf[:, 0:1]))
+    scales("l0", "lz")
     V("f1", "ini")
-    for m in range(3):
-        scan("w1%d" % m, T.w1[:, 130 * m:130 * m + 129], T.fa[:, 16:145], T.fb[:, 16:145], fc(15 + m))
+    for m in (1, 2, 3, 0):
+        V("ini" if m else "in0")
+        scan("w1%d" % m, T.w1[:, 130 * m:130 * m + 130], T.fa[:, 16:146], T.fb[:, 16:146], fc(15 + m))
     V("d0l")
-    for m in range(3):
+    for m in (1, 2, 3, 0):
         V("w1%d" % m)
-        scan("wv%d" % m, T.wv[:, 130 * m:130 * m + 129], T.d0[:, 0:129], T.w1[:, 130 * m:130 * m + 129], -1.0, A.max, A.min)
-    V("zm")
-    for m in range(3):
-        V("wv%d" % m)
-        ts("mf", T.mm4[:, m:80:8], T.em[:, 14 - m:24 - m], col(T.wv, 130 * m + 128), None, A.mult)
-    V("mf")
-    scan("ms", T.ms[:, :], T.kp[:, 0:80], T.mm4[:, :], 0.0, A.mult, A.add)
-    V("ms")
-    ts("offh", T.offh[:, :], T.ms[:, 7:80:8], -1024.0, float(Z), A.mult, A.add)
+        if m:
+            scan("wv", T.wv[:, 4 + m:520:4], T.d0[:, 0:129], T.w1[:, 130 * m:130 * m + 129], -1.0, A.max, A.min)
+        else:
+            V("u2", "fv")
+            ts("wv", T.cf[:, 2:3], fc(31), 8.0, fc(8), A.add, A.min)
+            scan("wv", T.wv[:, 0:520:4], T.d0[:, 0:130], T.w1[:, 0:130], -1.0, A.max, A.min)
+    codes("l0", "lq")
+    V("wv")
+    ts("offh", T.offh[:, :], T.wv[:, 512:534].indirect(T.cf[:, 2:3]), -1024.0, float(Z), A.mult, A.add)
 
     S("offh", "lz")
     act.wait_ge(sem.ts, 40)

@@ -8,20 +8,20 @@ PAIR, MOVE, BOTH = 24, 8, 30
 B = 48
 Z = B * (N + 1) + 8
 NOKEY = 24.0
-SC = 1.0 / 1024
+SC, MID = 1.0 / 1024, 236
 WHOLE = 1.5 * 2 ** 23
 
 F4, B2, I4, U2, MX, U1 = "float32", "bfloat16", "int32", "uint16", "float8_e4m3fn_x4", "uint8"
 SIZES = {
-    I4: dict(c1b=8, c2b=8, cm=8, cs=10, yi=64, yr=80),
-    U2: dict(cu1=8, cu=16, sh=2, cl=8, so=16, offp=48, kq=16, kl=2, km=2, cf=4, lk=8, hand2=4, sl=22, offl=2, offh=16),
-    F4: dict(r0=32, k0=32, yc=80, fc=32, d0i=128, d0=146, dl=34, slf=22, jm=10, st=96, stt=96, sw=96,
-             wv=534, ys=640, xal=16, xbl=16, wl=34, rep=96, rpt=96),
-    B2: dict(ra=160, ka=160, rb=224, kb=224, one=256, ident=256, kp=96, kr=96, tq=80, tn=8, gn=160, cnt=160, own=32,
-             ta=80, tb=80, ga=144, gb=144, ca=144, cb=144, ua=144, ub=144, xa=144, xb=144, xs=144, cum=144, mm=160, mt=160,
-             sg=160, tk=32, ka1=128, kb1=128, ka2=128, kb2=128, ka3=128, kb3=128,
+    I4: dict(c1b=8, c2b=8, cm=8, cs=8, yi=64, yr=64),
+    U2: dict(cu1=8, cu=8, cl=8, so=16, offp=48, kq=16, kl=2, km=2, cf=4, lk=8, hand2=4, sl=22, offl=2, offh=16),
+    F4: dict(r0=32, k0=32, yc=64, fc=32, d0i=136, slf=22, jm=10, st=96, stt=96, sw=96,
+             ys=640, dl=35, wl=35, rep=128, rpt=128, sd=8),
+    B2: dict(ra=160, ka=160, rb=224, kb=224, one=256, ident=256, kp=96, kr=96, tq=144, tn=8, gn=160, cnt=160, own=32,
+             ta=64, tb=64, ga=129, gb=129, ca=129, cb=129, ua=128, va=128, vb=128, xa=128, cum=128, mm=160, mt=288, onc=130,
+             d0=146, wv=538, xal=16, xbl=16, sg=216, tk=32, ka1=128, kb1=128, ka2=128, kb2=128, ka3=128, kb3=128,
              win=288, wt1=544, key=128, win2=288, wt2=544, thr=96, hand1=2, land1=48, sc=40, tot=32, sa=112, sb=112,
-             fa=146, fb=146, w1=520, vl=34, jd=96, xt=520, wt=2048),
+             fa=146, fb=146, w1=520, vl=35, jd=192, xt=520, wt=2048),
     MX: dict(xq=130, wq=512, oq=288, pq=64, o2q=32, rq=136, lq=448, hq=160),
     U1: dict(xz=130, wz=512, oz=288, pz=64, o2z=32, rz=136, lz=448, hz=160),
 }
@@ -72,7 +72,7 @@ def hand_on(g, core, T, topo):
         rel = relays(T, topo, s)
         if core not in rel:
             continue
-        cross, _, late = roads(T, topo, s)
+        cross, direct, late = roads(T, topo, s)
         j = rel.index(core)
         codes, h = j < 2, j % 2
         us = [u for u in range(1, N) if u != late][3 * h:3 * h + 3]
@@ -92,15 +92,23 @@ def hand_on(g, core, T, topo):
         g.wait_ge(T.sem.i1, 4)
         g.remote_dma_fused([xfer(core, at(T, s, cross[j]), topo, es, T.sem.i1, T.hand1[:, 0:1], T.land1[:, c:c + 1])],
                            local_sem=T.sem.lo)
+        key = lambda i, u, e: xfer(core, at(T, s, u), topo, e, T.sem.i2, T.hand2[:, i:i + 1], T.lk[:, N - u - 1:N - u])
         if codes:
+            if h == 0:
+                g.wait_ge(T.sem.i2, 8)
+                g.remote_dma_fused([key(0, direct[0], es)], local_sem=T.sem.lo)
             g.wait_ge(T.sem.tc, 16)
             two_calls(T.sem.tc, lambda i, u: [v.bitcast(dt.uint8) for v in block(T.rq, T.lq, i, u)])
         else:
             g.wait_ge(T.sem.i2, 8)
-            two_calls(T.sem.i2, lambda i, u: (T.hand2[:, i:i + 1], T.lk[:, N - u - 1:N - u]))
+            far = [(i, u) for i, u in enumerate(us) if u in cross]
+            g.remote_dma_fused([key(i, u, share[n]) for n, (i, u) in enumerate(far)], local_sem=T.sem.lo)
             g.wait_ge(T.sem.ts, 8)
-            two_calls(T.sem.ts, lambda i, u: block(T.rz, T.lz, i, u))
-        g.wait_ge(T.sem.lo, 24 if codes else 40)
+            for i, u in enumerate(us):
+                if u in cross:
+                    g.remote_dma_fused([xfer(core, at(T, s, u), topo, es, T.sem.ts, *block(T.rz, T.lz, i, u))],
+                                       local_sem=T.sem.lo)
+        g.wait_ge(T.sem.lo, 24 if j == 1 else 32)
         return
 
 
@@ -169,7 +177,8 @@ def rank_program(g, core, T, topo):
             done(g.iota(out, pattern, base, 0, allow_small_or_imprecise_dtypes=True), step)
 
     def quant_w(o):
-        done(vec.quantize_mx(T.wq[:, 128 * o:128 * o + 128], T.wz[:, 128 * o:128 * o + 128], T.wt[:, 512 * o:512 * o + 512]), "wq")
+        done(vec.quantize_mx(T.wq[:, 128 * o:128 * o + 128], T.wz[:, 128 * o:128 * o + 128], T.wt[:, 512 * o:512 * o + 512]),
+             "wq%d" % (o // 3))
 
     V = lambda *n: need(QV, *n)
     S = lambda *n: need(QA, *n)
@@ -185,47 +194,44 @@ def rank_program(g, core, T, topo):
     done(syn.dma_start(T.wt[:, :], T.w[:, :]), "w", 16)
 
     iota("r0", T.r0[:, :], [[1, 8], [0, 4]], 0)
-    iota("k16", T.ra[:, 32:64], [[0, 2], [1, 8], [0, 2]], 0)
-    iota("ra", T.ra[:, 0:32], [[-1, 2], [1, 16]], 1)
+    iota("k16", T.ra[:, 32:64], [[1, 8], [32, 2], [0, 2]], 0)
+    iota("ra", T.ra[:, 64:96], [[1, 8], [-32, 2], [-32, 2]], 64)
     iota("yi", T.yi[:, :], [[32, 8], [1, 8]], 33 * (N - 1 - s), True)
-    iota("rb", T.rb[:, 0:16], [[0, 2], [16, 4], [24, 2]], 7)
-    iota("rb", T.rb[:, 16:32], [[-80, 2], [16, 4], [-8, 2]], 95)
+    iota("rb", T.rb[:, 128:160], [[0, 2], [1, 16]], 0)
+    iota("rb", T.rb[:, 0:16], [[0, 2], [8, 4], [40, 2]], 7)
+    iota("rb", T.rb[:, 16:32], [[0, 2], [16, 4], [-64, 2]], 151)
     iota("rb", T.rb[:, 32:48], [[0, 2], [32, 4], [-256, 2]], 432)
     iota("rb", T.rb[:, 48:64], [[0, 2], [32, 4], [288, 2]], 144)
     iota("rb", T.rb[:, 64:96], [[-288, 2], [0, 2], [32, 8]], 288)
     iota("rb", T.rb[:, 96:128], [[256, 2], [0, 2], [32, 8]], 32)
 
     fill("one", T.one[:, :], 1.0)
-    fill("ra", T.ra[:, 64:96:2], 1.0 / 32)
-    fill("ra", T.ra[:, 65:96:2], 1.0)
-    fill("ra", T.ra[:, 128:160:2], -999.0)
+    fill("ra", T.ra[:, 0:32:2], 1.0 / 32)
+    fill("ra", T.ra[:, 1:32:2], 1.0)
+    fill("ra", T.ra[:, 128:160:2], -1024.0 - MOVE)
     fill("ra", T.ra[:, 129:160:2], float(-MOVE))
-    fill("ra", T.ra[:, 97:128:16], float(127 + MOVE))
-    fill("ra", T.ra[:, 99:128:16], float(143 + MOVE))
+    fill("ra", T.ra[:, 98:128:4], 0.0)
     V("r0")
     fill("r0x", T.r0[:, 4 * g1 + 1:4 * g1 + 3], 99.0)
     fill("r0x", col(T.r0, 4 * g2 + 2), 99.0)
     V("k16", "one")
-    ts("ra", T.ra[:, 96:128:2], T.ra[:, 32:64:2], 32.0, -1.0, A.mult, A.add)
-    for h in range(2):
-        ts("ra", T.ra[:, 101 + 16 * h:112 + 16 * h:2], T.ra[:, 36:48:2], 16.0, 127.0, A.mult, A.add)
+    ts("ra", T.ra[:, 96:128:4], T.ra[:, 32:64:4], 32.0, -1.0, A.mult, A.add)
+    for t in (1, 3):
+        ts("ra", T.ra[:, 96 + t:128:4], T.ra[:, 32:64:4], 16.0, 143.0, A.mult, A.add)
     V("r0x")
     turn("k0", T.k0[:, :], T.r0[:, :])
     scan("ident", T.ident[:, :], T.one[:, :], T.one[:, :], -1.0, A.add, A.mult)
     V("ra")
     turn("ka", T.ka[:, :], T.ra[:, :])
-    fill("yr", T.yr[:, 64:80], 999)
     V("yi")
-    ts("yr", T.yr[:, 0:64], T.yi[:, :], 0xE7, None, A.bitwise_and)
+    ts("yr", T.yr[:, :], T.yi[:, :], 0xE7, None, A.bitwise_and)
     V("k0", "ident")
     ts("cu1", T.tn[:, :], T.ident[:, 0:8], col(T.k0, 0), None, A.is_equal)
-    SH, K, MUL, BASE, LIM = [col(T.ka, 32 * i) for i in range(5)]
-    fill("sh", T.cs[:, 0:10:9], 64)
-    V("ka", "yr")
-    ts("yc", T.yc[:, :], T.yr[:, :], MUL, WHOLE, A.mult, A.add)
-    ts("sh", T.sh[:, 0:1], SH, 9.0, None, A.min)
+    MUL, KO, KX, BASE, LIM = [col(T.ka, 32 * i) for i in range(5)]
     ts("cu1", T.tk[:, 0:16], T.ident[:, 0:16], float(g1), None, A.is_equal)
     ts("cu1", T.tk[:, 16:32], T.ident[:, 0:16], float(g2), None, A.is_equal)
+    V("ka", "yr")
+    ts("yc", T.yc[:, :], T.yr[:, :], MUL, WHOLE, A.mult, A.add)
 
     V("c1")
     cp("cu1", T.cu1[:, :], T.c1b[:, :])
@@ -233,17 +239,23 @@ def rank_program(g, core, T, topo):
     S("one")
     lin("gn", T.gn[:, 128:160], T.one[:, 0:32], 0.0)
     lin("kp1", T.kp[:, :], T.one[:, 0:96])
-    lin("kp1", T.tq[:, :], T.one[:, 0:80], 999.0)
+    lin("kp1", T.tq[:, :], T.one[:, 0:144], 999.0)
+    lin("last", T.onc[:, 0:128], T.one[:, 0:128])
     lin("z1", T.win[:, 0:256], T.one[:, :], 128.0)
+    S("ka")
+    lin("last", col(T.onc, 128), LIM, 1.0 / 1024, 1.0 + MOVE / 1024)
+    lin("last", col(T.ga, 128), LIM, 0.0)
+    lin("last", col(T.gb, 128), BASE, -1.0)
+    lin("last", col(T.onc, 129), BASE, 1.0, -MOVE)
     S("cu1")
     take("gn", T.gn[:, 0:128], T.tn[:, 0:8].indirect(T.cu1[:, 0:8]))
     V("yc")
-    ts("ta", T.ta[:, :], T.yc[:, :], -WHOLE, K, A.add, A.is_equal)
+    ts("ta", T.ta[:, :], T.yc[:, :], -WHOLE, KO, A.add, A.is_equal)
     V("c2", "cm")
-    tt("cs", T.cs[:, 1:9], T.cm[:, :], T.c2b[:, :], A.add)
-    ts("tb", T.tb[:, :], T.yc[:, :], -WHOLE - 32, K, A.add, A.is_equal)
-    V("cs", "sh")
-    cp("cu", T.cu[:, :], T.cs[:, 0:10].indirect(T.sh[:, 0:1]))
+    tt("cs", T.cs[:, :], T.cm[:, :], T.c2b[:, :], A.add)
+    ts("tb", T.tb[:, :], T.yc[:, :], -WHOLE, KX, A.add, A.is_equal)
+    V("cs")
+    cp("cu", T.cu[:, :], T.cs[:, :])
     V("gn")
     scan("cnt", T.cnt[:, :], T.gn[:, :], T.one[:, 0:160], 0.0, A.add, A.mult)
 
@@ -253,131 +265,133 @@ def rank_program(g, core, T, topo):
     G("cnt")
     quarter = [off[0:4], off[4:8], on[0:4], on[4:8]]
     g.remote_dma_fused([xfer(core, rel[j], topo, quarter[j], sem.i1, CNT, T.hand1[:, 0:1]) for j in range(4)], local_sem=sem.lo)
-    g.remote_dma_fused([xfer(core, at(T, s, u), topo, es, sem.i1, CNT, col(T.land1, 8 + N - u))
-                        for u, es in zip(direct, (off[0:2], off[2:4], off[4:8]))], local_sem=sem.lo)
+    tr = [xfer(core, at(T, s, u), topo, es, sem.i1, CNT, col(T.land1, 8 + N - u)) for u, es in zip(direct, quarter[0:2] + [off])]
+    g.remote_dma_fused(tr[0:2], local_sem=sem.lo)
+    g.remote_dma_fused(tr[2:3], local_sem=sem.lo)
     for v in (1, 2):
         a = (s + 1 + v) % N
         iota("slf", T.slf[:, 8 * v - 8:8 * v - a], [[4, N - a]], 4 * a + v)
         if a:
             iota("slf", T.slf[:, 8 * v - a:8 * v], [[4, a]], v)
-    iota("jd", T.jd[:, :], [[64, 3], [0, 2], [1, 16]], 0)
-    iota("d0i", T.d0i[:, :], [[B, 8], [1, 16]], B)
+    iota("jd", T.jd[:, 0:96], [[64, 3], [0, 2], [1, 16]], 0)
+    iota("d0i", T.d0i[:, 0:128], [[B, 8], [1, 16]], B)
 
     take("g1", T.ka1[:, :], T.tk[:, 0:16].indirect(T.cu1[:, 0:8]))
     S("cu", "ta")
-    take("ga", T.ga[:, :], T.ta[:, 0:80].indirect(T.cu[:, 0:9]))
+    take("ga", T.ga[:, 0:128], T.ta[:, 0:64].indirect(T.cu[:, 0:8]))
     take("g2", T.kb1[:, :], T.tk[:, 16:32].indirect(T.cu1[:, 0:8]))
-    S("ident", "ka")
-    lin("xt0", T.xt[:, 512:520], T.one[:, 0:8], 0.0)
-    lin("r15", fc(28), SH, -1.0, 127.0)
+    R16, BK, Q16 = [col(T.kb, 128 + 32 * i) for i in range(3)]
+    V("cu", "tb")
+    cp("gb", T.gb[:, 0:128], T.tb[:, 0:64].indirect(T.cu[:, 0:8]))
+    V("rb")
+    turn("kb", T.kb[:, 0:160], T.rb[:, 0:160])
+    S("ident", "kb")
+    lin("r15", fc(28), R16, -1.0, 127.0)
+    lin("mm", T.mm[:, 0:16], T.one[:, 0:16], 0.0)
     lin("mm", T.mm[:, 144:160], T.one[:, 0:16], 0.0)
+    lin("xt0", T.xt[:, 512:520], T.one[:, 0:8], 0.0)
     S("kp1", "r15")
     lin("kp", T.kp[:, 0:96:8], T.one[:, 0:12], 0.0)
-    shift("kp", T.tq[:, 0:80:8], T.ident[:, 0:160:16], -1.0, fc(28))
-    for h in range(2):
-        lin("thr1", T.rb[:, 160 + 16 * h:176 + 16 * h], T.ra[:, 32:64:2], B, B)
-        lin("rc", T.rb[:, 128 + 16 * h:144 + 16 * h], T.ident[:, 0:16])
-    lin("thr1", T.thr[:, :], T.one[:, 0:96], 255.0)
-    lin("thr1", T.kr[:, :], T.one[:, 0:96], 0.0)
-    for q in range(4):
-        lin("rc", T.rb[:, 192 + 8 * q:200 + 8 * q], T.one[:, 0:8], -16 * q)
-    S("thr1")
-    lin("rc", T.rb[:, 167:192:8], T.one[:, 0:4], 2048.0)
+    shift("kp", T.tq[:, 0:144:16], T.ident[:, 0:144:16], -1.0, fc(28))
     lin("z1", T.win[:, 256:288], T.one[:, 0:32], 128.0)
     lin("z1", T.win2[:, 128:288], T.one[:, 0:160], NOKEY)
+    for q in range(4):
+        lin("rc", T.rb[:, 160 + 8 * q:168 + 8 * q], T.ident[:, 0:8])
+        lin("rc", T.rb[:, 192 + 8 * q:200 + 8 * q], T.one[:, 0:8], 16 * q)
+    lin("thr1", T.thr[:, :], T.one[:, 0:96], 255.0)
+    lin("thr1", T.kr[:, :], T.one[:, 0:96], 0.0)
     lin("z4", T.wt2[:, 0:128], T.one[:, 0:128], 0.0)
     lin("z4", T.wt2[:, 288:416], T.one[:, 0:128], 0.0)
-    V("cu", "tb")
-    cp("gb", T.gb[:, :], T.tb[:, 0:80].indirect(T.cu[:, 0:9]))
-    V("rb")
-    turn("kb", T.kb[:, 0:128], T.rb[:, 0:128])
     V("cnt")
     turn("own", T.own[:, :], T.cnt[:, 128:160])
+    V("gb", "last")
+    scan("cb", T.cb[:, :], T.gb[:, :], T.one[:, 0:129], 0.0, A.add, A.mult)
     V("ga")
-    scan("ca", T.ca[:, :], T.ga[:, :], T.one[:, 0:144], 0.0, A.add, A.mult)
-    V("gb")
-    scan("cb", T.cb[:, :], T.gb[:, :], T.one[:, 0:144], 0.0, A.add, A.mult)
+    scan("ca", T.ca[:, :], T.ga[:, :], T.onc[:, 0:129], 0.0, A.add, A.mult)
     V("g1")
     scan("k1", T.ka2[:, :], T.ka1[:, :], T.one[:, 0:128], -1.0, A.add, A.mult)
-    V("ca")
-    ts("ua", T.ua[:, :], T.ca[:, :], col(T.ca, 143), LIM, A.subtract, A.is_gt)
     V("cb")
-    ts("ub", T.ub[:, :], T.cb[:, :], col(T.cb, 143), float(-MOVE), A.subtract, A.is_gt)
+    ts("va", T.vb[:, :], T.cb[:, 0:128], col(T.cb, 128), col(T.onc, 129), A.subtract, A.max)
+    V("ca")
+    ts("va", T.va[:, :], T.ca[:, 0:128], col(T.ca, 128), LIM, A.subtract, A.max)
+    ts("ua", T.ua[:, :], T.ca[:, 0:128], col(T.ca, 128), LIM, A.subtract, A.is_gt)
     V("g2")
     scan("k1", T.kb2[:, :], T.kb1[:, :], T.one[:, 0:128], 31.0, A.add, A.mult)
+    V("va")
+    tt("cum", T.cum[:, :], T.va[:, :], T.vb[:, :], A.add)
     V("ua")
-    mask("xa", T.xa[:, :], T.ua[:, :], T.ga[:, :])
-    V("ub")
-    mask("xb", T.xb[:, :], T.ub[:, :], T.gb[:, :])
-    V("x", "xt0")
-    done(vec.quantize_mx(T.xq[:, :], T.xz[:, :], T.xt[:, :]), "xq")
-    V("xa", "xb")
-    tt("cum", T.xs[:, :], T.xa[:, :], T.xb[:, :], A.add)
-    scan("cum", T.cum[:, :], T.xa[:, :], T.xb[:, :], BASE)
+    mask("cum", T.xa[:, :], T.ua[:, :], T.ga[:, 0:128])
     V("k1")
     mask("k2", T.ka3[:, :], T.ka2[:, :], T.ka1[:, :])
     mask("k2", T.kb3[:, :], T.kb2[:, :], T.kb1[:, :])
-    R16, BK, Q16 = [col(T.kb, 128 + 32 * i) for i in range(3)]
     V("cum")
-    mask("mm", T.mm[:, 0:144], T.cum[:, :], T.xs[:, :])
-    V("k2")
-    tt("key", T.key[:, :], T.ka3[:, :], T.kb3[:, :], A.add)
+    mask("mm", T.mm[:, 16:144], T.cum[:, :], T.xa[:, :])
+    V("x", "xt0")
+    done(vec.quantize_mx(T.xq[:, :], T.xz[:, :], T.xt[:, :]), "xq")
     V("mm")
-    turn("mt", T.mt[:, :], T.mm[:, :])
-    V("kb")
+    turn("mt", T.mt[:, 0:128], T.mm[:, 16:144])
+    turn("mt", T.mt[:, 128:288], T.mm[:, 0:160])
+    V("k2", "kb")
+    tt("key", T.key[:, :], T.ka3[:, :], T.kb3[:, :], A.add)
     cp("cl", T.cl[:, 0:8:2], T.kb[:, 0:97:32])
-    V("rc")
-    turn("own", T.kb[:, 128:224], T.rb[:, 128:224])
     V("mt", "kp")
-    scan("sg", T.sg[:, 80:160], T.tq[:, :], T.mt[:, 1:160:2], 999.0, A.min, A.max)
-    scan("sg", T.sg[:, 0:80], T.kp[:, 0:80], T.mt[:, 0:160:2], 0.0, A.mult, A.add)
+    scan("sg", T.sg[:, 72:216], T.tq[:, :], T.mt[:, 1:288:2], 999.0, A.min, A.max)
+    scan("sg", T.sg[:, 0:72], T.kp[:, 0:72], T.mt[:, 0:288:4], 0.0, A.mult, A.add)
     V("w")
     quant_w(0)
     V("sg", "cl")
-    cp("so", T.so[:, :], T.sg[:, 0:160].indirect(T.cl[:, 0:1]))
-    quant_w(1)
+    cp("so", T.so[:, :], T.sg[:, 0:216].indirect(T.cl[:, 0:1]))
+    V("rc")
+    turn("kc", T.kb[:, 160:224], T.rb[:, 160:224])
     V("so", "key", "z1")
     cp("win2", T.win2[:, 16:272].indirect(T.so[:, 0:8]), T.key[:, :])
     cp("win", T.win[:, 16:272].indirect(T.so[:, 0:8]), T.ident[:, 0:128])
     V("win2")
     turn("wt2", T.wt2[:, 128:288], T.win2[:, 128:288])
     turn("wt2", T.wt2[:, 416:544], T.win2[:, 144:272])
+    S("cnt", "own", "thr1")
+    shift("jm1", T.jm[:, :], T.ident[:, 0:160:16], 1.0, R16)
+    take("z2", col(T.sc, 0), CNT)
+    lin("z2", T.land1[:, 16:48], T.one[:, 0:32], 0.0)
+    lin("z2", T.thr[:, 32:32 + PAIR], T.ident[:, 0:PAIR], -1.0, CAP)
+    lin("slf", T.slf[:, 18:20], T.one[:, 0:2], N - late - 1)
+    lin("slf", T.slf[:, 20:22], T.one[:, 0:2], N - late)
+    S("kc")
+    take("slf", T.slf[:, 16:18], T.kb[:, 160:162])
     V("win")
     turn("wt1", T.wt1[:, 0:288], T.win[:, 0:288])
     V("wt2", "z4")
     cp("kq", T.kq[:, :], T.wt2[:, 0:544].indirect(T.cl[:, 2:3]))
     turn("wt1", T.wt1[:, 288:544], T.win[:, 16:272])
-    quant_w(2)
+    V("slf")
+    cp("sl", T.sl[:, :], T.slf[:, :])
+    V("kq")
+    cp("kl", T.kl[:, :], T.kq[:, late - 1:N:N - late])
     V("wt1")
     for t in range(3):
         cp("offp", T.offp[:, t:48:3], T.wt1[:, 0:544].indirect(T.cl[:, 2 * t + 2:2 * t + 3]))
-    quant_w(3)
-
-    S("cnt", "own")
-    shift("jm1", T.jm[:, :], T.ident[:, 0:160:16], 1.0, R16)
-    lin("slf", T.slf[:, 16:18], T.kb[:, 160:162], 1.0 / B, -1.0)
-    lin("slf", T.slf[:, 18:20], T.one[:, 0:2], N - late - 1)
-    lin("slf", T.slf[:, 20:22], T.one[:, 0:2], N - late)
-    take("z2", col(T.sc, 0), CNT)
-    lin("z2", T.land1[:, 16:48], T.one[:, 0:32], 0.0)
-    lin("z2", T.thr[:, 32:32 + PAIR], T.ident[:, 0:PAIR], -1.0, CAP)
+    quant_w(1)
     S("jm1")
     lin("p2", T.fc[:, 0:2], T.jm[:, 0:2], -1.0, -1.0)
-    lin("in1", T.dl[:, 0:18:17], T.jm[:, 0:2], -1.0 / 64)
-    lin("in1", T.dl[:, 1:17], T.ident[:, 48:64], -1.0 / 64)
-    lin("in1", T.dl[:, 18:34], T.ident[:, 48:64], -1.0 / 64)
+    lin("in1", T.dl[:, 0:19:18], T.jm[:, 0:2], -1.0 / 64)
+    lin("in1", T.dl[:, 1:18], T.ident[:, 48:65], -1.0 / 64)
+    lin("in1", T.dl[:, 19:35], T.ident[:, 48:64], -1.0 / 64)
+    lin("in1", col(T.vl, 17), col(T.one, 0), -1.0)
     S("p2")
-    shift("in1", T.vl[:, 0:18:17], T.fc[:, 0:2], 1.0, col(T.own, 4 * gl))
-    lin("z3", T.fc[:, 23:27], T.jm[:, 0:4], -1.0, 7.0)
-    lin("z3", fc(27), R16, -SC, (Z - B - 16) * SC)
-    lin("z3", fc(8), R16, 1.0, 12.0)
+    shift("in1", T.vl[:, 0:19:18], T.fc[:, 0:2], 1.0, col(T.own, 4 * gl))
+    lin("z3", fc(23), R16, -1.0, 7.0)
+    lin("z2", col(T.sd, 0), CNT, -1.0, B)
+    lin("z2", col(T.sd, 7), col(T.one, 0), 2048.0)
+    lin("z2", T.d0i[:, 128:136], T.one[:, 0:8], B)
+    lin("z3", fc(27), R16, -SC, (MID - B - 16) * SC)
+    lin("z3", fc(8), R16, 1.0, 16.0)
     lin("z3", fc(4), R16, -1.0, 4.0)
     lin("z3", fc(5), R16, -100.0)
     lin("z3", T.kr[:, 0:96:8], T.one[:, 0:12], -4096.0)
     lin("z3", T.kr[:, 7:72:8], T.ident[:, 0:9], 16.0)
     lin("z3", col(T.kr, 79), col(T.one, 0), 4096.0)
     S("d0i")
-    lin("z3", T.d0[:, 0:128], T.d0i[:, :], -SC, Z * SC)
+    lin("z3", T.d0[:, 0:128], T.d0i[:, 0:128], -SC, MID * SC)
 
     picks = dict(o0=(T.oq, T.oz, 0, 0, 9), o1=(T.oq, T.oz, 144, 12, 21), p0=(T.pq, T.pz, 0, 10, 12), p1=(T.pq, T.pz, 32, 8, 10),
                  l0=(T.lq, T.lz, B - 16, 20, 24), l1=(T.lq, T.lz, Z - 8, 2, 3))
@@ -390,131 +404,138 @@ def rank_program(g, core, T, topo):
         q, z, c, a, b = picks[nm]
         take(step, z[:, c:c + 16 * (b - a)], T.xz[:, 0:130].indirect(T.offp[:, a:b]))
 
-    S("offp", "xq")
-    scales("o0", "oz")
-    scales("o1", "oz")
-    lin("z3", col(T.d0, 128), col(T.one, 0), 0.0)
+    lin("z3", col(T.d0, 128), col(T.one, 0), (MID - Z) * SC)
     lin("z3", T.fa[:, 144:146], T.one[:, 0:2], 8192.0)
     lin("z3", T.fa[:, 128:144], T.one[:, 0:16], 0.0)
     lin("z3", T.fb[:, 144:146], T.one[:, 0:2], 0.0)
-    lin("z3", T.wv[:, 520:524], T.one[:, 0:4], 0.0)
+    lin("z3", T.wv[:, 520:528], T.one[:, 0:8], (MID - Z) * SC)
+    S("jd")
+    shift("jd2", T.jd[:, 96:192], T.jd[:, 0:96], 1.0, Q16)
+    S("offp", "xq")
+    scales("o0", "oz")
+    scales("o1", "oz")
     V("offp", "xq")
-    codes("o0", "o0q")
     codes("o1", "o1q")
+    codes("o0", "o0q")
 
     G("kq")
     g.remote_dma_fused([xfer(core, rel[2 + h], topo, (off, on)[h], sem.i2, T.kq[:, 4 * h:4 * h + 3], T.hand2[:, 0:3])
                         for h in range(2)], local_sem=sem.lo)
-    g.remote_dma_fused([xfer(core, at(T, s, late), topo, off, sem.il, col(T.kq, late - 1), col(T.lk, N - late - 1))],
-                       local_sem=sem.lo)
-    for h in range(2):
+    g.remote_dma_fused([xfer(core, at(T, s, late), topo, off[0:4], sem.il, col(T.kq, late - 1), col(T.lk, N - late - 1)),
+                        xfer(core, at(T, s, direct[2]), topo, off[4:8], sem.i2, col(T.kq, direct[2] - 1),
+                             col(T.lk, N - direct[2] - 1)),
+                        xfer(core, rel[0], topo, on, sem.i2, col(T.kq, direct[0] - 1), col(T.hand2, 0))], local_sem=sem.lo)
+    for h in (1, 0):
         G("o%dq" % h)
         g.remote_dma_fused([xfer(core, rel[h], topo, off + on, sem.tc, T.oq[:, 144 * h:144 * h + 136].bitcast(dt.uint8),
                                  T.rq[:, :].bitcast(dt.uint8))], local_sem=sem.lo)
     G("oz")
     g.remote_dma_fused([xfer(core, rel[2 + h], topo, (off, on)[h], sem.ts, T.oz[:, 144 * h:144 * h + 136], T.rz[:, :])
                         for h in range(2)], local_sem=sem.lo)
+    for u in direct:
+        if u != late:
+            a, c, w = B * (u - 1 - (u > late)) + skip(u), B * (N - u + 1) + skip(u), 16 + PAIR - skip(u)
+            g.remote_dma_fused([xfer(core, at(T, s, u), topo, off, sem.ts, T.oz[:, a:a + w], T.lz[:, c:c + w])],
+                               local_sem=sem.lo)
 
     n1 = 0
     for u in range(1, N):
         d = roads(T, topo, (s - u) % N)[1]
-        n1 += (2, 2, 4)[d.index(u)] if u in d else 8
+        n1 += (4, 4, 8)[d.index(u)] if u in d else 8
     tA = lambda k, a, b: T.thr[:, 32:96].indirect(k[:, a:b])
     tB = lambda k, a, b: T.thr[:, 0:64].indirect(k[:, a:b])
     c = B * (N - late + 1) + 16
-    PK = col(T.rpt, 4 * s)
-    V("z2", "slf", "kq")
-    ts("sl", T.sl[:, :], T.slf[:, :], 31.0, None, A.min)
+    V("z2")
     vec.wait_ge(sem.i1, n1)
     scan("sc", T.sc[:, 1:40], T.land1[:, 9:48], T.one[:, 0:39], CNT, A.add, A.mult)
-    cp("kl", T.kl[:, :], T.kq[:, late - 1:N:N - late])
+    scan("sd", T.sd[:, 1:7], T.d0i[:, 128:134], T.land1[:, 9:15], col(T.sd, 0), A.add, A.subtract)
     codes("p0", "pq")
     V("sc")
     turn("tot", T.tot[:, :], T.sc[:, 8:40])
     codes("p1", "pq")
-    vec.wait_ge(sem.il, 8)
-    cp("km", T.km[:, 0:1], col(T.lk, N - late - 1))
+    codes("l1", "lq")
+    scales("p0", "pz")
     S("sc", "sl")
-    take("rep", T.rep[:, :], T.sc[:, 0:32].indirect(T.sl[:, 16:22]))
+    take("rep", T.rep[:, 0:32], T.sc[:, 0:32].indirect(T.sl[:, 16:18]))
+    S("sd")
+    take("rep", T.rep[:, 32:64], T.sd[:, 0:8].indirect(T.sl[:, 16:18]))
+    take("rep2", T.rep[:, 64:128], T.sc[:, 0:32].indirect(T.sl[:, 18:22]))
     V("tot", "kl")
     ts("f0", T.fa[:, 0:32], tA(T.kl, 0, 2), col(T.tot, 4 * g1 + 1), None, A.is_le)
     ts("f0", T.fb[:, 0:32], tB(T.kl, 0, 2), col(T.tot, 4 * g2 + 2), None, A.is_le)
     ts("za", fc(12), col(T.tot, 4 * s), float(CAP), -7.5, A.min, A.add)
     V("rep")
-    turn("rpt", T.rpt[:, :], T.rep[:, :])
+    turn("rpt", T.rpt[:, 0:64], T.rep[:, 0:64])
     V("f0", "in1")
     for i in range(2):
-        scan("vl", T.vl[:, 17 * i + 1:17 * i + 17], T.fa[:, 0:16], T.fb[:, 0:16], col(T.vl, 17 * i))
-    V("km")
-    sl, k = (s + N - late) % N, N - late
-    ts("xl", T.xal[:, :], tA(T.km, 0, 1), col(T.tot, 4 * ((sl + 1) % N) + 1), -SC, A.is_le, A.mult)
-    ts("xl", T.xbl[:, :], tB(T.km, 0, 1), col(T.tot, 4 * ((sl + 2) % N) + 2), -SC, A.is_le, A.mult)
-    scales("p0", "pz")
-    scales("p1", "pz")
+        scan("vl", T.vl[:, 18 * i + 1:18 * i + 17], T.fa[:, 0:16], T.fb[:, 0:16], col(T.vl, 18 * i))
+    V("rpt", "jd2", "rep2")
+    ts("st", T.st[:, :], T.jd[:, 96:192], col(T.rpt, 4 * s), col(T.rpt, 32 + 4 * s), A.is_ge, A.mult)
+    turn("rpt2", T.rpt[:, 64:128], T.rep[:, 64:128])
     S("tot")
     take("sa", T.sa[:, :], T.tot[:, 0:32].indirect(T.sl[:, 0:7]))
-    S("za")
+    S("za", "z3")
     lin("zc", fc(21), fc(12), 1.0 / 16, WHOLE)
-    S("rpt")
-    shift("pd", fc(9), PK, -1.0, BK)
-    shift("pd", fc(10), PK, 1.0, Q16)
-    lin("nl", fc(11), col(T.rpt, 32 + 4 * s), SC, (Z - c + 1) * SC)
+    shift("zc", fc(22), fc(12), 1.0, fc(23))
+    take("sa", T.sb[:, :], T.tot[:, 0:32].indirect(T.sl[:, 8:15]))
     S("zc")
     lin("zf", fc(19), fc(21), 1.0, -WHOLE)
-    S("nl")
-    shift("nl2", fc(14), col(T.rpt, 64 + 4 * s), -SC, fc(11))
-    take("sa", T.sb[:, :], T.tot[:, 0:32].indirect(T.sl[:, 8:15]))
+    S("rpt2")
+    lin("nl", fc(11), col(T.rpt, 64 + 4 * s), SC, (MID - c + 1) * SC)
+    scales("p1", "pz")
+    S("zf")
+    shift("in2", fc(6), fc(19), -16.0, fc(22))
+    shift("u1", fc(29), fc(19), 1.0, fc(4), F.Relu)
+    shift("u1", fc(30), fc(19), 100.0, fc(5), F.Relu)
     V("vl")
-    for i in range(2):
-        scan("wl", T.wl[:, 17 * i:17 * i + 17], T.dl[:, 17 * i:17 * i + 17], T.vl[:, 17 * i:17 * i + 17], -1.0, A.max, A.min)
-    codes("l1", "lq")
-    V("pd", "jd")
-    ts("st", T.st[:, :], T.jd[:, :], fc(10), fc(9), A.is_ge, A.mult)
-    V("wl")
-    ts("offl", T.offl[:, :], T.wl[:, 16:34:17], -64.0, 63.0, A.mult, A.min)
-    V("zf")
-    ts("c0", T.cf[:, 0:1], fc(19), 4.0, None, A.add)
+    scan("wl", T.wl[:, :], T.dl[:, :], T.vl[:, :], -1.0, A.max, A.min)
+    sl, k = (s + N - late) % N, N - late
+    vec.wait_ge(sem.il, 4)
+    cp("km", T.km[:, 0:1], col(T.lk, N - late - 1))
     V("st")
     turn("stt", T.stt[:, :], T.st[:, :])
+    V("wl")
+    ts("offl", T.offl[:, :], T.wl[:, 16:35:18], -64.0, 63.0, A.mult, A.min)
+    V("km")
+    ts("xl", T.xal[:, :], tA(T.km, 0, 1), col(T.tot, 4 * ((sl + 1) % N) + 1), -SC, A.is_le, A.mult)
+    V("stt", "z3")
+    scan("sw", T.sw[:, :], T.kr[:, :], T.stt[:, :], 0.0, A.add, A.max)
     V("offl", "pq")
     cp("o2q", T.o2q[:, :].bitcast(U32), T.pq[:, 0:64].bitcast(U32).indirect(T.offl[:, 0:2]))
 
-    S("zf", "z3")
-    shift("ze", fc(22), fc(19), -16.0, fc(12))
     S("offl", "pz")
     take("o2z", T.o2z[:, :], T.pz[:, 0:64].indirect(T.offl[:, 0:2]))
-    S("ze")
-    shift("in2", fc(6), fc(23), 1.0, fc(22))
-    shift("ini", T.fc[:, 16:19], T.fc[:, 24:27], 1.0, fc(22))
-    shift("u1", fc(29), fc(19), 1.0, fc(4), F.Relu)
-    S("in2")
+    S("nl", "in2")
+    shift("nl2", fc(14), col(T.rpt, 96 + 4 * s), -SC, fc(11))
     done(act.activation(fc(7), fc(6), F.Relu, scale=400.0), "in3")
-    shift("u1", fc(30), fc(19), 100.0, fc(5), F.Relu)
-    S("in3")
-    shift("in0", fc(15), fc(7), -1.0, fc(6))
     S("u1")
     shift("u2", fc(31), fc(29), -1.0, fc(30))
+    shift("ini", T.fc[:, 16:19], T.ident[:, 16:49:16], -1.0, fc(6))
+    S("in3", "sw")
+    shift("in0", fc(15), fc(7), -1.0, fc(6))
+    shift("mf", T.wv[:, 528:538], T.sw[:, 7:80:8], -SC, fc(27))
+
+    vec.wait_ge(sem.i2, 28)
+    V("sa")
+    tt("f1", T.fa[:, 32:128], tA(T.lk, 0, 6), T.sa[:, 0:96], A.is_le)
+    ts("xl", T.xbl[:, :], tB(T.km, 0, 1), col(T.tot, 4 * ((sl + 2) % N) + 2), -SC, A.is_le, A.mult)
+    tt("f1", T.fb[:, 32:144], tB(T.lk, 0, 7), T.sb[:, :], A.is_le)
+    V("xl", "nl2", "zf", "u2")
+    ts("c0", T.cf[:, 0:1], fc(19), 8.0, 7.0, A.mult, A.add)
+    scan("d0l", T.d0[:, 16 * k:16 * k + 16], T.xal[:, :], T.xbl[:, :], fc(14))
+    ts("wv", T.cf[:, 2:3], fc(31), 8.0, fc(8), A.add, A.min)
+    scales("l0", "lz")
+    S("c0")
+    shift("fv", T.d0[:, 129:145], T.sw[:, 0:96].indirect(T.cf[:, 0:1]), -SC, fc(27))
 
     G("o2q")
     g.remote_dma_fused([xfer(core, at(T, s, late), topo, off, sem.tc, T.o2q[:, 0:BOTH].bitcast(dt.uint8),
                              T.lq[:, c:c + BOTH].bitcast(dt.uint8))], local_sem=sem.lo)
     G("o2z")
     g.remote_dma_fused([xfer(core, at(T, s, late), topo, off, sem.ts, T.o2z[:, 0:BOTH], T.lz[:, c:c + BOTH])], local_sem=sem.lo)
-    g.wait_ge(sem.lo, 24 + 24 + 32 + 16 + 16)
+    g.wait_ge(sem.lo, 32 + 32 + 32 + 32 + 16)
 
-    vec.wait_ge(sem.i2, 32)
-    V("sa")
-    tt("f1", T.fa[:, 32:128], tA(T.lk, 0, 6), T.sa[:, 0:96], A.is_le)
-    tt("f1", T.fb[:, 32:144], tB(T.lk, 0, 7), T.sb[:, :], A.is_le)
-    V("stt", "xl", "nl2", "z3")
-    scan("sw", T.sw[:, :], T.kr[:, :], T.stt[:, :], 0.0, A.add, A.max)
-    scan("d0l", T.d0[:, 16 * k:16 * k + 16], T.xal[:, :], T.xbl[:, :], fc(14))
-    S("sw")
-    shift("mf", T.wv[:, 524:534], T.sw[:, 7:80:8], -SC, fc(27), F.Relu)
     scales("l1", "lz")
-    S("mf", "c0")
-    take("fv", T.d0[:, 129:145], T.wv[:, 520:534].indirect(T.cf[:, 0:1]))
-    scales("l0", "lz")
     V("f1", "ini")
     for m in (1, 2, 3, 0):
         V("ini" if m else "in0")
@@ -525,21 +546,23 @@ def rank_program(g, core, T, topo):
         if m:
             scan("wv", T.wv[:, 4 + m:520:4], T.d0[:, 0:129], T.w1[:, 130 * m:130 * m + 129], -1.0, A.max, A.min)
         else:
-            V("u2", "fv")
-            ts("wv", T.cf[:, 2:3], fc(31), 8.0, fc(8), A.add, A.min)
+            V("fv")
             scan("wv", T.wv[:, 0:520:4], T.d0[:, 0:130], T.w1[:, 0:130], -1.0, A.max, A.min)
     codes("l0", "lq")
-    V("wv")
-    ts("offh", T.offh[:, :], T.wv[:, 512:534].indirect(T.cf[:, 2:3]), -1024.0, float(Z), A.mult, A.add)
+    V("wv", "mf")
+    ts("offh", T.offh[:, :], T.wv[:, 512:538].indirect(T.cf[:, 2:3]), -1024.0, float(MID), A.mult, A.add)
+    quant_w(2)
 
     S("offh", "lz")
-    act.wait_ge(sem.ts, 40)
+    act.wait_ge(sem.ts, 56)
     take("hz", T.hz[:, :], T.lz[:, 0:Z + 8].indirect(T.offh[:, 0:10]))
     V("offh", "lq")
     vec.wait_ge(sem.tc, 40)
     cp("hq", T.hq[:, :].bitcast(U32), T.lq[:, 0:Z + 8].bitcast(U32).indirect(T.offh[:, 0:10]))
-    need(QT, "wq", "hq", "hz")
+    quant_w(3)
+    need(QT, "hq", "hz")
     for o in range(O):
+        need(QT, "wq%d" % (o // 3))
         done(ten.matmul_mx(T.ps[:, 512 * o:512 * o + ROOM], T.wq[:, 128 * o:128 * o + 128], T.wz[:, 128 * o:128 * o + 128],
                            T.hq[:, 0:ROOM], T.hz[:, 0:ROOM], True, True), "t%d" % o)
     for o in range(O):

import numpy as np
from concourse.bass import DstId, RemoteDMATransfer
from concourse.mybir import dt, AluOpType, AxisListType, ActivationFunctionType

N = 8
CAP, ROOM, O = 144, 160, 4
PAIR, MOVE, BOTH = 24, 8, 30
B = 48
Z = B * (N + 1) + 8
NOKEY = 24.0
SC, MID = 1.0 / 1024, 236
WHOLE = 1.5 * 2 ** 23

F4, B2, I4, U2, MX, U1 = "float32", "bfloat16", "int32", "uint16", "float8_e4m3fn_x4", "uint8"
SIZES = {
    I4: dict(c1b=8, c2b=8, cm=8, cs=8, yi=64, yr=64),
    U2: dict(cu1=8, cu=8, cl=8, so=16, offp=48, kq=16, kl=2, km=2, cf=4, lk=8, hand2=4, sl=22, offl=2, offh=16),
    F4: dict(r0=32, k0=32, yc=64, fc=32, d0i=136, slf=22, jm=10, st=96, stt=96, sw=96,
             ys=640, dl=35, wl=35, rep=128, rpt=128, sd=8),
    B2: dict(ra=160, ka=160, rb=224, kb=224, one=256, ident=256, kp=96, kr=96, tq=144, tn=8, gn=160, cnt=160, own=32,
             ta=64, tb=64, ga=129, gb=129, ca=129, cb=129, ua=128, va=128, vb=128, xa=128, cum=128, mm=160, mt=288, onc=130,
             d0=146, wv=538, xal=16, xbl=16, sg=216, tk=32, ka1=128, kb1=128, ka2=128, kb2=128, ka3=128, kb3=128,
             win=288, wt1=544, key=128, win2=288, wt2=544, thr=96, hand1=2, land1=48, sc=40, tot=32, sa=112, sb=112,
             fa=146, fb=146, w1=520, vl=35, jd=192, xt=520, wt=2048),
    MX: dict(xq=130, wq=512, oq=288, pq=64, o2q=32, rq=136, lq=448, hq=160),
    U1: dict(xz=130, wz=512, oz=288, pz=64, o2z=32, rz=136, lz=448, hz=160),
}
SCRATCH = {"ps": ("psum", [128, 2048], F4)}
for _d in SIZES:
    for _n in SIZES[_d]:
        SCRATCH[_n] = ("sbuf", [128, SIZES[_d][_n]], _d)
SEMAPHORES = ["i1", "i2", "il", "tc", "ts", "lo"] + ["s%d" % _i for _i in range(140)]


def bits(es):
    m = 0
    for e in es:
        m |= 1 << e
    return m


def at(T, s, u):
    return T.cores[(s + u) % N]


def roads(T, topo, s):
    cross = [u for u in range(1, N) if not topo.may_write(T.cores[s], at(T, s, u))]
    direct = [u for u in range(1, N) if u not in cross]
    return cross, direct, [u for u in direct if u > 2][0]


def relays(T, topo, s):
    me = T.cores[s]
    r = [c for c in topo.cores_of(me) if c != me and T.rank_of(c) is None
         and all(topo.may_write(c, at(T, s, u)) for u in range(1, N))]
    near = [c for c in r if topo.die(c) == topo.die(me)]
    far = [c for c in r if topo.die(c) != topo.die(me)]
    return [far[0], near[0], near[1], far[1]]


def xfer(core, d, topo, es, sem, src, dst):
    rid, pid = topo.addr(d, core)
    return RemoteDMATransfer(dst_ids=[DstId(rid=rid, pnc=pid)], dma_engine_mask=bits(es), remote_sem=sem, src=src, dst=dst)


def skip(u):
    return MOVE if u <= 2 else 0


def hand_on(g, core, T, topo):
    for s in range(N):
        rel = relays(T, topo, s)
        if core not in rel:
            continue
        cross, direct, late = roads(T, topo, s)
        j = rel.index(core)
        codes, h = j < 2, j % 2
        us = [u for u in range(1, N) if u != late][3 * h:3 * h + 3]
        es = topo.engines(core, at(T, s, us[0]))
        share = [es[0:4], es[4:8], es]

        def two_calls(sem, piece):
            tr = [xfer(core, at(T, s, u), topo, share[i], sem, *piece(i, u)) for i, u in enumerate(us)]
            g.remote_dma_fused(tr[0:2], local_sem=T.sem.lo)
            g.remote_dma_fused(tr[2:3], local_sem=T.sem.lo)

        def block(a, b, i, u):
            c, w = B * (N - u + 1) + skip(u), 16 + PAIR - skip(u)
            return a[:, B * i + skip(u):B * i + skip(u) + w], b[:, c:c + w]

        c = 8 + N - cross[j]
        g.wait_ge(T.sem.i1, 4)
        g.remote_dma_fused([xfer(core, at(T, s, cross[j]), topo, es, T.sem.i1, T.hand1[:, 0:1], T.land1[:, c:c + 1])],
                           local_sem=T.sem.lo)
        key = lambda i, u, e: xfer(core, at(T, s, u), topo, e, T.sem.i2, T.hand2[:, i:i + 1], T.lk[:, N - u - 1:N - u])
        if codes:
            if h == 0:
                g.wait_ge(T.sem.i2, 8)
                g.remote_dma_fused([key(0, direct[0], es)], local_sem=T.sem.lo)
            g.wait_ge(T.sem.tc, 16)
            two_calls(T.sem.tc, lambda i, u: [v.bitcast(dt.uint8) for v in block(T.rq, T.lq, i, u)])
        else:
            g.wait_ge(T.sem.i2, 8)
            far = [(i, u) for i, u in enumerate(us) if u in cross]
            g.remote_dma_fused([key(i, u, share[n]) for n, (i, u) in enumerate(far)], local_sem=T.sem.lo)
            g.wait_ge(T.sem.ts, 8)
            for i, u in enumerate(us):
                if u in cross:
                    g.remote_dma_fused([xfer(core, at(T, s, u), topo, es, T.sem.ts, *block(T.rz, T.lz, i, u))],
                                       local_sem=T.sem.lo)
        g.wait_ge(T.sem.lo, 24 if j == 1 else 32)
        return


def rank_program(g, core, T, topo):
    s = T.rank_of(core)
    if s is None:
        hand_on(g, core, T, topo)
        return
    A, F = AluOpType, ActivationFunctionType
    sem = T.sem
    vec, act, ten, syn = g.vector, g.scalar, g.tensor, g.sync
    cross, direct, late = roads(T, topo, s)
    rel = relays(T, topo, s)
    U32 = dt.uint32

    steps, seen = {}, set()

    def done(ins, step, n=1):
        if step not in steps:
            steps[step] = [sem["s%d" % len(steps)], 0]
        steps[step][1] += n
        ins.then_inc(steps[step][0], n)

    def need(q, *names):
        for nm in names:
            if (q[0], nm) not in seen:
                seen.add((q[0], nm))
                q[1].wait_ge(steps[nm][0], steps[nm][1])

    QV, QA, QG, QT, QS = ("v", vec), ("a", act), ("g", g), ("t", ten), ("s", syn)

    def ts(step, out, in0, a, b, op0, op1=None):
        done(vec.tensor_scalar(out, in0, a, None, op0) if op1 is None else vec.tensor_scalar(out, in0, a, b, op0, op1), step)

    def tt(step, out, a, b, op):
        done(vec.tensor_tensor(out, a, b, op), step)

    def cp(step, out, a):
        done(vec.tensor_copy(out, a), step)

    def fill(step, out, c):
        done(vec.memset(out, c), step)

    def scan(step, out, a, b, ini, op0=A.add, op1=A.add):
        done(vec.tensor_tensor_scan(out, a, b, ini, op0, op1), step)

    def mask(step, out, rising, flags):
        scan(step, out, rising, flags, 0.0, A.max, A.mult)

    def turn(step, out, a):
        done(vec.transpose(out, a), step)

    def lin(step, out, a, scale=1.0, bias=0.0):
        done(act.activation(out, a, F.Copy, bias=float(bias), scale=float(scale)), step)

    def shift(step, out, a, scale, bias, f=F.Identity):
        done(act.activation(out, a, f, bias=bias, scale=float(scale)), step)

    def take(step, out, a):
        done(act.activation(out, a, F.Copy), step)

    def iota(step, out, pattern, base, whole=False):
        if whole:
            done(g.iota(out, pattern, base, 0), step)
        else:
            done(g.iota(out, pattern, base, 0, allow_small_or_imprecise_dtypes=True), step)

    def quant_w(o):
        done(vec.quantize_mx(T.wq[:, 128 * o:128 * o + 128], T.wz[:, 128 * o:128 * o + 128], T.wt[:, 512 * o:512 * o + 512]),
             "wq%d" % (o // 3))

    V = lambda *n: need(QV, *n)
    S = lambda *n: need(QA, *n)
    G = lambda *n: need(QG, *n)
    col = lambda t, i: t[:, i:i + 1]
    fc = lambda i: col(T.fc, i)
    g1, g2, gl = (s + 1) % N, (s + 2) % N, (s + late) % N

    for big, src, nm in ((T.c1b, T.c1, "c1"), (T.c2b, T.c2, "c2")):
        for q in range(8):
            done((syn if q % 2 else act).dma_start(big[16 * q:16 * q + 16, :], src[:, :]), nm, 16)
    done(syn.dma_start(T.xt[:, 0:512], T.x[:, :]), "x", 16)
    done(syn.dma_start(T.wt[:, :], T.w[:, :]), "w", 16)

    iota("r0", T.r0[:, :], [[1, 8], [0, 4]], 0)
    iota("k16", T.ra[:, 32:64], [[1, 8], [32, 2], [0, 2]], 0)
    iota("ra", T.ra[:, 64:96], [[1, 8], [-32, 2], [-32, 2]], 64)
    iota("yi", T.yi[:, :], [[32, 8], [1, 8]], 33 * (N - 1 - s), True)
    iota("rb", T.rb[:, 128:160], [[0, 2], [1, 16]], 0)
    iota("rb", T.rb[:, 0:16], [[0, 2], [8, 4], [40, 2]], 7)
    iota("rb", T.rb[:, 16:32], [[0, 2], [16, 4], [-64, 2]], 151)
    iota("rb", T.rb[:, 32:48], [[0, 2], [32, 4], [-256, 2]], 432)
    iota("rb", T.rb[:, 48:64], [[0, 2], [32, 4], [288, 2]], 144)
    iota("rb", T.rb[:, 64:96], [[-288, 2], [0, 2], [32, 8]], 288)
    iota("rb", T.rb[:, 96:128], [[256, 2], [0, 2], [32, 8]], 32)

    fill("one", T.one[:, :], 1.0)
    fill("ra", T.ra[:, 0:32:2], 1.0 / 32)
    fill("ra", T.ra[:, 1:32:2], 1.0)
    fill("ra", T.ra[:, 128:160:2], -1024.0 - MOVE)
    fill("ra", T.ra[:, 129:160:2], float(-MOVE))
    fill("ra", T.ra[:, 98:128:4], 0.0)
    V("r0")
    fill("r0x", T.r0[:, 4 * g1 + 1:4 * g1 + 3], 99.0)
    fill("r0x", col(T.r0, 4 * g2 + 2), 99.0)
    V("k16", "one")
    ts("ra", T.ra[:, 96:128:4], T.ra[:, 32:64:4], 32.0, -1.0, A.mult, A.add)
    for t in (1, 3):
        ts("ra", T.ra[:, 96 + t:128:4], T.ra[:, 32:64:4], 16.0, 143.0, A.mult, A.add)
    V("r0x")
    turn("k0", T.k0[:, :], T.r0[:, :])
    scan("ident", T.ident[:, :], T.one[:, :], T.one[:, :], -1.0, A.add, A.mult)
    V("ra")
    turn("ka", T.ka[:, :], T.ra[:, :])
    V("yi")
    ts("yr", T.yr[:, :], T.yi[:, :], 0xE7, None, A.bitwise_and)
    V("k0", "ident")
    ts("cu1", T.tn[:, :], T.ident[:, 0:8], col(T.k0, 0), None, A.is_equal)
    MUL, KO, KX, BASE, LIM = [col(T.ka, 32 * i) for i in range(5)]
    ts("cu1", T.tk[:, 0:16], T.ident[:, 0:16], float(g1), None, A.is_equal)
    ts("cu1", T.tk[:, 16:32], T.ident[:, 0:16], float(g2), None, A.is_equal)
    V("ka", "yr")
    ts("yc", T.yc[:, :], T.yr[:, :], MUL, WHOLE, A.mult, A.add)

    V("c1")
    cp("cu1", T.cu1[:, :], T.c1b[:, :])
    ts("cm", T.cm[:, :], T.c1b[:, :], 8, None, A.mult)
    S("one")
    lin("gn", T.gn[:, 128:160], T.one[:, 0:32], 0.0)
    lin("kp1", T.kp[:, :], T.one[:, 0:96])
    lin("kp1", T.tq[:, :], T.one[:, 0:144], 999.0)
    lin("last", T.onc[:, 0:128], T.one[:, 0:128])
    lin("z1", T.win[:, 0:256], T.one[:, :], 128.0)
    S("ka")
    lin("last", col(T.onc, 128), LIM, 1.0 / 1024, 1.0 + MOVE / 1024)
    lin("last", col(T.ga, 128), LIM, 0.0)
    lin("last", col(T.gb, 128), BASE, -1.0)
    lin("last", col(T.onc, 129), BASE, 1.0, -MOVE)
    S("cu1")
    take("gn", T.gn[:, 0:128], T.tn[:, 0:8].indirect(T.cu1[:, 0:8]))
    V("yc")
    ts("ta", T.ta[:, :], T.yc[:, :], -WHOLE, KO, A.add, A.is_equal)
    V("c2", "cm")
    tt("cs", T.cs[:, :], T.cm[:, :], T.c2b[:, :], A.add)
    ts("tb", T.tb[:, :], T.yc[:, :], -WHOLE, KX, A.add, A.is_equal)
    V("cs")
    cp("cu", T.cu[:, :], T.cs[:, :])
    V("gn")
    scan("cnt", T.cnt[:, :], T.gn[:, :], T.one[:, 0:160], 0.0, A.add, A.mult)

    off = topo.engines(core, at(T, s, late))
    on = [e for e in topo.engines(core, rel[0]) if e not in off]
    CNT = col(T.cnt, 127)
    G("cnt")
    quarter = [off[0:4], off[4:8], on[0:4], on[4:8]]
    g.remote_dma_fused([xfer(core, rel[j], topo, quarter[j], sem.i1, CNT, T.hand1[:, 0:1]) for j in range(4)], local_sem=sem.lo)
    tr = [xfer(core, at(T, s, u), topo, es, sem.i1, CNT, col(T.land1, 8 + N - u)) for u, es in zip(direct, quarter[0:2] + [off])]
    g.remote_dma_fused(tr[0:2], local_sem=sem.lo)
    g.remote_dma_fused(tr[2:3], local_sem=sem.lo)
    for v in (1, 2):
        a = (s + 1 + v) % N
        iota("slf", T.slf[:, 8 * v - 8:8 * v - a], [[4, N - a]], 4 * a + v)
        if a:
            iota("slf", T.slf[:, 8 * v - a:8 * v], [[4, a]], v)
    iota("jd", T.jd[:, 0:96], [[64, 3], [0, 2], [1, 16]], 0)
    iota("d0i", T.d0i[:, 0:128], [[B, 8], [1, 16]], B)

    take("g1", T.ka1[:, :], T.tk[:, 0:16].indirect(T.cu1[:, 0:8]))
    S("cu", "ta")
    take("ga", T.ga[:, 0:128], T.ta[:, 0:64].indirect(T.cu[:, 0:8]))
    take("g2", T.kb1[:, :], T.tk[:, 16:32].indirect(T.cu1[:, 0:8]))
    R16, BK, Q16 = [col(T.kb, 128 + 32 * i) for i in range(3)]
    V("cu", "tb")
    cp("gb", T.gb[:, 0:128], T.tb[:, 0:64].indirect(T.cu[:, 0:8]))
    V("rb")
    turn("kb", T.kb[:, 0:160], T.rb[:, 0:160])
    S("ident", "kb")
    lin("r15", fc(28), R16, -1.0, 127.0)
    lin("mm", T.mm[:, 0:16], T.one[:, 0:16], 0.0)
    lin("mm", T.mm[:, 144:160], T.one[:, 0:16], 0.0)
    lin("xt0", T.xt[:, 512:520], T.one[:, 0:8], 0.0)
    S("kp1", "r15")
    lin("kp", T.kp[:, 0:96:8], T.one[:, 0:12], 0.0)
    shift("kp", T.tq[:, 0:144:16], T.ident[:, 0:144:16], -1.0, fc(28))
    lin("z1", T.win[:, 256:288], T.one[:, 0:32], 128.0)
    lin("z1", T.win2[:, 128:288], T.one[:, 0:160], NOKEY)
    for q in range(4):
        lin("rc", T.rb[:, 160 + 8 * q:168 + 8 * q], T.ident[:, 0:8])
        lin("rc", T.rb[:, 192 + 8 * q:200 + 8 * q], T.one[:, 0:8], 16 * q)
    lin("thr1", T.thr[:, :], T.one[:, 0:96], 255.0)
    lin("thr1", T.kr[:, :], T.one[:, 0:96], 0.0)
    lin("z4", T.wt2[:, 0:128], T.one[:, 0:128], 0.0)
    lin("z4", T.wt2[:, 288:416], T.one[:, 0:128], 0.0)
    V("cnt")
    turn("own", T.own[:, :], T.cnt[:, 128:160])
    V("gb", "last")
    scan("cb", T.cb[:, :], T.gb[:, :], T.one[:, 0:129], 0.0, A.add, A.mult)
    V("ga")
    scan("ca", T.ca[:, :], T.ga[:, :], T.onc[:, 0:129], 0.0, A.add, A.mult)
    V("g1")
    scan("k1", T.ka2[:, :], T.ka1[:, :], T.one[:, 0:128], -1.0, A.add, A.mult)
    V("cb")
    ts("va", T.vb[:, :], T.cb[:, 0:128], col(T.cb, 128), col(T.onc, 129), A.subtract, A.max)
    V("ca")
    ts("va", T.va[:, :], T.ca[:, 0:128], col(T.ca, 128), LIM, A.subtract, A.max)
    ts("ua", T.ua[:, :], T.ca[:, 0:128], col(T.ca, 128), LIM, A.subtract, A.is_gt)
    V("g2")
    scan("k1", T.kb2[:, :], T.kb1[:, :], T.one[:, 0:128], 31.0, A.add, A.mult)
    V("va")
    tt("cum", T.cum[:, :], T.va[:, :], T.vb[:, :], A.add)
    V("ua")
    mask("cum", T.xa[:, :], T.ua[:, :], T.ga[:, 0:128])
    V("k1")
    mask("k2", T.ka3[:, :], T.ka2[:, :], T.ka1[:, :])
    mask("k2", T.kb3[:, :], T.kb2[:, :], T.kb1[:, :])
    V("cum")
    mask("mm", T.mm[:, 16:144], T.cum[:, :], T.xa[:, :])
    V("x", "xt0")
    done(vec.quantize_mx(T.xq[:, :], T.xz[:, :], T.xt[:, :]), "xq")
    V("mm")
    turn("mt", T.mt[:, 0:128], T.mm[:, 16:144])
    turn("mt", T.mt[:, 128:288], T.mm[:, 0:160])
    V("k2", "kb")
    tt("key", T.key[:, :], T.ka3[:, :], T.kb3[:, :], A.add)
    cp("cl", T.cl[:, 0:8:2], T.kb[:, 0:97:32])
    V("mt", "kp")
    scan("sg", T.sg[:, 72:216], T.tq[:, :], T.mt[:, 1:288:2], 999.0, A.min, A.max)
    scan("sg", T.sg[:, 0:72], T.kp[:, 0:72], T.mt[:, 0:288:4], 0.0, A.mult, A.add)
    V("w")
    quant_w(0)
    V("sg", "cl")
    cp("so", T.so[:, :], T.sg[:, 0:216].indirect(T.cl[:, 0:1]))
    V("rc")
    turn("kc", T.kb[:, 160:224], T.rb[:, 160:224])
    V("so", "key", "z1")
    cp("win2", T.win2[:, 16:272].indirect(T.so[:, 0:8]), T.key[:, :])
    cp("win", T.win[:, 16:272].indirect(T.so[:, 0:8]), T.ident[:, 0:128])
    V("win2")
    turn("wt2", T.wt2[:, 128:288], T.win2[:, 128:288])
    turn("wt2", T.wt2[:, 416:544], T.win2[:, 144:272])
    S("cnt", "own", "thr1")
    shift("jm1", T.jm[:, :], T.ident[:, 0:160:16], 1.0, R16)
    take("z2", col(T.sc, 0), CNT)
    lin("z2", T.land1[:, 16:48], T.one[:, 0:32], 0.0)
    lin("z2", T.thr[:, 32:32 + PAIR], T.ident[:, 0:PAIR], -1.0, CAP)
    lin("slf", T.slf[:, 18:20], T.one[:, 0:2], N - late - 1)
    lin("slf", T.slf[:, 20:22], T.one[:, 0:2], N - late)
    S("kc")
    take("slf", T.slf[:, 16:18], T.kb[:, 160:162])
    V("win")
    turn("wt1", T.wt1[:, 0:288], T.win[:, 0:288])
    V("wt2", "z4")
    cp("kq", T.kq[:, :], T.wt2[:, 0:544].indirect(T.cl[:, 2:3]))
    turn("wt1", T.wt1[:, 288:544], T.win[:, 16:272])
    V("slf")
    cp("sl", T.sl[:, :], T.slf[:, :])
    V("kq")
    cp("kl", T.kl[:, :], T.kq[:, late - 1:N:N - late])
    V("wt1")
    for t in range(3):
        cp("offp", T.offp[:, t:48:3], T.wt1[:, 0:544].indirect(T.cl[:, 2 * t + 2:2 * t + 3]))
    quant_w(1)
    S("jm1")
    lin("p2", T.fc[:, 0:2], T.jm[:, 0:2], -1.0, -1.0)
    lin("in1", T.dl[:, 0:19:18], T.jm[:, 0:2], -1.0 / 64)
    lin("in1", T.dl[:, 1:18], T.ident[:, 48:65], -1.0 / 64)
    lin("in1", T.dl[:, 19:35], T.ident[:, 48:64], -1.0 / 64)
    lin("in1", col(T.vl, 17), col(T.one, 0), -1.0)
    S("p2")
    shift("in1", T.vl[:, 0:19:18], T.fc[:, 0:2], 1.0, col(T.own, 4 * gl))
    lin("z3", fc(23), R16, -1.0, 7.0)
    lin("z2", col(T.sd, 0), CNT, -1.0, B)
    lin("z2", col(T.sd, 7), col(T.one, 0), 2048.0)
    lin("z2", T.d0i[:, 128:136], T.one[:, 0:8], B)
    lin("z3", fc(27), R16, -SC, (MID - B - 16) * SC)
    lin("z3", fc(8), R16, 1.0, 16.0)
    lin("z3", fc(4), R16, -1.0, 4.0)
    lin("z3", fc(5), R16, -100.0)
    lin("z3", T.kr[:, 0:96:8], T.one[:, 0:12], -4096.0)
    lin("z3", T.kr[:, 7:72:8], T.ident[:, 0:9], 16.0)
    lin("z3", col(T.kr, 79), col(T.one, 0), 4096.0)
    S("d0i")
    lin("z3", T.d0[:, 0:128], T.d0i[:, 0:128], -SC, MID * SC)

    picks = dict(o0=(T.oq, T.oz, 0, 0, 9), o1=(T.oq, T.oz, 144, 12, 21), p0=(T.pq, T.pz, 0, 10, 12), p1=(T.pq, T.pz, 32, 8, 10),
                 l0=(T.lq, T.lz, B - 16, 20, 24), l1=(T.lq, T.lz, Z - 8, 2, 3))

    def codes(nm, step):
        q, z, c, a, b = picks[nm]
        cp(step, q[:, c:c + 16 * (b - a)].bitcast(U32), T.xq[:, 0:130].bitcast(U32).indirect(T.offp[:, a:b]))

    def scales(nm, step):
        q, z, c, a, b = picks[nm]
        take(step, z[:, c:c + 16 * (b - a)], T.xz[:, 0:130].indirect(T.offp[:, a:b]))

    lin("z3", col(T.d0, 128), col(T.one, 0), (MID - Z) * SC)
    lin("z3", T.fa[:, 144:146], T.one[:, 0:2], 8192.0)
    lin("z3", T.fa[:, 128:144], T.one[:, 0:16], 0.0)
    lin("z3", T.fb[:, 144:146], T.one[:, 0:2], 0.0)
    lin("z3", T.wv[:, 520:528], T.one[:, 0:8], (MID - Z) * SC)
    S("jd")
    shift("jd2", T.jd[:, 96:192], T.jd[:, 0:96], 1.0, Q16)
    S("offp", "xq")
    scales("o0", "oz")
    scales("o1", "oz")
    V("offp", "xq")
    codes("o1", "o1q")
    codes("o0", "o0q")

    G("kq")
    g.remote_dma_fused([xfer(core, rel[2 + h], topo, (off, on)[h], sem.i2, T.kq[:, 4 * h:4 * h + 3], T.hand2[:, 0:3])
                        for h in range(2)], local_sem=sem.lo)
    g.remote_dma_fused([xfer(core, at(T, s, late), topo, off[0:4], sem.il, col(T.kq, late - 1), col(T.lk, N - late - 1)),
                        xfer(core, at(T, s, direct[2]), topo, off[4:8], sem.i2, col(T.kq, direct[2] - 1),
                             col(T.lk, N - direct[2] - 1)),
                        xfer(core, rel[0], topo, on, sem.i2, col(T.kq, direct[0] - 1), col(T.hand2, 0))], local_sem=sem.lo)
    for h in (1, 0):
        G("o%dq" % h)
        g.remote_dma_fused([xfer(core, rel[h], topo, off + on, sem.tc, T.oq[:, 144 * h:144 * h + 136].bitcast(dt.uint8),
                                 T.rq[:, :].bitcast(dt.uint8))], local_sem=sem.lo)
    G("oz")
    g.remote_dma_fused([xfer(core, rel[2 + h], topo, (off, on)[h], sem.ts, T.oz[:, 144 * h:144 * h + 136], T.rz[:, :])
                        for h in range(2)], local_sem=sem.lo)
    for u in direct:
        if u != late:
            a, c, w = B * (u - 1 - (u > late)) + skip(u), B * (N - u + 1) + skip(u), 16 + PAIR - skip(u)
            g.remote_dma_fused([xfer(core, at(T, s, u), topo, off, sem.ts, T.oz[:, a:a + w], T.lz[:, c:c + w])],
                               local_sem=sem.lo)

    n1 = 0
    for u in range(1, N):
        d = roads(T, topo, (s - u) % N)[1]
        n1 += (4, 4, 8)[d.index(u)] if u in d else 8
    tA = lambda k, a, b: T.thr[:, 32:96].indirect(k[:, a:b])
    tB = lambda k, a, b: T.thr[:, 0:64].indirect(k[:, a:b])
    c = B * (N - late + 1) + 16
    V("z2")
    vec.wait_ge(sem.i1, n1)
    scan("sc", T.sc[:, 1:40], T.land1[:, 9:48], T.one[:, 0:39], CNT, A.add, A.mult)
    scan("sd", T.sd[:, 1:7], T.d0i[:, 128:134], T.land1[:, 9:15], col(T.sd, 0), A.add, A.subtract)
    codes("p0", "pq")
    V("sc")
    turn("tot", T.tot[:, :], T.sc[:, 8:40])
    codes("p1", "pq")
    codes("l1", "lq")
    scales("p0", "pz")
    S("sc", "sl")
    take("rep", T.rep[:, 0:32], T.sc[:, 0:32].indirect(T.sl[:, 16:18]))
    S("sd")
    take("rep", T.rep[:, 32:64], T.sd[:, 0:8].indirect(T.sl[:, 16:18]))
    take("rep2", T.rep[:, 64:128], T.sc[:, 0:32].indirect(T.sl[:, 18:22]))
    V("tot", "kl")
    ts("f0", T.fa[:, 0:32], tA(T.kl, 0, 2), col(T.tot, 4 * g1 + 1), None, A.is_le)
    ts("f0", T.fb[:, 0:32], tB(T.kl, 0, 2), col(T.tot, 4 * g2 + 2), None, A.is_le)
    ts("za", fc(12), col(T.tot, 4 * s), float(CAP), -7.5, A.min, A.add)
    V("rep")
    turn("rpt", T.rpt[:, 0:64], T.rep[:, 0:64])
    V("f0", "in1")
    for i in range(2):
        scan("vl", T.vl[:, 18 * i + 1:18 * i + 17], T.fa[:, 0:16], T.fb[:, 0:16], col(T.vl, 18 * i))
    V("rpt", "jd2", "rep2")
    ts("st", T.st[:, :], T.jd[:, 96:192], col(T.rpt, 4 * s), col(T.rpt, 32 + 4 * s), A.is_ge, A.mult)
    turn("rpt2", T.rpt[:, 64:128], T.rep[:, 64:128])
    S("tot")
    take("sa", T.sa[:, :], T.tot[:, 0:32].indirect(T.sl[:, 0:7]))
    S("za", "z3")
    lin("zc", fc(21), fc(12), 1.0 / 16, WHOLE)
    shift("zc", fc(22), fc(12), 1.0, fc(23))
    take("sa", T.sb[:, :], T.tot[:, 0:32].indirect(T.sl[:, 8:15]))
    S("zc")
    lin("zf", fc(19), fc(21), 1.0, -WHOLE)
    S("rpt2")
    lin("nl", fc(11), col(T.rpt, 64 + 4 * s), SC, (MID - c + 1) * SC)
    scales("p1", "pz")
    S("zf")
    shift("in2", fc(6), fc(19), -16.0, fc(22))
    shift("u1", fc(29), fc(19), 1.0, fc(4), F.Relu)
    shift("u1", fc(30), fc(19), 100.0, fc(5), F.Relu)
    V("vl")
    scan("wl", T.wl[:, :], T.dl[:, :], T.vl[:, :], -1.0, A.max, A.min)
    sl, k = (s + N - late) % N, N - late
    vec.wait_ge(sem.il, 4)
    cp("km", T.km[:, 0:1], col(T.lk, N - late - 1))
    V("st")
    turn("stt", T.stt[:, :], T.st[:, :])
    V("wl")
    ts("offl", T.offl[:, :], T.wl[:, 16:35:18], -64.0, 63.0, A.mult, A.min)
    V("km")
    ts("xl", T.xal[:, :], tA(T.km, 0, 1), col(T.tot, 4 * ((sl + 1) % N) + 1), -SC, A.is_le, A.mult)
    V("stt", "z3")
    scan("sw", T.sw[:, :], T.kr[:, :], T.stt[:, :], 0.0, A.add, A.max)
    V("offl", "pq")
    cp("o2q", T.o2q[:, :].bitcast(U32), T.pq[:, 0:64].bitcast(U32).indirect(T.offl[:, 0:2]))

    S("offl", "pz")
    take("o2z", T.o2z[:, :], T.pz[:, 0:64].indirect(T.offl[:, 0:2]))
    S("nl", "in2")
    shift("nl2", fc(14), col(T.rpt, 96 + 4 * s), -SC, fc(11))
    done(act.activation(fc(7), fc(6), F.Relu, scale=400.0), "in3")
    S("u1")
    shift("u2", fc(31), fc(29), -1.0, fc(30))
    shift("ini", T.fc[:, 16:19], T.ident[:, 16:49:16], -1.0, fc(6))
    S("in3", "sw")
    shift("in0", fc(15), fc(7), -1.0, fc(6))
    shift("mf", T.wv[:, 528:538], T.sw[:, 7:80:8], -SC, fc(27))

    vec.wait_ge(sem.i2, 28)
    V("sa")
    tt("f1", T.fa[:, 32:128], tA(T.lk, 0, 6), T.sa[:, 0:96], A.is_le)
    ts("xl", T.xbl[:, :], tB(T.km, 0, 1), col(T.tot, 4 * ((sl + 2) % N) + 2), -SC, A.is_le, A.mult)
    tt("f1", T.fb[:, 32:144], tB(T.lk, 0, 7), T.sb[:, :], A.is_le)
    V("xl", "nl2", "zf", "u2")
    ts("c0", T.cf[:, 0:1], fc(19), 8.0, 7.0, A.mult, A.add)
    scan("d0l", T.d0[:, 16 * k:16 * k + 16], T.xal[:, :], T.xbl[:, :], fc(14))
    ts("wv", T.cf[:, 2:3], fc(31), 8.0, fc(8), A.add, A.min)
    scales("l0", "lz")
    S("c0")
    shift("fv", T.d0[:, 129:145], T.sw[:, 0:96].indirect(T.cf[:, 0:1]), -SC, fc(27))

    G("o2q")
    g.remote_dma_fused([xfer(core, at(T, s, late), topo, off, sem.tc, T.o2q[:, 0:BOTH].bitcast(dt.uint8),
                             T.lq[:, c:c + BOTH].bitcast(dt.uint8))], local_sem=sem.lo)
    G("o2z")
    g.remote_dma_fused([xfer(core, at(T, s, late), topo, off, sem.ts, T.o2z[:, 0:BOTH], T.lz[:, c:c + BOTH])], local_sem=sem.lo)
    g.wait_ge(sem.lo, 32 + 32 + 32 + 32 + 16)

    scales("l1", "lz")
    V("f1", "ini")
    for m in (1, 2, 3, 0):
        V("ini" if m else "in0")
        scan("w1%d" % m, T.w1[:, 130 * m:130 * m + 130], T.fa[:, 16:146], T.fb[:, 16:146], fc(15 + m))
    V("d0l")
    for m in (1, 2, 3, 0):
        V("w1%d" % m)
        if m:
            scan("wv", T.wv[:, 4 + m:520:4], T.d0[:, 0:129], T.w1[:, 130 * m:130 * m + 129], -1.0, A.max, A.min)
        else:
            V("fv")
            scan("wv", T.wv[:, 0:520:4], T.d0[:, 0:130], T.w1[:, 0:130], -1.0, A.max, A.min)
    codes("l0", "lq")
    V("wv", "mf")
    ts("offh", T.offh[:, :], T.wv[:, 512:538].indirect(T.cf[:, 2:3]), -1024.0, float(MID), A.mult, A.add)
    quant_w(2)

    S("offh", "lz")
    act.wait_ge(sem.ts, 56)
    take("hz", T.hz[:, :], T.lz[:, 0:Z + 8].indirect(T.offh[:, 0:10]))
    V("offh", "lq")
    vec.wait_ge(sem.tc, 40)
    cp("hq", T.hq[:, :].bitcast(U32), T.lq[:, 0:Z + 8].bitcast(U32).indirect(T.offh[:, 0:10]))
    quant_w(3)
    need(QT, "hq", "hz")
    for o in range(O):
        need(QT, "wq%d" % (o // 3))
        done(ten.matmul_mx(T.ps[:, 512 * o:512 * o + ROOM], T.wq[:, 128 * o:128 * o + 128], T.wz[:, 128 * o:128 * o + 128],
                           T.hq[:, 0:ROOM], T.hz[:, 0:ROOM], True, True), "t%d" % o)
    for o in range(O):
        y, p = T.ys[:, ROOM * o:ROOM * o + ROOM], T.ps[:, 512 * o:512 * o + ROOM]
        if o % 2 == 0:
            V("t%d" % o)
            cp("y%d" % o, y, p)
        else:
            S("t%d" % o)
            take("y%d" % o, y, p)
    for q, o, e in ((QS, 0, 1), (QA, 1, 4)):
        need(q, *["y%d" % i for i in range(o, e)])
        done(q[1].dma_start(T.y[:, ROOM * o:ROOM * e], T.ys[:, ROOM * o:ROOM * e]), "out", 16)
    S("out")
